import numpy as np
import ml_dtypes


def mxq(x, axis, fmt="e4m3"):
    dtype, down = {"e4m3": (ml_dtypes.float8_e4m3fn, 7), "e5m2": (ml_dtypes.float8_e5m2, 14)}[fmt]
    v = np.moveaxis(np.asarray(x, np.float32).astype(ml_dtypes.bfloat16).astype(np.float64), axis, -1)
    blocks = v.reshape(v.shape[:-1] + (-1, 32))
    amax = np.abs(blocks).max(-1, keepdims=True)
    byte = np.maximum(np.where(amax > 0, np.frexp(amax)[1] - 1 + 127, 0) - down, 1)
    scale = np.exp2(byte - 127.0)
    codes = (blocks / scale).astype(np.float32).astype(dtype).astype(np.float64)
    return np.moveaxis((codes * scale).reshape(v.shape), -1, axis)


WIDE = False


def mx_kscale(k):
    if not WIDE:
        return np.ones(k)
    levels = np.array([10, -10, 5, -5, 0])
    if k % 512:
        return np.exp2(np.random.permutation(np.resize(levels, k // 32))).repeat(32)
    a = np.empty((k // 512, 16))
    for p in range(k // 512):
        a[p, :8] = np.random.permutation(np.resize(levels, 8))
        for g in range(8):
            far = levels[np.abs(levels - a[p, g]) >= 10]
            a[p, g + 8] = far[np.random.randint(len(far))]
    return np.exp2(a.ravel()).repeat(32)


def f64(x):
    return np.asarray(x).astype(np.float64)


def striped(idx):
    return np.tile(idx.reshape(-1, 16).T, (8, 1)).astype(np.uint16)


def unstriped(offs):
    return offs[:16].T.reshape(-1).astype(np.int64)


E2M1 = np.array([0.0, 0.5, 1.0, 1.5, 2.0, 3.0, 4.0, 6.0, -0.0, -0.5, -1.0, -1.5, -2.0, -3.0, -4.0, -6.0])


def pack_weight(w, fmt):
    k, n = w.shape
    w = f64(np.asarray(w, np.float32).astype(ml_dtypes.bfloat16)).reshape(k // 32, 32, n)
    amax = np.abs(w).max(1)
    if fmt == "e4m3":
        byte = np.frexp(amax)[1] - 1 + 127 - 7
    else:
        mant, ex = np.frexp(amax / 6.0)
        byte = np.where(mant > 0.5, ex, ex - 1) + 127
    byte = np.clip(np.where(amax > 0, byte, 1), 1, 254)
    scaled = (w * np.exp2(127.0 - byte)[:, None, :]).reshape(k, n).astype(np.float32)
    by_word = np.ascontiguousarray(scaled.reshape(k // 512, 128, 4, n).transpose(0, 1, 3, 2))
    if fmt == "e4m3":
        words = by_word.astype(ml_dtypes.float8_e4m3fn).view(np.uint8)
    else:
        c = by_word.astype(ml_dtypes.float4_e2m1fn).view(np.uint8) & 0xF
        words = (c[..., 0::2] | (c[..., 1::2] << 4)).reshape(k // 512, 128, 2 * n)
    return np.ascontiguousarray(words), np.ascontiguousarray(byte.astype(np.uint8).reshape(k // 512, 16, n))


def unpack_weight(words, scales, fmt):
    g, _, n = scales.shape
    words = np.ascontiguousarray(words).reshape(g, 128, n, -1)
    if fmt == "e4m3":
        vals = words.view(ml_dtypes.float8_e4m3fn).astype(np.float64)
    else:
        nib = np.empty((g, 128, n, 4), np.uint8)
        nib[..., 0::2] = words & 0xF
        nib[..., 1::2] = words >> 4
        vals = E2M1[nib]
    vals = vals * np.repeat(np.exp2(scales.astype(np.float64) - 127.0), 8, axis=1)[..., None]
    return vals.transpose(0, 1, 3, 2).reshape(g * 512, n)


def gelu(v):
    return 0.5 * v * (1.0 + np.tanh(np.sqrt(2.0 / np.pi) * (v + 0.044715 * v**3)))


def striped8(idx):
    return np.concatenate([v.reshape(-1, 16).T for v in idx]).astype(np.uint16)


def unstriped8(offs):
    return np.stack([offs[16 * g:16 * g + 16].T.reshape(-1) for g in range(8)]).astype(np.int64)


def heads(xT, wgt, idx8):
    k = np.arange(xT.shape[0])
    return wgt[k // 4 % 128] * xT[k[:, None], idx8[k % 512 // 64]]


K, T, S, H, N = 1024, 2048, 1024, 1024, 512

def setup_inputs():
    n = np.random.standard_normal
    s = mx_kscale(K)[:, None]
    u = mx_kscale(H)[:, None]
    xT = n((K, T)) * s
    wgt = np.repeat(np.random.uniform(0.5, 2.0, (8, S)), 16, axis=0)
    offs = striped8(np.stack([np.random.permutation(T)[:S] for _ in range(8)]))
    w1 = 0.6 * n((K, H)) / np.sqrt(K) / s
    mu = 0.5 * n(H)
    amp = np.random.uniform(0.5, 1.5, H) * u[:, 0]
    wf_words, wf_scales = pack_weight(n((H, N)) / np.sqrt(H) / u, "e2m1")
    return {
        "xT": xT.astype(np.float32),
        "wgt": wgt.astype(np.float32),
        "offs": offs,
        "w1": w1.astype(np.float32),
        "mu": mu.astype(np.float32),
        "amp": amp.astype(np.float32),
        "wf_words": wf_words,
        "wf_scales": wf_scales,
    }

def reference(xT, wgt, offs, w1, mu, amp, wf_words, wf_scales):
    xg = heads(f64(xT), f64(wgt), unstriped8(offs))
    d = (mxq(f64(w1), 0, "e4m3").T @ mxq(xg, 0, "e4m3")) - f64(mu)[:, None]
    h = f64(amp)[:, None] * np.exp(-np.square(d))
    wf = unpack_weight(wf_words, wf_scales, "e2m1")
    return wf.T @ mxq(h, 0, "e4m3")

@@ -1,0 +1,313 @@
+from contextlib import ExitStack
+
+import concourse.mybir as mybir
+
+K, T, S, H, N = 1024, 2048, 1024, 1024, 512
+FLOPS = 2 * K * H * S + 2 * H * N * S
+
+F32 = mybir.dt.float32
+BF16 = mybir.dt.bfloat16
+I32 = mybir.dt.int32
+U32 = mybir.dt.uint32
+U16 = mybir.dt.uint16
+U8 = mybir.dt.uint8
+FP8X4 = mybir.dt.float8_e4m3fn_x4
+FP4X4 = mybir.dt.float4_e2m1fn_x4
+MULT = mybir.AluOpType.mult
+ACT = mybir.ActivationFunctionType
+
+P = 128
+PACK = 4
+PASS = 512
+HALF = 512
+BANK = 512
+
+
+def tile_list_radial_shell_features_kernel(tc, xT, wgt, offs, w1, mu, amp, wf_words, wf_scales, out):
+    nc = tc.nc
+    with ExitStack() as ctx:
+        keep = ctx.enter_context(tc.tile_pool(name="keep", bufs=1))
+        ring = ctx.enter_context(tc.tile_pool(name="ring", bufs=3))
+        psd = ctx.enter_context(tc.psum_pool(name="psd", bufs=4))
+        pso = ctx.enter_context(tc.psum_pool(name="pso", bufs=4))
+
+        offsets = keep.tile([P, S // 16], U16, name="offsets")
+        wg = [keep.tile([P, HALF], F32, name=f"wg{h}") for h in range(2)]
+        planes = [[keep.tile([P, T], F32, name=f"plane{a}{i}") for i in range(PACK)] for a in range(2)]
+        picked = [[keep.tile([P, PACK, HALF], F32, name=f"picked{a}{h}", tag=f"picked{a}{h}") for h in range(2)] for a in range(2)]
+        xb = {}
+        xc = [[keep.tile([P, HALF], U32, name=f"xc{a}{h}", align_bytes=64) for h in range(2)] for a in range(2)]
+        xs = [[keep.tile([P, HALF], U8, name=f"xs{a}{h}", align_bytes=64) for h in range(2)] for a in range(2)]
+        wraw = [[[keep.tile([P, PACK, 256], F32, name=f"wraw{b}{a}{u}") for u in range(2)] for a in range(2)] for b in range(2)]
+        wb = [[keep.tile([P, PACK, P, PACK], BF16, name=f"wb{b}{a}", align_bytes=64) for a in range(2)] for b in range(2)]
+        wc = [[keep.tile([P, PASS], U32, name=f"wc{b}{a}", align_bytes=64) for a in range(2)] for b in range(2)]
+        ws = [[keep.tile([P, PASS], U8, name=f"ws{b}{a}", align_bytes=64) for a in range(2)] for b in range(2)]
+        hc = [[keep.tile([P, HALF], U32, name=f"hc{b}{h}", align_bytes=64) for h in range(2)] for b in range(2)]
+        hs = [[keep.tile([P, HALF], U8, name=f"hs{b}{h}", align_bytes=64) for h in range(2)] for b in range(2)]
+        mu_t = keep.tile([P, 2, PACK], F32, name="mu_t")
+        amp_t = keep.tile([P, 2, PACK], F32, name="amp_t")
+        fw = keep.tile([P, 2, 2 * N], U8, name="fw", align_bytes=64)
+        fs = keep.tile([P, 2, N], U8, name="fs", align_bytes=64)
+        warm = keep.tile([P, 8], F32, name="warm")
+
+        x_rows = xT.rearrange("(a p i) t -> a i p t", a=2, i=PACK)
+        w_rows = w1.rearrange("(a p i) r -> a p i r", a=2, i=PACK)
+
+        def load_plane(a, i):
+            nc.sync.dma_start(planes[a][i][:], x_rows[a, i])
+
+        def load_w(b, a, u):
+            c0 = PASS * b + 256 * u
+            nc.sync.dma_start(wraw[b][a][u][:], w_rows[a, :, :, c0 : c0 + 256])
+
+        def gather(a, i, j0, n):
+            h, c = divmod(j0, HALF)
+            nc.vector.tensor_tensor(
+                picked[a][h][:, i, c : c + n],
+                planes[a][i][:].indirect(offsets[:, j0 // 16 : (j0 + n) // 16]),
+                wg[h][:, c : c + n],
+                MULT,
+            )
+
+        def copy_on(eng, dst, src):
+            if eng == "v":
+                nc.vector.tensor_copy(dst, src)
+            else:
+                nc.scalar.copy(dst, src)
+
+        def weave_x(eng, a, j0, n):
+            h, c = divmod(j0, HALF)
+            if (a, h) not in xb:
+                xb[(a, h)] = ring.tile([P, HALF, PACK], BF16, name="xb", tag="xb", bufs=4, align_bytes=64)
+            copy_on(
+                eng,
+                xb[(a, h)][:, c : c + n, :].rearrange("p (c e) i -> p c i e", e=2),
+                picked[a][h][:, :, c : c + n].rearrange("p i (c e) -> p c i e", e=2),
+            )
+
+        def quant_x(a, j0, n):
+            h, c = divmod(j0, HALF)
+            nc.vector.quantize_mx(
+                xc[a][h][:, c : c + n].bitcast(FP8X4),
+                xs[a][h][:, c : c + n],
+                xb[(a, h)][:, c : c + n, :].rearrange("p c i -> p (c i)"),
+            )
+
+        def weave_w(eng, b, a, u):
+            copy_on(
+                eng,
+                wb[b][a][:, :, 64 * u : 64 * u + 64, :].rearrange("p t m i -> p m i t"),
+                wraw[b][a][u][:].rearrange("p i (m t) -> p m i t", t=PACK),
+            )
+
+        def quant_w(b, a, t0, nt):
+            nc.vector.quantize_mx(
+                wc[b][a][:, P * t0 : P * (t0 + nt)].bitcast(FP8X4),
+                ws[b][a][:, P * t0 : P * (t0 + nt)],
+                wb[b][a][:, t0 : t0 + nt].rearrange("p t m i -> p (t m i)"),
+            )
+
+        squares = {}
+
+        def distances(b, j0, n):
+            h, c = divmod(j0, HALF)
+            per_bank = BANK // n
+            sq = ring.tile([P, PACK, n], F32, name="sq", tag="sq")
+            squares[(b, j0)] = sq
+            for t0 in range(0, PACK, per_bank):
+                bank = psd.tile([P, BANK], F32, name="dbank", tag="dbank")
+                ts = range(t0, min(PACK, t0 + per_bank))
+                for t in ts:
+                    for a in range(2):
+                        nc.tensor.matmul_mx(
+                            bank[:, (t - t0) * n : (t - t0 + 1) * n],
+                            lhsT=wc[b][a][:, P * t : P * (t + 1)].bitcast(FP8X4),
+                            lhsT_scale=ws[b][a][:, P * t : P * (t + 1)],
+                            rhs=xc[a][h][:, c : c + n].bitcast(FP8X4),
+                            rhs_scale=xs[a][h][:, c : c + n],
+                            start=(a == 0),
+                            stop=(a == 1),
+                        )
+                for t in ts:
+                    nc.scalar.activation(
+                        sq[:, t, :],
+                        bank[:, (t - t0) * n : (t - t0 + 1) * n],
+                        ACT.Square,
+                        bias=mu_t[:, b, t : t + 1],
+                        scale=-1.0,
+                    )
+
+        gauss = {}
+        hbs = {}
+
+        def exps(b, j0, n):
+            ex = ring.tile([P, PACK, n], F32, name="ex", tag="ex", bufs=5)
+            gauss[(b, j0)] = ex
+            nc.scalar.activation(ex[:], squares[(b, j0)][:], ACT.Exp, scale=-1.0)
+
+        def amps(b, j0, n):
+            hb = ring.tile([P, n, PACK], BF16, name="hb", tag="hb", align_bytes=64)
+            hbs[(b, j0)] = hb
+            nc.vector.tensor_tensor(
+                hb[:].rearrange("p (c e) t -> p c t e", e=2),
+                gauss[(b, j0)][:].rearrange("p t (c e) -> p c t e", e=2),
+                amp_t[:, b, :].rearrange("p (c t e) -> p c t e", c=1, e=1).to_broadcast([P, n // 2, PACK, 2]),
+                MULT,
+            )
+
+        def quant_h(b, j0, n):
+            h, c = divmod(j0, HALF)
+            nc.vector.quantize_mx(
+                hc[b][h][:, c : c + n].bitcast(FP8X4),
+                hs[b][h][:, c : c + n],
+                hbs[(b, j0)][:].rearrange("p c t -> p (c t)"),
+            )
+
+        stage = {}
+        staged = [0]
+
+        def features(j0, n, engs):
+            h, c = divmod(j0, HALF)
+            per_bank = (N // P) // len(engs)
+            step = n if n == BANK else P
+            for k, m0 in enumerate(range(0, N // P, per_bank)):
+                bank = pso.tile([P, BANK], F32, name="obank", tag="obank")
+                for m in range(m0, m0 + per_bank):
+                    for s0 in range(0, n, step):
+                        for b in range(2):
+                            o0 = (m - m0) * n + s0
+                            nc.tensor.matmul_mx(
+                                bank[:, o0 : o0 + step],
+                                lhsT=fw[:, b, 2 * P * m : 2 * P * (m + 1)].bitcast(FP4X4),
+                                lhsT_scale=fs[:, b, P * m : P * (m + 1)],
+                                rhs=hc[b][h][:, c + s0 : c + s0 + step].bitcast(FP8X4),
+                                rhs_scale=hs[b][h][:, c + s0 : c + s0 + step],
+                                start=(b == 0),
+                                stop=(b == 1),
+                            )
+                width = per_bank * n
+                half, first = divmod(staged[0], 2048)
+                staged[0] += width
+                if half not in stage:
+                    stage[half] = keep.tile([P, 2048], F32, name="stage", tag=f"picked0{half}")
+                res = stage[half][:, first : first + width]
+                copy_on(engs[k], res, bank[:, :width])
+                nc.sync.dma_start(
+                    out[P * m0 : P * (m0 + per_bank), j0 : j0 + n].rearrange("(m p) j -> p m j", p=P),
+                    res.rearrange("p (m j) -> p m j", j=n),
+                )
+
+        nc.sync.dma_start(offsets[:], offs)
+        nc.gpsimd.memset(fs[:].rearrange("p a n -> p (a n)").bitcast(I32), 0)
+        nc.gpsimd.memset(warm[:, 0:1], 0.0)
+        nc.scalar.activation(warm[:, 4:5], warm[:, 0:1], ACT.Exp)
+        nc.sync.dma_start(wg[0][:], wgt[:, 0 * HALF : (0 + 1) * HALF])
+        load_plane(0, 2)
+        nc.sync.dma_start(wg[1][:], wgt[:, 1 * HALF : (1 + 1) * HALF])
+        load_plane(1, 0)
+        load_plane(0, 3)
+        load_plane(0, 0)
+        load_plane(0, 1)
+        load_w(0, 1, 0)
+        load_plane(1, 1)
+        load_plane(1, 3)
+        load_plane(1, 2)
+        load_w(0, 0, 1)
+        load_w(0, 0, 0)
+        load_w(0, 1, 1)
+        load_w(1, 1, 1)
+        nc.sync.dma_start(mu_t[:], mu.rearrange("(b p t) -> p b t", b=2, t=PACK))
+        nc.sync.dma_start(amp_t[:], amp.rearrange("(b p t) -> p b t", b=2, t=PACK))
+        load_w(1, 0, 1)
+        load_w(1, 0, 0)
+        load_w(1, 1, 0)
+        nc.sync.dma_start(fw[:].bitcast(I32), wf_words.rearrange("a p n -> p a n").bitcast(I32))
+        for q in range(4):
+            nc.sync.dma_start(
+                fs[32 * q : 32 * q + 4].bitcast(I32),
+                wf_scales[:, 4 * q : 4 * q + 4, :].rearrange("a r n -> r a n").bitcast(I32),
+            )
+
+        weave_w("v", 0, 0, 0)
+        weave_w("v", 1, 0, 1)
+        gather(0, 2, 0, 512)
+        gather(0, 0, 512, 512)
+        gather(0, 2, 512, 512)
+        gather(0, 3, 512, 512)
+        gather(0, 1, 0, 512)
+        gather(1, 2, 0, 512)
+        gather(0, 0, 0, 512)
+        gather(0, 3, 0, 512)
+        weave_w("s", 0, 0, 1)
+        gather(1, 1, 0, 512)
+        gather(1, 0, 0, 512)
+        gather(1, 3, 0, 256)
+        weave_x("s", 0, 0, 512)
+        weave_w("s", 0, 1, 1)
+        gather(1, 3, 256, 256)
+        quant_x(0, 0, 512)
+        weave_x("v", 1, 256, 256)
+        weave_x("s", 1, 0, 256)
+        quant_w(0, 0, 0, 4)
+        weave_w("v", 1, 1, 0)
+        weave_w("v", 1, 0, 0)
+        weave_w("s", 0, 1, 0)
+        quant_w(0, 1, 2, 2)
+        gather(0, 1, 512, 512)
+        weave_x("s", 0, 512, 512)
+        quant_w(0, 1, 0, 2)
+        quant_x(1, 0, 256)
+        distances(0, 0, 256)
+        quant_x(1, 256, 256)
+        weave_w("s", 1, 1, 1)
+        distances(0, 256, 256)
+        exps(0, 0, 256)
+        gather(1, 2, 512, 512)
+        quant_w(1, 0, 0, 4)
+        quant_w(1, 1, 0, 4)
+        distances(1, 0, 256)
+        quant_x(0, 512, 512)
+        gather(1, 3, 512, 512)
+        distances(1, 256, 256)
+        exps(1, 256, 256)
+        gather(1, 1, 512, 512)
+        gather(1, 0, 512, 512)
+        exps(0, 256, 256)
+        weave_x("v", 1, 512, 256)
+        quant_x(1, 512, 256)
+        distances(1, 512, 256)
+        amps(0, 256, 256)
+        exps(1, 0, 256)
+        amps(1, 256, 256)
+        exps(1, 512, 256)
+        distances(0, 512, 256)
+        amps(1, 0, 256)
+        exps(0, 512, 256)
+        amps(0, 512, 256)
+        weave_x("v", 1, 768, 256)
+        amps(1, 512, 256)
+        quant_h(1, 0, 256)
+        quant_x(1, 768, 256)
+        distances(0, 768, 256)
+        distances(1, 768, 128)
+        quant_h(1, 512, 256)
+        amps(0, 0, 256)
+        exps(1, 768, 128)
+        quant_h(0, 0, 256)
+        exps(0, 768, 256)
+        distances(1, 896, 128)
+        amps(0, 768, 256)
+        exps(1, 896, 128)
+        amps(1, 768, 128)
+        quant_h(0, 512, 256)
+        quant_h(0, 256, 256)
+        quant_h(1, 768, 128)
+        amps(1, 896, 128)
+        quant_h(1, 256, 256)
+        features(256, 256, "sv")
+        features(0, 256, "vv")
+        quant_h(0, 768, 256)
+        features(768, 128, "v")
+        quant_h(1, 896, 128)
+        features(512, 256, "ss")
+        features(896, 128, "vs")

@@ -38,7 +38,7 @@ def tile_list_radial_shell_features_kernel(tc, xT, wgt, offs, w1, mu, amp, wf_wo
         xb = {}
         xc = [[keep.tile([P, HALF], U32, name=f"xc{a}{h}", align_bytes=64) for h in range(2)] for a in range(2)]
         xs = [[keep.tile([P, HALF], U8, name=f"xs{a}{h}", align_bytes=64) for h in range(2)] for a in range(2)]
-        wraw = [[[keep.tile([P, PACK, 256], F32, name=f"wraw{b}{a}{u}") for u in range(2)] for a in range(2)] for b in range(2)]
+        wraw = [[keep.tile([P, PACK, PASS], F32, name=f"wraw{b}{a}") for a in range(2)] for b in range(2)]
         wb = [[keep.tile([P, PACK, P, PACK], BF16, name=f"wb{b}{a}", align_bytes=64) for a in range(2)] for b in range(2)]
         wc = [[keep.tile([P, PASS], U32, name=f"wc{b}{a}", align_bytes=64) for a in range(2)] for b in range(2)]
         ws = [[keep.tile([P, PASS], U8, name=f"ws{b}{a}", align_bytes=64) for a in range(2)] for b in range(2)]
@@ -56,9 +56,8 @@ def tile_list_radial_shell_features_kernel(tc, xT, wgt, offs, w1, mu, amp, wf_wo
         def load_plane(a, i):
             nc.sync.dma_start(planes[a][i][:], x_rows[a, i])
 
-        def load_w(b, a, u):
-            c0 = PASS * b + 256 * u
-            nc.sync.dma_start(wraw[b][a][u][:], w_rows[a, :, :, c0 : c0 + 256])
+        def load_w(b, a):
+            nc.sync.dma_start(wraw[b][a][:], w_rows[a, :, :, PASS * b : PASS * (b + 1)])
 
         def gather(a, i, j0, n):
             h, c = divmod(j0, HALF)
@@ -93,11 +92,11 @@ def tile_list_radial_shell_features_kernel(tc, xT, wgt, offs, w1, mu, amp, wf_wo
                 xb[(a, h)][:, c : c + n, :].rearrange("p c i -> p (c i)"),
             )
 
-        def weave_w(eng, b, a, u):
+        def weave_w(eng, b, a, v):
             copy_on(
                 eng,
-                wb[b][a][:, :, 64 * u : 64 * u + 64, :].rearrange("p t m i -> p m i t"),
-                wraw[b][a][u][:].rearrange("p i (m t) -> p m i t", t=PACK),
+                wb[b][a][:, 2 * v : 2 * v + 2].rearrange("p e m i -> p m i e"),
+                wraw[b][a][:].rearrange("p i (m v e) -> p v m i e", v=2, e=2)[:, v],
             )
 
         def quant_w(b, a, t0, nt):
@@ -202,25 +201,21 @@ def tile_list_radial_shell_features_kernel(tc, xT, wgt, offs, w1, mu, amp, wf_wo
         nc.gpsimd.memset(warm[:, 0:1], 0.0)
         nc.scalar.activation(warm[:, 4:5], warm[:, 0:1], ACT.Exp)
         nc.sync.dma_start(wg[0][:], wgt[:, 0 * HALF : (0 + 1) * HALF])
-        load_plane(0, 2)
-        nc.sync.dma_start(wg[1][:], wgt[:, 1 * HALF : (1 + 1) * HALF])
-        load_plane(1, 0)
-        load_plane(0, 3)
         load_plane(0, 0)
+        nc.sync.dma_start(wg[1][:], wgt[:, 1 * HALF : (1 + 1) * HALF])
         load_plane(0, 1)
-        load_w(0, 1, 0)
+        load_plane(0, 2)
+        load_plane(0, 3)
+        load_plane(1, 0)
         load_plane(1, 1)
-        load_plane(1, 3)
         load_plane(1, 2)
-        load_w(0, 0, 1)
-        load_w(0, 0, 0)
-        load_w(0, 1, 1)
-        load_w(1, 1, 1)
+        load_plane(1, 3)
+        load_w(0, 0)
+        load_w(0, 1)
         nc.sync.dma_start(mu_t[:], mu.rearrange("(b p t) -> p b t", b=2, t=PACK))
         nc.sync.dma_start(amp_t[:], amp.rearrange("(b p t) -> p b t", b=2, t=PACK))
-        load_w(1, 0, 1)
-        load_w(1, 0, 0)
-        load_w(1, 1, 0)
+        load_w(1, 0)
+        load_w(1, 1)
         nc.sync.dma_start(fw[:].bitcast(I32), wf_words.rearrange("a p n -> p a n").bitcast(I32))
         for q in range(4):
             nc.sync.dma_start(
@@ -228,86 +223,86 @@ def tile_list_radial_shell_features_kernel(tc, xT, wgt, offs, w1, mu, amp, wf_wo
                 wf_scales[:, 4 * q : 4 * q + 4, :].rearrange("a r n -> r a n").bitcast(I32),
             )
 
-        weave_w("v", 0, 0, 0)
-        weave_w("v", 1, 0, 1)
-        gather(0, 2, 0, 512)
-        gather(0, 0, 512, 512)
-        gather(0, 2, 512, 512)
-        gather(0, 3, 512, 512)
-        gather(0, 1, 0, 512)
-        gather(1, 2, 0, 512)
         gather(0, 0, 0, 512)
-        gather(0, 3, 0, 512)
-        weave_w("s", 0, 0, 1)
-        gather(1, 1, 0, 512)
-        gather(1, 0, 0, 512)
-        gather(1, 3, 0, 256)
-        weave_x("s", 0, 0, 512)
-        weave_w("s", 0, 1, 1)
-        gather(1, 3, 256, 256)
-        quant_x(0, 0, 512)
-        weave_x("v", 1, 256, 256)
-        weave_x("s", 1, 0, 256)
-        quant_w(0, 0, 0, 4)
-        weave_w("v", 1, 1, 0)
-        weave_w("v", 1, 0, 0)
-        weave_w("s", 0, 1, 0)
-        quant_w(0, 1, 2, 2)
+        gather(0, 0, 512, 512)
+        gather(0, 1, 0, 512)
         gather(0, 1, 512, 512)
+        gather(0, 2, 0, 512)
+        gather(0, 2, 512, 512)
+        gather(0, 3, 0, 512)
+        weave_x("s", 0, 0, 512)
+        gather(0, 3, 512, 512)
         weave_x("s", 0, 512, 512)
-        quant_w(0, 1, 0, 2)
-        quant_x(1, 0, 256)
-        distances(0, 0, 256)
-        quant_x(1, 256, 256)
-        weave_w("s", 1, 1, 1)
-        distances(0, 256, 256)
-        exps(0, 0, 256)
-        gather(1, 2, 512, 512)
-        quant_w(1, 0, 0, 4)
-        quant_w(1, 1, 0, 4)
-        distances(1, 0, 256)
-        quant_x(0, 512, 512)
-        gather(1, 3, 512, 512)
-        distances(1, 256, 256)
-        exps(1, 256, 256)
-        gather(1, 1, 512, 512)
+        gather(1, 0, 0, 512)
         gather(1, 0, 512, 512)
-        exps(0, 256, 256)
+        gather(1, 1, 0, 512)
+        gather(1, 1, 512, 512)
+        gather(1, 2, 0, 512)
+        gather(1, 3, 0, 256)
+        weave_x("s", 1, 0, 256)
+        gather(1, 3, 256, 256)
+        weave_x("s", 1, 256, 256)
+        gather(1, 2, 512, 512)
+        gather(1, 3, 512, 512)
+        weave_w("s", 0, 0, 0)
+        weave_w("s", 0, 0, 1)
+        quant_x(0, 0, 512)
+        quant_x(1, 0, 256)
+        weave_w("s", 0, 1, 1)
+        quant_w(0, 0, 0, 4)
+        weave_x("s", 1, 768, 256)
+        weave_w("v", 0, 1, 0)
+        quant_w(0, 1, 2, 2)
+        quant_x(1, 256, 256)
+        quant_w(0, 1, 0, 2)
+        quant_x(0, 512, 512)
+        distances(0, 0, 256)
         weave_x("v", 1, 512, 256)
-        quant_x(1, 512, 256)
-        distances(1, 512, 256)
-        amps(0, 256, 256)
-        exps(1, 0, 256)
-        amps(1, 256, 256)
-        exps(1, 512, 256)
+        weave_w("v", 1, 0, 1)
+        distances(0, 256, 256)
+        quant_x(1, 512, 512)
+        weave_w("v", 1, 0, 0)
+        exps(0, 0, 256)
+        weave_w("v", 1, 1, 0)
+        quant_w(1, 0, 0, 4)
+        exps(0, 256, 256)
+        weave_w("v", 1, 1, 1)
+        quant_w(1, 1, 0, 2)
         distances(0, 512, 256)
-        amps(1, 0, 256)
-        exps(0, 512, 256)
-        amps(0, 512, 256)
-        weave_x("v", 1, 768, 256)
-        amps(1, 512, 256)
-        quant_h(1, 0, 256)
-        quant_x(1, 768, 256)
-        distances(0, 768, 256)
-        distances(1, 768, 128)
-        quant_h(1, 512, 256)
+        quant_w(1, 1, 2, 2)
         amps(0, 0, 256)
-        exps(1, 768, 128)
+        distances(1, 0, 256)
+        amps(0, 256, 256)
+        exps(0, 512, 256)
         quant_h(0, 0, 256)
+        quant_h(0, 256, 256)
+        distances(1, 256, 256)
+        amps(0, 512, 256)
+        exps(1, 0, 256)
+        quant_h(0, 512, 256)
+        distances(1, 512, 256)
+        amps(1, 0, 256)
+        exps(1, 256, 256)
+        quant_h(1, 0, 256)
+        distances(0, 768, 256)
+        amps(1, 256, 256)
+        features(0, 256, "vv")
+        exps(1, 512, 256)
+        distances(1, 768, 128)
+        quant_h(1, 256, 256)
+        amps(1, 512, 256)
         exps(0, 768, 256)
+        quant_h(1, 512, 256)
         distances(1, 896, 128)
         amps(0, 768, 256)
+        features(256, 256, "vs")
+        exps(1, 768, 128)
         exps(1, 896, 128)
+        quant_h(0, 768, 256)
         amps(1, 768, 128)
-        quant_h(0, 512, 256)
-        quant_h(0, 256, 256)
+        features(512, 256, "vs")
         quant_h(1, 768, 128)
         amps(1, 896, 128)
-        quant_h(1, 256, 256)
-        features(256, 256, "sv")
-        features(0, 256, "vv")
-        quant_h(0, 768, 256)
-        features(768, 128, "v")
         quant_h(1, 896, 128)
-        features(512, 256, "ss")
-        features(896, 128, "vs")
+        features(768, 128, "s")
+        features(896, 128, "sv")

@@ -28,12 +28,11 @@ def tile_list_radial_shell_features_kernel(tc, xT, wgt, offs, w1, mu, amp, wf_wo
     with ExitStack() as ctx:
         keep = ctx.enter_context(tc.tile_pool(name="keep", bufs=1))
         ring = ctx.enter_context(tc.tile_pool(name="ring", bufs=3))
-        psd = ctx.enter_context(tc.psum_pool(name="psd", bufs=4))
-        pso = ctx.enter_context(tc.psum_pool(name="pso", bufs=4))
+        psum = ctx.enter_context(tc.psum_pool(name="psum", bufs=8))
 
         offsets = keep.tile([P, S // 16], U16, name="offsets")
         wg = [keep.tile([P, HALF], F32, name=f"wg{h}") for h in range(2)]
-        planes = [[keep.tile([P, T], F32, name=f"plane{a}{i}") for i in range(PACK)] for a in range(2)]
+        planes = [[keep.tile([P, T], F32, name=f"plane{a}{i}", tag=f"plane{PACK * a + i}") for i in range(PACK)] for a in range(2)]
         picked = [[keep.tile([P, PACK, HALF], F32, name=f"picked{a}{h}", tag=f"picked{a}{h}") for h in range(2)] for a in range(2)]
         xb = {}
         xc = [[keep.tile([P, HALF], U32, name=f"xc{a}{h}", align_bytes=64) for h in range(2)] for a in range(2)]
@@ -108,13 +107,13 @@ def tile_list_radial_shell_features_kernel(tc, xT, wgt, offs, w1, mu, amp, wf_wo
 
         squares = {}
 
-        def distances(b, j0, n):
+        def distances(b, j0, n, per_bank=None):
             h, c = divmod(j0, HALF)
-            per_bank = BANK // n
-            sq = ring.tile([P, PACK, n], F32, name="sq", tag="sq")
+            per_bank = per_bank or BANK // n
+            sq = keep.tile([P, PACK, n], F32, name="sq", tag=f"plane{len(squares) % 2}")
             squares[(b, j0)] = sq
             for t0 in range(0, PACK, per_bank):
-                bank = psd.tile([P, BANK], F32, name="dbank", tag="dbank")
+                bank = psum.tile([P, BANK], F32, name="dbank", tag="bank")
                 ts = range(t0, min(PACK, t0 + per_bank))
                 for t in ts:
                     for a in range(2):
@@ -140,7 +139,7 @@ def tile_list_radial_shell_features_kernel(tc, xT, wgt, offs, w1, mu, amp, wf_wo
         hbs = {}
 
         def exps(b, j0, n):
-            ex = ring.tile([P, PACK, n], F32, name="ex", tag="ex", bufs=5)
+            ex = keep.tile([P, PACK, n], F32, name="ex", tag=f"plane{2 + len(gauss) % 4}")
             gauss[(b, j0)] = ex
             nc.scalar.activation(ex[:], squares[(b, j0)][:], ACT.Exp, scale=-1.0)
 
@@ -170,7 +169,7 @@ def tile_list_radial_shell_features_kernel(tc, xT, wgt, offs, w1, mu, amp, wf_wo
             per_bank = (N // P) // len(engs)
             step = n if n == BANK else P
             for k, m0 in enumerate(range(0, N // P, per_bank)):
-                bank = pso.tile([P, BANK], F32, name="obank", tag="obank")
+                bank = psum.tile([P, BANK], F32, name="obank", tag="bank")
                 for m in range(m0, m0 + per_bank):
                     for s0 in range(0, n, step):
                         for b in range(2):
@@ -208,9 +207,9 @@ def tile_list_radial_shell_features_kernel(tc, xT, wgt, offs, w1, mu, amp, wf_wo
         load_plane(0, 3)
         load_plane(1, 0)
         load_plane(1, 1)
+        load_w(0, 0)
         load_plane(1, 2)
         load_plane(1, 3)
-        load_w(0, 0)
         load_w(0, 1)
         nc.sync.dma_start(mu_t[:], mu.rearrange("(b p t) -> p b t", b=2, t=PACK))
         nc.sync.dma_start(amp_t[:], amp.rearrange("(b p t) -> p b t", b=2, t=PACK))
@@ -237,72 +236,63 @@ def tile_list_radial_shell_features_kernel(tc, xT, wgt, offs, w1, mu, amp, wf_wo
         gather(1, 0, 512, 512)
         gather(1, 1, 0, 512)
         gather(1, 1, 512, 512)
-        gather(1, 2, 0, 512)
-        gather(1, 3, 0, 256)
-        weave_x("s", 1, 0, 256)
-        gather(1, 3, 256, 256)
-        weave_x("s", 1, 256, 256)
-        gather(1, 2, 512, 512)
-        gather(1, 3, 512, 512)
         weave_w("s", 0, 0, 0)
         weave_w("s", 0, 0, 1)
         quant_x(0, 0, 512)
-        quant_x(1, 0, 256)
-        weave_w("s", 0, 1, 1)
+        gather(1, 2, 0, 512)
+        gather(1, 2, 512, 512)
+        gather(1, 3, 0, 256)
+        weave_x("s", 1, 0, 256)
         quant_w(0, 0, 0, 4)
-        weave_x("s", 1, 768, 256)
+        gather(1, 3, 256, 256)
         weave_w("v", 0, 1, 0)
+        weave_w("s", 0, 1, 1)
+        quant_x(1, 0, 256)
+        quant_w(0, 1, 0, 1)
+        quant_w(0, 1, 1, 1)
         quant_w(0, 1, 2, 2)
-        quant_x(1, 256, 256)
-        quant_w(0, 1, 0, 2)
-        quant_x(0, 512, 512)
-        distances(0, 0, 256)
-        weave_x("v", 1, 512, 256)
-        weave_w("v", 1, 0, 1)
-        distances(0, 256, 256)
-        quant_x(1, 512, 512)
-        weave_w("v", 1, 0, 0)
+        weave_x("s", 1, 256, 256)
+        distances(0, 0, 256, 1)
         exps(0, 0, 256)
+        gather(1, 3, 512, 512)
+        quant_x(1, 256, 256)
+        distances(0, 256, 256)
+        exps(0, 256, 256)
+        weave_x("v", 1, 512, 512)
+        quant_x(0, 512, 512)
+        quant_x(1, 512, 512)
+        distances(0, 512, 512)
+        exps(0, 512, 512)
+        weave_w("v", 1, 0, 0)
+        weave_w("v", 1, 0, 1)
         weave_w("v", 1, 1, 0)
         quant_w(1, 0, 0, 4)
-        exps(0, 256, 256)
-        weave_w("v", 1, 1, 1)
         quant_w(1, 1, 0, 2)
-        distances(0, 512, 256)
-        quant_w(1, 1, 2, 2)
+        weave_w("v", 1, 1, 1)
         amps(0, 0, 256)
-        distances(1, 0, 256)
-        amps(0, 256, 256)
-        exps(0, 512, 256)
+        quant_w(1, 1, 2, 2)
+        distances(1, 0, 512)
+        exps(1, 0, 512)
         quant_h(0, 0, 256)
+        amps(0, 256, 256)
+        amps(0, 512, 512)
         quant_h(0, 256, 256)
-        distances(1, 256, 256)
-        amps(0, 512, 256)
-        exps(1, 0, 256)
-        quant_h(0, 512, 256)
+        quant_h(0, 512, 512)
         distances(1, 512, 256)
-        amps(1, 0, 256)
-        exps(1, 256, 256)
-        quant_h(1, 0, 256)
-        distances(0, 768, 256)
-        amps(1, 256, 256)
-        features(0, 256, "vv")
-        exps(1, 512, 256)
         distances(1, 768, 128)
-        quant_h(1, 256, 256)
-        amps(1, 512, 256)
-        exps(0, 768, 256)
-        quant_h(1, 512, 256)
-        distances(1, 896, 128)
-        amps(0, 768, 256)
-        features(256, 256, "vs")
+        exps(1, 512, 256)
         exps(1, 768, 128)
+        distances(1, 896, 128)
         exps(1, 896, 128)
-        quant_h(0, 768, 256)
+        amps(1, 0, 512)
+        quant_h(1, 0, 512)
+        amps(1, 512, 256)
         amps(1, 768, 128)
-        features(512, 256, "vs")
+        quant_h(1, 512, 256)
         quant_h(1, 768, 128)
+        features(0, 512, "svss")
         amps(1, 896, 128)
         quant_h(1, 896, 128)
+        features(512, 256, "sv")
         features(768, 128, "s")
         features(896, 128, "sv")

@@ -18,281 +18,293 @@ ACT = mybir.ActivationFunctionType
 
 P = 128
 PACK = 4
-PASS = 512
-HALF = 512
+PASS = P * PACK
+PASSES = K // PASS
 BANK = 512
+BANKS = 8
+LIST_ROWS = 16
+HALF = S // 2
+QUARTER = S // 4
+EIGHTH = S // 8
+OUT_STEP = 128
+SQUARE_SLOTS = 2
+EXP_SLOTS = 4
+WOVEN_H_SLOTS = 3
+VECTOR, SCALAR = "vector", "scalar"
 
 
 def tile_list_radial_shell_features_kernel(tc, xT, wgt, offs, w1, mu, amp, wf_words, wf_scales, out):
     nc = tc.nc
     with ExitStack() as ctx:
         keep = ctx.enter_context(tc.tile_pool(name="keep", bufs=1))
-        ring = ctx.enter_context(tc.tile_pool(name="ring", bufs=3))
-        psum = ctx.enter_context(tc.psum_pool(name="psum", bufs=8))
+        ring = ctx.enter_context(tc.tile_pool(name="ring", bufs=WOVEN_H_SLOTS))
+        psum = ctx.enter_context(tc.psum_pool(name="psum", bufs=BANKS))
 
-        offsets = keep.tile([P, S // 16], U16, name="offsets")
-        wg = [keep.tile([P, HALF], F32, name=f"wg{h}") for h in range(2)]
-        planes = [[keep.tile([P, T], F32, name=f"plane{a}{i}", tag=f"plane{PACK * a + i}") for i in range(PACK)] for a in range(2)]
-        picked = [[keep.tile([P, PACK, HALF], F32, name=f"picked{a}{h}", tag=f"picked{a}{h}") for h in range(2)] for a in range(2)]
-        xb = {}
-        xc = [[keep.tile([P, HALF], U32, name=f"xc{a}{h}", align_bytes=64) for h in range(2)] for a in range(2)]
-        xs = [[keep.tile([P, HALF], U8, name=f"xs{a}{h}", align_bytes=64) for h in range(2)] for a in range(2)]
-        wraw = [[keep.tile([P, PACK, PASS], F32, name=f"wraw{b}{a}") for a in range(2)] for b in range(2)]
-        wb = [[keep.tile([P, PACK, P, PACK], BF16, name=f"wb{b}{a}", align_bytes=64) for a in range(2)] for b in range(2)]
-        wc = [[keep.tile([P, PASS], U32, name=f"wc{b}{a}", align_bytes=64) for a in range(2)] for b in range(2)]
-        ws = [[keep.tile([P, PASS], U8, name=f"ws{b}{a}", align_bytes=64) for a in range(2)] for b in range(2)]
-        hc = [[keep.tile([P, HALF], U32, name=f"hc{b}{h}", align_bytes=64) for h in range(2)] for b in range(2)]
-        hs = [[keep.tile([P, HALF], U8, name=f"hs{b}{h}", align_bytes=64) for h in range(2)] for b in range(2)]
-        mu_t = keep.tile([P, 2, PACK], F32, name="mu_t")
-        amp_t = keep.tile([P, 2, PACK], F32, name="amp_t")
-        fw = keep.tile([P, 2, 2 * N], U8, name="fw", align_bytes=64)
-        fs = keep.tile([P, 2, N], U8, name="fs", align_bytes=64)
-        warm = keep.tile([P, 8], F32, name="warm")
+        def grid(name, shape, dtype, inner=2, **options):
+            return [
+                [
+                    keep.tile(shape, dtype, name=f"{name}{inner * u + v}", tag=f"{name}{inner * u + v}", **options)
+                    for v in range(inner)
+                ]
+                for u in range(PASSES)
+            ]
 
-        x_rows = xT.rearrange("(a p i) t -> a i p t", a=2, i=PACK)
-        w_rows = w1.rearrange("(a p i) r -> a p i r", a=2, i=PACK)
+        offsets = keep.tile([P, S // LIST_ROWS], U16, name="offsets")
+        weights = [keep.tile([P, HALF], F32, name=f"weights{half}") for half in range(2)]
+        planes = grid("plane", [P, T], F32, inner=PACK)
+        picked = grid("picked", [P, PACK, HALF], F32)
+        x_woven = grid("x_woven", [P, HALF, PACK], BF16, align_bytes=64)
+        x_codes = grid("x_codes", [P, HALF], U32, align_bytes=64)
+        x_scales = grid("x_scales", [P, HALF], U8, align_bytes=64)
+        w_raw = grid("w_raw", [P, PACK, PASS], F32)
+        w_woven = grid("w_woven", [P, PACK, P, PACK], BF16, align_bytes=64)
+        w_codes = grid("w_codes", [P, PASS], U32, align_bytes=64)
+        w_scales = grid("w_scales", [P, PASS], U8, align_bytes=64)
+        h_codes = grid("h_codes", [P, HALF], U32, align_bytes=64)
+        h_scales = grid("h_scales", [P, HALF], U8, align_bytes=64)
+        centres = keep.tile([P, PASSES, 2 * PACK], F32, name="centres")
+        amplitudes = keep.tile([P, PASSES, 2 * PACK], F32, name="amplitudes")
+        f_words = keep.tile([P, PASSES, 2 * N], U8, name="f_words", align_bytes=64)
+        f_scales = keep.tile([P, PASSES, N], U8, name="f_scales", align_bytes=64)
+
+        x_rows = xT.rearrange("(a p i) t -> a i p t", a=PASSES, i=PACK)
+        w_rows = w1.rearrange("(a p i) r -> a p i r", a=PASSES, i=PACK)
+
+        def load_weights(half):
+            nc.sync.dma_start(weights[half][:], wgt[:, half * HALF : (half + 1) * HALF])
 
         def load_plane(a, i):
             nc.sync.dma_start(planes[a][i][:], x_rows[a, i])
 
         def load_w(b, a):
-            nc.sync.dma_start(wraw[b][a][:], w_rows[a, :, :, PASS * b : PASS * (b + 1)])
+            nc.sync.dma_start(w_raw[b][a][:], w_rows[a, :, :, PASS * b : PASS * (b + 1)])
 
-        def gather(a, i, j0, n):
-            h, c = divmod(j0, HALF)
-            nc.vector.tensor_tensor(
-                picked[a][h][:, i, c : c + n],
-                planes[a][i][:].indirect(offsets[:, j0 // 16 : (j0 + n) // 16]),
-                wg[h][:, c : c + n],
-                MULT,
-            )
+        def load_along_r(tile, vector):
+            nc.sync.dma_start(tile[:, :, :PACK], vector.rearrange("(b p t) -> p b t", b=PASSES, t=PACK))
 
-        def copy_on(eng, dst, src):
-            if eng == "v":
+        def place(j0, n):
+            half, first = divmod(j0, HALF)
+            return half, slice(first, first + n)
+
+        def copy_on(engine, dst, src):
+            if engine == VECTOR:
                 nc.vector.tensor_copy(dst, src)
             else:
-                nc.scalar.copy(dst, src)
+                nc.scalar.activation(dst, src, ACT.Copy)
 
-        def weave_x(eng, a, j0, n):
-            h, c = divmod(j0, HALF)
-            if (a, h) not in xb:
-                xb[(a, h)] = ring.tile([P, HALF, PACK], BF16, name="xb", tag="xb", bufs=4, align_bytes=64)
+        def gather(a, i, j0, n):
+            half, cols = place(j0, n)
+            listed = offsets[:, j0 // LIST_ROWS : (j0 + n) // LIST_ROWS]
+            nc.vector.tensor_tensor(
+                picked[a][half][:, i, cols], planes[a][i][:].indirect(listed), weights[half][:, cols], MULT
+            )
+
+        def weave_x(engine, a, j0, n):
+            half, cols = place(j0, n)
             copy_on(
-                eng,
-                xb[(a, h)][:, c : c + n, :].rearrange("p (c e) i -> p c i e", e=2),
-                picked[a][h][:, :, c : c + n].rearrange("p i (c e) -> p c i e", e=2),
+                engine,
+                x_woven[a][half][:, cols, :].rearrange("p (c e) i -> p c i e", e=2),
+                picked[a][half][:, :, cols].rearrange("p i (c e) -> p c i e", e=2),
             )
 
-        def quant_x(a, j0, n):
-            h, c = divmod(j0, HALF)
+        def quantise_x(a, j0, n):
+            half, cols = place(j0, n)
             nc.vector.quantize_mx(
-                xc[a][h][:, c : c + n].bitcast(FP8X4),
-                xs[a][h][:, c : c + n],
-                xb[(a, h)][:, c : c + n, :].rearrange("p c i -> p (c i)"),
+                x_codes[a][half][:, cols].bitcast(FP8X4),
+                x_scales[a][half][:, cols],
+                x_woven[a][half][:, cols, :].rearrange("p c i -> p (c i)"),
             )
 
-        def weave_w(eng, b, a, v):
+        def weave_w(engine, b, a, pair):
             copy_on(
-                eng,
-                wb[b][a][:, 2 * v : 2 * v + 2].rearrange("p e m i -> p m i e"),
-                wraw[b][a][:].rearrange("p i (m v e) -> p v m i e", v=2, e=2)[:, v],
+                engine,
+                w_woven[b][a][:, 2 * pair : 2 * pair + 2].rearrange("p e m i -> p m i e"),
+                w_raw[b][a][:].rearrange("p i (m v e) -> p v m i e", v=2, e=2)[:, pair],
             )
 
-        def quant_w(b, a, t0, nt):
+        def quantise_w(b, a, t0, count):
+            cols = slice(P * t0, P * (t0 + count))
             nc.vector.quantize_mx(
-                wc[b][a][:, P * t0 : P * (t0 + nt)].bitcast(FP8X4),
-                ws[b][a][:, P * t0 : P * (t0 + nt)],
-                wb[b][a][:, t0 : t0 + nt].rearrange("p t m i -> p (t m i)"),
+                w_codes[b][a][:, cols].bitcast(FP8X4),
+                w_scales[b][a][:, cols],
+                w_woven[b][a][:, t0 : t0 + count].rearrange("p t m i -> p (t m i)"),
             )
 
-        squares = {}
+        squares, exps, h_woven = {}, {}, {}
 
-        def distances(b, j0, n, per_bank=None):
-            h, c = divmod(j0, HALF)
-            per_bank = per_bank or BANK // n
-            sq = keep.tile([P, PACK, n], F32, name="sq", tag=f"plane{len(squares) % 2}")
-            squares[(b, j0)] = sq
+        def square_distances(b, j0, n, per_bank):
+            half, cols = place(j0, n)
+            square = keep.tile([P, PACK, n], F32, name="square", tag=f"plane{len(squares) % SQUARE_SLOTS}")
+            squares[(b, j0)] = square
             for t0 in range(0, PACK, per_bank):
-                bank = psum.tile([P, BANK], F32, name="dbank", tag="bank")
-                ts = range(t0, min(PACK, t0 + per_bank))
-                for t in ts:
-                    for a in range(2):
+                bank = psum.tile([P, BANK], F32, name="distance_bank", tag="bank")
+                sums = {t: bank[:, (t - t0) * n : (t - t0 + 1) * n] for t in range(t0, t0 + per_bank)}
+                for t in sums:
+                    for a in range(PASSES):
                         nc.tensor.matmul_mx(
-                            bank[:, (t - t0) * n : (t - t0 + 1) * n],
-                            lhsT=wc[b][a][:, P * t : P * (t + 1)].bitcast(FP8X4),
-                            lhsT_scale=ws[b][a][:, P * t : P * (t + 1)],
-                            rhs=xc[a][h][:, c : c + n].bitcast(FP8X4),
-                            rhs_scale=xs[a][h][:, c : c + n],
+                            sums[t],
+                            lhsT=w_codes[b][a][:, P * t : P * (t + 1)].bitcast(FP8X4),
+                            lhsT_scale=w_scales[b][a][:, P * t : P * (t + 1)],
+                            rhs=x_codes[a][half][:, cols].bitcast(FP8X4),
+                            rhs_scale=x_scales[a][half][:, cols],
                             start=(a == 0),
-                            stop=(a == 1),
+                            stop=(a == PASSES - 1),
                         )
-                for t in ts:
+                for t in sums:
                     nc.scalar.activation(
-                        sq[:, t, :],
-                        bank[:, (t - t0) * n : (t - t0 + 1) * n],
-                        ACT.Square,
-                        bias=mu_t[:, b, t : t + 1],
-                        scale=-1.0,
+                        square[:, t, :], sums[t], ACT.Square, bias=centres[:, b, t : t + 1], scale=-1.0
                     )
 
-        gauss = {}
-        hbs = {}
+        def exp_negative(b, j0, n):
+            slot = SQUARE_SLOTS + len(exps) % EXP_SLOTS
+            gauss = keep.tile([P, PACK, n], F32, name="gauss", tag=f"plane{slot}")
+            exps[(b, j0)] = gauss
+            nc.scalar.activation(gauss[:], squares[(b, j0)][:], ACT.Exp, scale=-1.0)
 
-        def exps(b, j0, n):
-            ex = keep.tile([P, PACK, n], F32, name="ex", tag=f"plane{2 + len(gauss) % 4}")
-            gauss[(b, j0)] = ex
-            nc.scalar.activation(ex[:], squares[(b, j0)][:], ACT.Exp, scale=-1.0)
-
-        def amps(b, j0, n):
-            hb = ring.tile([P, n, PACK], BF16, name="hb", tag="hb", align_bytes=64)
-            hbs[(b, j0)] = hb
+        def weave_h(b, j0, n):
+            woven = ring.tile([P, n, PACK], BF16, name="h_woven", tag="h_woven", align_bytes=64)
+            h_woven[(b, j0)] = woven
+            by_t = amplitudes[:, b, :PACK].rearrange("p (c t e) -> p c t e", c=1, e=1)
             nc.vector.tensor_tensor(
-                hb[:].rearrange("p (c e) t -> p c t e", e=2),
-                gauss[(b, j0)][:].rearrange("p t (c e) -> p c t e", e=2),
-                amp_t[:, b, :].rearrange("p (c t e) -> p c t e", c=1, e=1).to_broadcast([P, n // 2, PACK, 2]),
+                woven[:].rearrange("p (c e) t -> p c t e", e=2),
+                exps[(b, j0)][:].rearrange("p t (c e) -> p c t e", e=2),
+                by_t.to_broadcast([P, n // 2, PACK, 2]),
                 MULT,
             )
 
-        def quant_h(b, j0, n):
-            h, c = divmod(j0, HALF)
+        def quantise_h(b, j0, n):
+            half, cols = place(j0, n)
             nc.vector.quantize_mx(
-                hc[b][h][:, c : c + n].bitcast(FP8X4),
-                hs[b][h][:, c : c + n],
-                hbs[(b, j0)][:].rearrange("p c t -> p (c t)"),
+                h_codes[b][half][:, cols].bitcast(FP8X4),
+                h_scales[b][half][:, cols],
+                h_woven[(b, j0)][:].rearrange("p c t -> p (c t)"),
             )
 
-        stage = {}
-        staged = [0]
+        staging = {}
+        staged_widths = []
 
-        def features(j0, n, engs):
-            h, c = divmod(j0, HALF)
-            per_bank = (N // P) // len(engs)
-            step = n if n == BANK else P
-            for k, m0 in enumerate(range(0, N // P, per_bank)):
-                bank = psum.tile([P, BANK], F32, name="obank", tag="bank")
+        def features(j0, n, engines):
+            half, cols = place(j0, n)
+            per_bank = (N // P) // len(engines)
+            width = per_bank * n
+            for engine, m0 in zip(engines, range(0, N // P, per_bank)):
+                bank = psum.tile([P, BANK], F32, name="feature_bank", tag="bank")
                 for m in range(m0, m0 + per_bank):
-                    for s0 in range(0, n, step):
-                        for b in range(2):
-                            o0 = (m - m0) * n + s0
+                    for step in range(0, n, OUT_STEP):
+                        moving = slice(cols.start + step, cols.start + step + OUT_STEP)
+                        first_out = (m - m0) * n + step
+                        for b in range(PASSES):
                             nc.tensor.matmul_mx(
-                                bank[:, o0 : o0 + step],
-                                lhsT=fw[:, b, 2 * P * m : 2 * P * (m + 1)].bitcast(FP4X4),
-                                lhsT_scale=fs[:, b, P * m : P * (m + 1)],
-                                rhs=hc[b][h][:, c + s0 : c + s0 + step].bitcast(FP8X4),
-                                rhs_scale=hs[b][h][:, c + s0 : c + s0 + step],
+                                bank[:, first_out : first_out + OUT_STEP],
+                                lhsT=f_words[:, b, 2 * P * m : 2 * P * (m + 1)].bitcast(FP4X4),
+                                lhsT_scale=f_scales[:, b, P * m : P * (m + 1)],
+                                rhs=h_codes[b][half][:, moving].bitcast(FP8X4),
+                                rhs_scale=h_scales[b][half][:, moving],
                                 start=(b == 0),
-                                stop=(b == 1),
+                                stop=(b == PASSES - 1),
                             )
-                width = per_bank * n
-                half, first = divmod(staged[0], 2048)
-                staged[0] += width
-                if half not in stage:
-                    stage[half] = keep.tile([P, 2048], F32, name="stage", tag=f"picked0{half}")
-                res = stage[half][:, first : first + width]
-                copy_on(engs[k], res, bank[:, :width])
+                which, first = divmod(sum(staged_widths), PACK * HALF)
+                staged_widths.append(width)
+                if which not in staging:
+                    staging[which] = keep.tile([P, PACK * HALF], F32, name="staging", tag=f"picked{which}")
+                result = staging[which][:, first : first + width]
+                copy_on(engine, result, bank[:, :width])
                 nc.sync.dma_start(
                     out[P * m0 : P * (m0 + per_bank), j0 : j0 + n].rearrange("(m p) j -> p m j", p=P),
-                    res.rearrange("p (m j) -> p m j", j=n),
+                    result.rearrange("p (m j) -> p m j", j=n),
                 )
 
         nc.sync.dma_start(offsets[:], offs)
-        nc.gpsimd.memset(fs[:].rearrange("p a n -> p (a n)").bitcast(I32), 0)
-        nc.gpsimd.memset(warm[:, 0:1], 0.0)
-        nc.scalar.activation(warm[:, 4:5], warm[:, 0:1], ACT.Exp)
-        nc.sync.dma_start(wg[0][:], wgt[:, 0 * HALF : (0 + 1) * HALF])
+        nc.gpsimd.memset(f_scales[:].rearrange("p b n -> p (b n)").bitcast(I32), 0)
+        load_weights(0)
         load_plane(0, 0)
-        nc.sync.dma_start(wg[1][:], wgt[:, 1 * HALF : (1 + 1) * HALF])
-        load_plane(0, 1)
-        load_plane(0, 2)
-        load_plane(0, 3)
-        load_plane(1, 0)
-        load_plane(1, 1)
+        load_weights(1)
+        for a, i in [divmod(plane, PACK) for plane in range(1, PASSES * PACK - 1)]:
+            load_plane(a, i)
         load_w(0, 0)
-        load_plane(1, 2)
-        load_plane(1, 3)
+        load_plane(1, PACK - 1)
         load_w(0, 1)
-        nc.sync.dma_start(mu_t[:], mu.rearrange("(b p t) -> p b t", b=2, t=PACK))
-        nc.sync.dma_start(amp_t[:], amp.rearrange("(b p t) -> p b t", b=2, t=PACK))
+        load_along_r(centres, mu)
         load_w(1, 0)
         load_w(1, 1)
-        nc.sync.dma_start(fw[:].bitcast(I32), wf_words.rearrange("a p n -> p a n").bitcast(I32))
+        load_along_r(amplitudes, amp)
+        nc.sync.dma_start(f_words[:].bitcast(I32), wf_words.rearrange("b p n -> p b n").bitcast(I32))
         for q in range(4):
             nc.sync.dma_start(
-                fs[32 * q : 32 * q + 4].bitcast(I32),
-                wf_scales[:, 4 * q : 4 * q + 4, :].rearrange("a r n -> r a n").bitcast(I32),
+                f_scales[32 * q : 32 * q + 4].bitcast(I32),
+                wf_scales[:, 4 * q : 4 * q + 4, :].rearrange("b r n -> r b n").bitcast(I32),
             )
 
-        gather(0, 0, 0, 512)
-        gather(0, 0, 512, 512)
-        gather(0, 1, 0, 512)
-        gather(0, 1, 512, 512)
-        gather(0, 2, 0, 512)
-        gather(0, 2, 512, 512)
-        gather(0, 3, 0, 512)
-        weave_x("s", 0, 0, 512)
-        gather(0, 3, 512, 512)
-        weave_x("s", 0, 512, 512)
-        gather(1, 0, 0, 512)
-        gather(1, 0, 512, 512)
-        gather(1, 1, 0, 512)
-        gather(1, 1, 512, 512)
-        weave_w("s", 0, 0, 0)
-        weave_w("s", 0, 0, 1)
-        quant_x(0, 0, 512)
-        gather(1, 2, 0, 512)
-        gather(1, 2, 512, 512)
-        gather(1, 3, 0, 256)
-        weave_x("s", 1, 0, 256)
-        quant_w(0, 0, 0, 4)
-        gather(1, 3, 256, 256)
-        weave_w("v", 0, 1, 0)
-        weave_w("s", 0, 1, 1)
-        quant_x(1, 0, 256)
-        quant_w(0, 1, 0, 1)
-        quant_w(0, 1, 1, 1)
-        quant_w(0, 1, 2, 2)
-        weave_x("s", 1, 256, 256)
-        distances(0, 0, 256, 1)
-        exps(0, 0, 256)
-        gather(1, 3, 512, 512)
-        quant_x(1, 256, 256)
-        distances(0, 256, 256)
-        exps(0, 256, 256)
-        weave_x("v", 1, 512, 512)
-        quant_x(0, 512, 512)
-        quant_x(1, 512, 512)
-        distances(0, 512, 512)
-        exps(0, 512, 512)
-        weave_w("v", 1, 0, 0)
-        weave_w("v", 1, 0, 1)
-        weave_w("v", 1, 1, 0)
-        quant_w(1, 0, 0, 4)
-        quant_w(1, 1, 0, 2)
-        weave_w("v", 1, 1, 1)
-        amps(0, 0, 256)
-        quant_w(1, 1, 2, 2)
-        distances(1, 0, 512)
-        exps(1, 0, 512)
-        quant_h(0, 0, 256)
-        amps(0, 256, 256)
-        amps(0, 512, 512)
-        quant_h(0, 256, 256)
-        quant_h(0, 512, 512)
-        distances(1, 512, 256)
-        distances(1, 768, 128)
-        exps(1, 512, 256)
-        exps(1, 768, 128)
-        distances(1, 896, 128)
-        exps(1, 896, 128)
-        amps(1, 0, 512)
-        quant_h(1, 0, 512)
-        amps(1, 512, 256)
-        amps(1, 768, 128)
-        quant_h(1, 512, 256)
-        quant_h(1, 768, 128)
-        features(0, 512, "svss")
-        amps(1, 896, 128)
-        quant_h(1, 896, 128)
-        features(512, 256, "sv")
-        features(768, 128, "s")
-        features(896, 128, "sv")
+        q0, q1, q2, q3 = range(0, S, QUARTER)
+        last = PACK - 1
+
+        for i in range(PACK):
+            for j0 in (0, HALF):
+                gather(0, i, j0, HALF)
+        for j0 in (0, HALF):
+            weave_x(SCALAR, 0, j0, HALF)
+        for i in range(last):
+            for j0 in (0, HALF):
+                gather(1, i, j0, HALF)
+        for pair in range(2):
+            weave_w(SCALAR, 0, 0, pair)
+        quantise_w(0, 0, 0, PACK)
+
+        gather(1, last, q0, QUARTER)
+        weave_x(SCALAR, 1, q0, QUARTER)
+        gather(1, last, q1, QUARTER)
+        gather(1, last, q2, QUARTER)
+        weave_w(SCALAR, 0, 1, 1)
+        weave_w(VECTOR, 0, 1, 0)
+        quantise_w(0, 1, 0, PACK)
+        quantise_x(1, q0, QUARTER)
+        weave_x(SCALAR, 1, q1, QUARTER)
+        quantise_x(1, q1, QUARTER)
+        quantise_x(0, 0, HALF)
+        for pair in (1, 0):
+            weave_w(VECTOR, 1, 0, pair)
+        square_distances(0, q0, QUARTER, 1)
+        square_distances(0, q1, QUARTER, BANK // QUARTER)
+        for j0 in (q0, q1):
+            exp_negative(0, j0, QUARTER)
+
+        gather(1, last, q3, QUARTER)
+        for j0 in (q2, q3):
+            weave_x(VECTOR, 1, j0, QUARTER)
+        quantise_x(0, HALF, HALF)
+        for j0 in (q2, q3):
+            quantise_x(1, j0, QUARTER)
+        for j0 in (q2, q3):
+            square_distances(0, j0, QUARTER, BANK // QUARTER)
+        for j0 in (q2, q3):
+            exp_negative(0, j0, QUARTER)
+        weave_w(VECTOR, 1, 1, 0)
+        quantise_w(1, 1, 0, 2)
+        quantise_w(1, 0, 0, PACK)
+        weave_w(VECTOR, 1, 1, 1)
+        quantise_w(1, 1, 2, 2)
+        for j0 in (q0, q1):
+            weave_h(0, j0, QUARTER)
+            quantise_h(0, j0, QUARTER)
+
+        tail = [(q3, EIGHTH), (q3 + EIGHTH, EIGHTH)]
+        for j0 in (q0, q1):
+            square_distances(1, j0, QUARTER, BANK // QUARTER)
+        for j0 in (q0, q1):
+            exp_negative(1, j0, QUARTER)
+        for j0, n in [(q2, QUARTER)] + tail:
+            square_distances(1, j0, n, BANK // n)
+            exp_negative(1, j0, n)
+        for b, j0 in [(0, q2), (0, q3), (1, q0), (1, q1), (1, q2)]:
+            weave_h(b, j0, QUARTER)
+            quantise_h(b, j0, QUARTER)
+
+        features(q0, QUARTER, (VECTOR, SCALAR))
+        for j0, n in tail:
+            weave_h(1, j0, n)
+        for j0, n in tail:
+            quantise_h(1, j0, n)
+        features(q1, QUARTER, (SCALAR, SCALAR))
+        features(q2, QUARTER, (SCALAR, VECTOR))
+        features(*tail[0], (SCALAR,))
+        features(*tail[1], (VECTOR, SCALAR))

@@ -14,6 +14,7 @@ U8 = mybir.dt.uint8
 FP8X4 = mybir.dt.float8_e4m3fn_x4
 FP4X4 = mybir.dt.float4_e2m1fn_x4
 MULT = mybir.AluOpType.mult
+SUBTRACT = mybir.AluOpType.subtract
 ACT = mybir.ActivationFunctionType
 
 P = 128
@@ -26,10 +27,6 @@ LIST_ROWS = 16
 HALF = S // 2
 QUARTER = S // 4
 EIGHTH = S // 8
-OUT_STEP = 128
-SQUARE_SLOTS = 2
-EXP_SLOTS = 4
-WOVEN_H_SLOTS = 3
 VECTOR, SCALAR = "vector", "scalar"
 
 
@@ -37,41 +34,33 @@ def tile_list_radial_shell_features_kernel(tc, xT, wgt, offs, w1, mu, amp, wf_wo
     nc = tc.nc
     with ExitStack() as ctx:
         keep = ctx.enter_context(tc.tile_pool(name="keep", bufs=1))
-        ring = ctx.enter_context(tc.tile_pool(name="ring", bufs=WOVEN_H_SLOTS))
         psum = ctx.enter_context(tc.psum_pool(name="psum", bufs=BANKS))
 
-        def grid(name, shape, dtype, inner=2, **options):
-            return [
-                [
-                    keep.tile(shape, dtype, name=f"{name}{inner * u + v}", tag=f"{name}{inner * u + v}", **options)
-                    for v in range(inner)
-                ]
-                for u in range(PASSES)
-            ]
+        def tile(name, shape, dtype, tag=None):
+            return keep.tile(shape, dtype, name=name, tag=tag or name, align_bytes=64)
 
         offsets = keep.tile([P, S // LIST_ROWS], U16, name="offsets")
-        weights = [keep.tile([P, HALF], F32, name=f"weights{half}") for half in range(2)]
-        planes = grid("plane", [P, T], F32, inner=PACK)
-        picked = grid("picked", [P, PACK, HALF], F32)
-        x_woven = grid("x_woven", [P, HALF, PACK], BF16, align_bytes=64)
-        x_codes = grid("x_codes", [P, HALF], U32, align_bytes=64)
-        x_scales = grid("x_scales", [P, HALF], U8, align_bytes=64)
-        w_raw = grid("w_raw", [P, PACK, PASS], F32)
-        w_woven = grid("w_woven", [P, PACK, P, PACK], BF16, align_bytes=64)
-        w_codes = grid("w_codes", [P, PASS], U32, align_bytes=64)
-        w_scales = grid("w_scales", [P, PASS], U8, align_bytes=64)
-        h_codes = grid("h_codes", [P, HALF], U32, align_bytes=64)
-        h_scales = grid("h_scales", [P, HALF], U8, align_bytes=64)
-        centres = keep.tile([P, PASSES, 2 * PACK], F32, name="centres")
-        amplitudes = keep.tile([P, PASSES, 2 * PACK], F32, name="amplitudes")
-        f_words = keep.tile([P, PASSES, 2 * N], U8, name="f_words", align_bytes=64)
-        f_scales = keep.tile([P, PASSES, N], U8, name="f_scales", align_bytes=64)
+        weights = tile("weights", [P, S], F32)
+        planes = [[tile(f"plane{PACK * a + i}", [P, T], F32) for i in range(PACK)] for a in range(PASSES)]
+        picked = [tile(f"picked{a}", [P, PACK, S], F32) for a in range(PASSES)]
+        w_raw = [[tile(f"w_raw{b}{a}", [P, PACK, PASS], F32) for a in range(PASSES)] for b in range(PASSES)]
+        w_woven = [[tile(f"w_woven{b}{a}", [P, PACK * P * PACK], BF16) for a in range(PASSES)] for b in range(PASSES)]
+        w_scales = [[tile(f"w_scales{b}{a}", [P, PASS], U8) for a in range(PASSES)] for b in range(PASSES)]
+        x_scales = [tile(f"x_scales{a}", [P, S], U8) for a in range(PASSES)]
+        h_codes = [tile(f"h_codes{b}", [P, S], U32) for b in range(PASSES)]
+        h_scales = [tile(f"h_scales{b}", [P, S], U8) for b in range(PASSES)]
+        centres = tile("centres", [P, PASSES, 2 * PACK], F32)
+        amplitudes = tile("amplitudes", [P, PASSES, 2 * PACK], F32)
+        f_words = tile("f_words", [P, PASSES, 2 * N], U8)
+        f_scales = tile("f_scales", [P, PASSES, N], U8)
+        x_woven, x_codes, w_codes = {}, {}, {}
+        squares, exps, h_woven = {}, {}, {}
 
         x_rows = xT.rearrange("(a p i) t -> a i p t", a=PASSES, i=PACK)
         w_rows = w1.rearrange("(a p i) r -> a p i r", a=PASSES, i=PACK)
 
-        def load_weights(half):
-            nc.sync.dma_start(weights[half][:], wgt[:, half * HALF : (half + 1) * HALF])
+        def load_weights(j0, n):
+            nc.sync.dma_start(weights[:, j0 : j0 + n], wgt[:, j0 : j0 + n])
 
         def load_plane(a, i):
             nc.sync.dma_start(planes[a][i][:], x_rows[a, i])
@@ -79,12 +68,16 @@ def tile_list_radial_shell_features_kernel(tc, xT, wgt, offs, w1, mu, amp, wf_wo
         def load_w(b, a):
             nc.sync.dma_start(w_raw[b][a][:], w_rows[a, :, :, PASS * b : PASS * (b + 1)])
 
-        def load_along_r(tile, vector):
-            nc.sync.dma_start(tile[:, :, :PACK], vector.rearrange("(b p t) -> p b t", b=PASSES, t=PACK))
+        def load_along_r(dst, vector):
+            nc.sync.dma_start(dst[:, :, :PACK], vector.rearrange("(b p t) -> p b t", b=PASSES, t=PACK))
 
-        def place(j0, n):
-            half, first = divmod(j0, HALF)
-            return half, slice(first, first + n)
+        def load_filter():
+            nc.sync.dma_start(f_words[:].bitcast(I32), wf_words.rearrange("b p n -> p b n").bitcast(I32))
+            for q in range(4):
+                nc.sync.dma_start(
+                    f_scales[32 * q : 32 * q + 4].bitcast(I32),
+                    wf_scales[:, 4 * q : 4 * q + 4, :].rearrange("b r n -> r b n").bitcast(I32),
+                )
 
         def copy_on(engine, dst, src):
             if engine == VECTOR:
@@ -92,133 +85,168 @@ def tile_list_radial_shell_features_kernel(tc, xT, wgt, offs, w1, mu, amp, wf_wo
             else:
                 nc.scalar.activation(dst, src, ACT.Copy)
 
+        def holder(tiles, key, j0):
+            first = max(k[-1] for k in tiles if k[:-1] == key and k[-1] <= j0)
+            return tiles[key + (first,)], j0 - first
+
         def gather(a, i, j0, n):
-            half, cols = place(j0, n)
             listed = offsets[:, j0 // LIST_ROWS : (j0 + n) // LIST_ROWS]
             nc.vector.tensor_tensor(
-                picked[a][half][:, i, cols], planes[a][i][:].indirect(listed), weights[half][:, cols], MULT
+                picked[a][:, i, j0 : j0 + n], planes[a][i][:].indirect(listed), weights[:, j0 : j0 + n], MULT
             )
 
-        def weave_x(engine, a, j0, n):
-            half, cols = place(j0, n)
+        def weave_x(engine, a, j0, n, tag=None):
+            woven = tile(f"x_woven{a}_{j0}", [P, n * PACK], BF16, tag)
+            x_woven[(a, j0)] = woven
             copy_on(
                 engine,
-                x_woven[a][half][:, cols, :].rearrange("p (c e) i -> p c i e", e=2),
-                picked[a][half][:, :, cols].rearrange("p i (c e) -> p c i e", e=2),
+                woven[:].rearrange("p (c e i) -> p c i e", e=2, i=PACK),
+                picked[a][:, :, j0 : j0 + n].rearrange("p i (c e) -> p c i e", e=2),
             )
 
-        def quantise_x(a, j0, n):
-            half, cols = place(j0, n)
+        def quantise_x(a, j0, n, tag=None):
+            woven, first = holder(x_woven, (a,), j0)
+            codes = tile(f"x_codes{a}_{j0}", [P, n], U32, tag)
+            x_codes[(a, j0)] = codes
             nc.vector.quantize_mx(
-                x_codes[a][half][:, cols].bitcast(FP8X4),
-                x_scales[a][half][:, cols],
-                x_woven[a][half][:, cols, :].rearrange("p c i -> p (c i)"),
+                codes[:].bitcast(FP8X4), x_scales[a][:, j0 : j0 + n], woven[:, PACK * first : PACK * (first + n)]
             )
 
-        def weave_w(engine, b, a, pair):
+        def weave_w_pair(engine, b, a, pair):
+            width = 2 * P * PACK
             copy_on(
                 engine,
-                w_woven[b][a][:, 2 * pair : 2 * pair + 2].rearrange("p e m i -> p m i e"),
+                w_woven[b][a][:, pair * width : (pair + 1) * width].rearrange("p (e m i) -> p m i e", e=2, i=PACK),
                 w_raw[b][a][:].rearrange("p i (m v e) -> p v m i e", v=2, e=2)[:, pair],
             )
 
-        def quantise_w(b, a, t0, count):
-            cols = slice(P * t0, P * (t0 + count))
-            nc.vector.quantize_mx(
-                w_codes[b][a][:, cols].bitcast(FP8X4),
-                w_scales[b][a][:, cols],
-                w_woven[b][a][:, t0 : t0 + count].rearrange("p t m i -> p (t m i)"),
+        def weave_w(b, a):
+            nc.vector.tensor_copy(
+                w_woven[b][a][:].rearrange("p (v e m i) -> p v m i e", v=2, e=2, i=PACK),
+                w_raw[b][a][:].rearrange("p i (m v e) -> p v m i e", v=2, e=2),
             )
 
-        squares, exps, h_woven = {}, {}, {}
+        def quantise_w(b, a, t0, count, tag=None):
+            codes = tile(f"w_codes{b}{a}_{t0}", [P, P * count], U32, tag)
+            w_codes[(b, a, t0)] = codes
+            nc.vector.quantize_mx(
+                codes[:].bitcast(FP8X4),
+                w_scales[b][a][:, P * t0 : P * (t0 + count)],
+                w_woven[b][a][:, P * PACK * t0 : P * PACK * (t0 + count)],
+            )
 
-        def square_distances(b, j0, n, per_bank):
-            half, cols = place(j0, n)
-            square = keep.tile([P, PACK, n], F32, name="square", tag=f"plane{len(squares) % SQUARE_SLOTS}")
+        def square_distances(b, j0, n, per_bank, tag, on_vector=()):
+            square = tile(f"square{b}_{j0}", [P, PACK, n], F32, tag)
             squares[(b, j0)] = square
+            pieces = sorted({k[1] for k in x_codes if j0 <= k[1] < j0 + n} | {j0}) + [j0 + n]
             for t0 in range(0, PACK, per_bank):
                 bank = psum.tile([P, BANK], F32, name="distance_bank", tag="bank")
-                sums = {t: bank[:, (t - t0) * n : (t - t0 + 1) * n] for t in range(t0, t0 + per_bank)}
-                for t in sums:
-                    for a in range(PASSES):
-                        nc.tensor.matmul_mx(
-                            sums[t],
-                            lhsT=w_codes[b][a][:, P * t : P * (t + 1)].bitcast(FP8X4),
-                            lhsT_scale=w_scales[b][a][:, P * t : P * (t + 1)],
-                            rhs=x_codes[a][half][:, cols].bitcast(FP8X4),
-                            rhs_scale=x_scales[a][half][:, cols],
-                            start=(a == 0),
-                            stop=(a == PASSES - 1),
-                        )
-                for t in sums:
+                for t in range(t0, t0 + per_bank):
+                    for c0, c1 in zip(pieces, pieces[1:]):
+                        lo = (t - t0) * n + c0 - j0
+                        for a in range(PASSES):
+                            wc, wt = holder(w_codes, (b, a), t)
+                            xc, xj = holder(x_codes, (a,), c0)
+                            nc.tensor.matmul_mx(
+                                bank[:, lo : lo + c1 - c0],
+                                lhsT=wc[:, P * wt : P * (wt + 1)].bitcast(FP8X4),
+                                lhsT_scale=w_scales[b][a][:, P * t : P * (t + 1)],
+                                rhs=xc[:, xj : xj + c1 - c0].bitcast(FP8X4),
+                                rhs_scale=x_scales[a][:, c0:c1],
+                                start=(a == 0),
+                                stop=(a == PASSES - 1),
+                            )
+                if t0 in on_vector:
+                    shifted = tile(f"shifted{b}_{j0}_{t0}", [P, per_bank, n], F32)
+                    nc.vector.tensor_tensor(
+                        shifted[:],
+                        bank[:, : per_bank * n].rearrange("p (t j) -> p t j", j=n),
+                        centres[:, b, t0 : t0 + per_bank].unsqueeze(2).to_broadcast([P, per_bank, n]),
+                        SUBTRACT,
+                    )
+                    nc.vector.tensor_tensor(square[:, t0 : t0 + per_bank, :], shifted[:], shifted[:], MULT)
+                    continue
+                for t in range(t0, t0 + per_bank):
                     nc.scalar.activation(
-                        square[:, t, :], sums[t], ACT.Square, bias=centres[:, b, t : t + 1], scale=-1.0
+                        square[:, t, :],
+                        bank[:, (t - t0) * n : (t - t0 + 1) * n],
+                        ACT.Square,
+                        bias=centres[:, b, t : t + 1],
+                        scale=-1.0,
                     )
 
-        def exp_negative(b, j0, n):
-            slot = SQUARE_SLOTS + len(exps) % EXP_SLOTS
-            gauss = keep.tile([P, PACK, n], F32, name="gauss", tag=f"plane{slot}")
+        def exp_negative(b, j0, n, tag):
+            square, first = holder(squares, (b,), j0)
+            gauss = tile(f"gauss{b}_{j0}", [P, PACK, n], F32, tag)
             exps[(b, j0)] = gauss
-            nc.scalar.activation(gauss[:], squares[(b, j0)][:], ACT.Exp, scale=-1.0)
+            nc.scalar.activation(gauss[:], square[:, :, first : first + n], ACT.Exp, scale=-1.0)
 
-        def weave_h(b, j0, n):
-            woven = ring.tile([P, n, PACK], BF16, name="h_woven", tag="h_woven", align_bytes=64)
-            h_woven[(b, j0)] = woven
+        def weave_h(b, j0, n, tag, width=None):
+            gauss, first = holder(exps, (b,), j0)
+            if tag == "shared":
+                whole, start = holder(h_woven, (b,), j0)
+            else:
+                whole, start = tile(f"h_woven{b}_{j0}", [P, (width or n) * PACK], BF16, tag), 0
+                h_woven[(b, j0)] = whole
+            woven = whole[:, PACK * start : PACK * (start + n)]
             by_t = amplitudes[:, b, :PACK].rearrange("p (c t e) -> p c t e", c=1, e=1)
             nc.vector.tensor_tensor(
-                woven[:].rearrange("p (c e) t -> p c t e", e=2),
-                exps[(b, j0)][:].rearrange("p t (c e) -> p c t e", e=2),
+                woven.rearrange("p (c e t) -> p c t e", e=2, t=PACK),
+                gauss[:, :, first : first + n].rearrange("p t (c e) -> p c t e", e=2),
                 by_t.to_broadcast([P, n // 2, PACK, 2]),
                 MULT,
             )
 
         def quantise_h(b, j0, n):
-            half, cols = place(j0, n)
+            woven, first = holder(h_woven, (b,), j0)
             nc.vector.quantize_mx(
-                h_codes[b][half][:, cols].bitcast(FP8X4),
-                h_scales[b][half][:, cols],
-                h_woven[(b, j0)][:].rearrange("p c t -> p (c t)"),
+                h_codes[b][:, j0 : j0 + n].bitcast(FP8X4),
+                h_scales[b][:, j0 : j0 + n],
+                woven[:, PACK * first : PACK * (first + n)],
             )
 
-        staging = {}
-        staged_widths = []
+        banks, stagings = {}, {}
 
-        def features(j0, n, engines):
-            half, cols = place(j0, n)
-            per_bank = (N // P) // len(engines)
-            width = per_bank * n
-            for engine, m0 in zip(engines, range(0, N // P, per_bank)):
-                bank = psum.tile([P, BANK], F32, name="feature_bank", tag="bank")
-                for m in range(m0, m0 + per_bank):
-                    for step in range(0, n, OUT_STEP):
-                        moving = slice(cols.start + step, cols.start + step + OUT_STEP)
-                        first_out = (m - m0) * n + step
-                        for b in range(PASSES):
+        def products(j0, n, count, blocks):
+            per_bank = (N // P) // count
+            step = BANK if n == BANK else P
+            for m0 in range(0, N // P, per_bank):
+                if 0 in blocks:
+                    banks[(j0, m0 // per_bank)] = psum.tile([P, BANK], F32, name="feature_bank", tag="bank")
+                bank = banks[(j0, m0 // per_bank)]
+                for b in blocks:
+                    for m in range(m0, m0 + per_bank):
+                        for s0 in range(0, n, step):
+                            moving = slice(j0 + s0, j0 + s0 + step)
+                            first_out = (m - m0) * n + s0
                             nc.tensor.matmul_mx(
-                                bank[:, first_out : first_out + OUT_STEP],
+                                bank[:, first_out : first_out + step],
                                 lhsT=f_words[:, b, 2 * P * m : 2 * P * (m + 1)].bitcast(FP4X4),
                                 lhsT_scale=f_scales[:, b, P * m : P * (m + 1)],
-                                rhs=h_codes[b][half][:, moving].bitcast(FP8X4),
-                                rhs_scale=h_scales[b][half][:, moving],
-                                start=(b == 0),
-                                stop=(b == PASSES - 1),
+                                rhs=h_codes[b][:, moving].bitcast(FP8X4),
+                                rhs_scale=h_scales[b][:, moving],
+                                start=(b == 0 and first_out == 0),
+                                stop=(b == PASSES - 1 and first_out + step == per_bank * n),
                             )
-                which, first = divmod(sum(staged_widths), PACK * HALF)
-                staged_widths.append(width)
-                if which not in staging:
-                    staging[which] = keep.tile([P, PACK * HALF], F32, name="staging", tag=f"picked{which}")
-                result = staging[which][:, first : first + width]
-                copy_on(engine, result, bank[:, :width])
-                nc.sync.dma_start(
-                    out[P * m0 : P * (m0 + per_bank), j0 : j0 + n].rearrange("(m p) j -> p m j", p=P),
-                    result.rearrange("p (m j) -> p m j", j=n),
-                )
 
+        def store(engine, j0, n, count, which, tag=None):
+            per_bank = (N // P) // count
+            width = per_bank * n
+            m0 = which * per_bank
+            result = tile(f"staging{j0}_{which}", [P, width], F32, tag)
+            copy_on(engine, result[:], banks[(j0, which)][:, :width])
+            nc.sync.dma_start(
+                out[P * m0 : P * (m0 + per_bank), j0 : j0 + n].rearrange("(m p) j -> p m j", p=P),
+                result[:].rearrange("p (m j) -> p m j", j=n),
+            )
+
+        q0, q1, q2, q3 = range(0, S, QUARTER)
+        e0, e1 = q3, q3 + EIGHTH
         nc.sync.dma_start(offsets[:], offs)
-        nc.gpsimd.memset(f_scales[:].rearrange("p b n -> p (b n)").bitcast(I32), 0)
-        load_weights(0)
+        nc.vector.memset(f_scales[:].rearrange("p b n -> p (b n)").bitcast(I32), 0)
+        load_weights(0, HALF)
         load_plane(0, 0)
-        load_weights(1)
+        load_weights(HALF, HALF)
         for a, i in [divmod(plane, PACK) for plane in range(1, PASSES * PACK - 1)]:
             load_plane(a, i)
         load_w(0, 0)
@@ -228,83 +256,78 @@ def tile_list_radial_shell_features_kernel(tc, xT, wgt, offs, w1, mu, amp, wf_wo
         load_w(1, 0)
         load_w(1, 1)
         load_along_r(amplitudes, amp)
-        nc.sync.dma_start(f_words[:].bitcast(I32), wf_words.rearrange("b p n -> p b n").bitcast(I32))
-        for q in range(4):
-            nc.sync.dma_start(
-                f_scales[32 * q : 32 * q + 4].bitcast(I32),
-                wf_scales[:, 4 * q : 4 * q + 4, :].rearrange("b r n -> r b n").bitcast(I32),
-            )
+        load_filter()
 
-        q0, q1, q2, q3 = range(0, S, QUARTER)
-        last = PACK - 1
-
-        for i in range(PACK):
-            for j0 in (0, HALF):
-                gather(0, i, j0, HALF)
-        for j0 in (0, HALF):
-            weave_x(SCALAR, 0, j0, HALF)
-        for i in range(last):
-            for j0 in (0, HALF):
-                gather(1, i, j0, HALF)
+        gather(0, 0, 0, HALF)
+        gather(0, 0, HALF, HALF)
+        for i in range(1, PACK):
+            gather(0, i, 0, S)
+        weave_x(SCALAR, 0, 0, S)
+        gather(1, 0, 0, S)
+        gather(1, 1, 0, S)
+        quantise_x(0, 0, S, "plane5")
+        gather(1, 2, 0, S)
         for pair in range(2):
-            weave_w(SCALAR, 0, 0, pair)
+            weave_w_pair(SCALAR, 0, 0, pair)
         quantise_w(0, 0, 0, PACK)
-
-        gather(1, last, q0, QUARTER)
+        gather(1, 3, q0, QUARTER)
         weave_x(SCALAR, 1, q0, QUARTER)
-        gather(1, last, q1, QUARTER)
-        gather(1, last, q2, QUARTER)
-        weave_w(SCALAR, 0, 1, 1)
-        weave_w(VECTOR, 0, 1, 0)
-        quantise_w(0, 1, 0, PACK)
-        quantise_x(1, q0, QUARTER)
+        gather(1, 3, q1, QUARTER)
         weave_x(SCALAR, 1, q1, QUARTER)
+        gather(1, 3, HALF, HALF)
+        quantise_x(1, q0, QUARTER)
+        weave_w_pair(VECTOR, 0, 1, 0)
+        weave_w_pair(SCALAR, 0, 1, 1)
         quantise_x(1, q1, QUARTER)
-        quantise_x(0, 0, HALF)
-        for pair in (1, 0):
-            weave_w(VECTOR, 1, 0, pair)
-        square_distances(0, q0, QUARTER, 1)
-        square_distances(0, q1, QUARTER, BANK // QUARTER)
-        for j0 in (q0, q1):
-            exp_negative(0, j0, QUARTER)
+        quantise_w(0, 1, 0, 2)
+        quantise_w(0, 1, 2, 2)
 
-        gather(1, last, q3, QUARTER)
-        for j0 in (q2, q3):
-            weave_x(VECTOR, 1, j0, QUARTER)
-        quantise_x(0, HALF, HALF)
-        for j0 in (q2, q3):
-            quantise_x(1, j0, QUARTER)
-        for j0 in (q2, q3):
-            square_distances(0, j0, QUARTER, BANK // QUARTER)
-        for j0 in (q2, q3):
-            exp_negative(0, j0, QUARTER)
-        weave_w(VECTOR, 1, 1, 0)
-        quantise_w(1, 1, 0, 2)
+        def chunk(b, j0, n, per_bank, square_tag, exp_tag, on_vector=()):
+            square_distances(b, j0, n, per_bank, square_tag, on_vector)
+            exp_negative(b, j0, n, exp_tag)
+
+        def finish_h(b, j0, n, tag=None, width=None):
+            weave_h(b, j0, n, tag, width)
+            quantise_h(b, j0, n)
+
+        chunk(0, q0, QUARTER, 1, "plane0", "plane3")
+        chunk(0, q1, QUARTER, 2, "plane1", "plane4")
+        weave_w(1, 0)
         quantise_w(1, 0, 0, PACK)
-        weave_w(VECTOR, 1, 1, 1)
-        quantise_w(1, 1, 2, 2)
-        for j0 in (q0, q1):
-            weave_h(0, j0, QUARTER)
-            quantise_h(0, j0, QUARTER)
-
-        tail = [(q3, EIGHTH), (q3 + EIGHTH, EIGHTH)]
-        for j0 in (q0, q1):
-            square_distances(1, j0, QUARTER, BANK // QUARTER)
-        for j0 in (q0, q1):
-            exp_negative(1, j0, QUARTER)
-        for j0, n in [(q2, QUARTER)] + tail:
-            square_distances(1, j0, n, BANK // n)
-            exp_negative(1, j0, n)
-        for b, j0 in [(0, q2), (0, q3), (1, q0), (1, q1), (1, q2)]:
-            weave_h(b, j0, QUARTER)
-            quantise_h(b, j0, QUARTER)
-
-        features(q0, QUARTER, (VECTOR, SCALAR))
-        for j0, n in tail:
-            weave_h(1, j0, n)
-        for j0, n in tail:
-            quantise_h(1, j0, n)
-        features(q1, QUARTER, (SCALAR, SCALAR))
-        features(q2, QUARTER, (SCALAR, VECTOR))
-        features(*tail[0], (SCALAR,))
-        features(*tail[1], (VECTOR, SCALAR))
+        weave_w(1, 1)
+        quantise_w(1, 1, 0, PACK)
+        weave_x(VECTOR, 1, HALF, HALF, "w_raw11")
+        chunk(1, q0, QUARTER, 2, "plane2", "plane6")
+        finish_h(0, q0, QUARTER, "w_woven11", HALF)
+        quantise_x(1, HALF, HALF)
+        chunk(1, q1, QUARTER, 2, "plane0", "plane7")
+        finish_h(0, q1, QUARTER, "shared")
+        finish_h(1, q0, QUARTER)
+        chunk(0, q2, QUARTER, 2, "plane1", "w_raw00")
+        products(q0, QUARTER, 2, (0, 1))
+        finish_h(1, q1, QUARTER)
+        chunk(1, q2, QUARTER, 2, "plane2", "plane3")
+        products(q1, QUARTER, 2, (0, 1))
+        store(VECTOR, q0, QUARTER, 2, 0)
+        store(VECTOR, q0, QUARTER, 2, 1)
+        finish_h(0, q2, QUARTER)
+        chunk(0, q3, QUARTER, 2, "plane0", "plane4")
+        store(VECTOR, q1, QUARTER, 2, 0)
+        store(VECTOR, q1, QUARTER, 2, 1)
+        finish_h(1, q2, QUARTER)
+        chunk(1, e0, EIGHTH, 4, "plane1", "plane6")
+        chunk(1, e1, EIGHTH, 4, "plane2", "plane7")
+        products(q2, QUARTER, 2, (0,))
+        products(q2, QUARTER, 2, (1,))
+        finish_h(0, q3, QUARTER)
+        store(VECTOR, q2, QUARTER, 2, 0)
+        products(e0, EIGHTH, 1, (0,))
+        products(e1, EIGHTH, 2, (0,))
+        finish_h(1, e0, EIGHTH)
+        products(e0, EIGHTH, 1, (1,))
+        finish_h(1, e1, EIGHTH)
+        products(e1, EIGHTH, 2, (1,))
+        store(SCALAR, q2, QUARTER, 2, 1)
+        store(SCALAR, e0, EIGHTH, 1, 0)
+        store(VECTOR, e1, EIGHTH, 2, 0)
+        store(SCALAR, e1, EIGHTH, 2, 1)

@@ -1,6 +1,7 @@
 from contextlib import ExitStack
 
 import concourse.mybir as mybir
+from concourse.masks import make_identity
 
 K, T, S, H, N = 1024, 2048, 1024, 1024, 512
 FLOPS = 2 * K * H * S + 2 * H * N * S
@@ -53,6 +54,8 @@ def tile_list_radial_shell_features_kernel(tc, xT, wgt, offs, w1, mu, amp, wf_wo
         amplitudes = tile("amplitudes", [P, PASSES, 2 * PACK], F32)
         f_words = tile("f_words", [P, PASSES, 2 * N], U8)
         f_scales = tile("f_scales", [P, PASSES, N], U8)
+        identity = tile("identity", [P, P], F32)
+        shell_rows = tile("shell_rows", [P, S], F32)
         x_woven, x_codes, w_codes = {}, {}, {}
         squares, exps, h_woven = {}, {}, {}
 
@@ -61,6 +64,26 @@ def tile_list_radial_shell_features_kernel(tc, xT, wgt, offs, w1, mu, amp, wf_wo
 
         def load_weights(j0, n):
             nc.sync.dma_start(weights[:, j0 : j0 + n], wgt[:, j0 : j0 + n])
+
+        def turn(src, n):
+            bank = psum.tile([P, BANK], F32, name="turned", tag="bank")
+            for c in range(n // P):
+                nc.tensor.transpose(bank[:, P * c : P * (c + 1)], src[:, P * c : P * (c + 1)], identity[:])
+            return bank[:, :n]
+
+        def spread_weights(firsts, n):
+            blocks = n // P
+            by_entry = [turn(shell_rows[:, j0 : j0 + n], n) for j0 in firsts]
+            spread = [tile(f"spread{j0}", [P, n], F32) for j0 in firsts]
+            for dst, src in zip(spread, by_entry):
+                nc.scalar.copy(
+                    dst[:].rearrange("j (c g r) -> j c g r", c=blocks, r=LIST_ROWS),
+                    src.rearrange("j (c g r) -> j c g r", c=blocks, r=PACK)[:, :, : P // LIST_ROWS, 0:1].to_broadcast(
+                        [P, blocks, P // LIST_ROWS, LIST_ROWS]
+                    ),
+                )
+            for j0, src in zip(firsts, spread):
+                copy_on(SCALAR, weights[:, j0 : j0 + n], turn(src[:], n))
 
         def load_plane(a, i):
             nc.sync.dma_start(planes[a][i][:], x_rows[a, i])
@@ -138,13 +161,13 @@ def tile_list_radial_shell_features_kernel(tc, xT, wgt, offs, w1, mu, amp, wf_wo
         def square_distances(b, j0, n, per_bank, tag, on_vector=()):
             square = tile(f"square{b}_{j0}", [P, PACK, n], F32, tag)
             squares[(b, j0)] = square
-            pieces = sorted({k[1] for k in x_codes if j0 <= k[1] < j0 + n} | {j0}) + [j0 + n]
             for t0 in range(0, PACK, per_bank):
                 bank = psum.tile([P, BANK], F32, name="distance_bank", tag="bank")
-                for t in range(t0, t0 + per_bank):
-                    for c0, c1 in zip(pieces, pieces[1:]):
-                        lo = (t - t0) * n + c0 - j0
-                        for a in range(PASSES):
+                for a in range(PASSES):
+                    cuts = sorted({k[1] for k in x_codes if k[0] == a and j0 <= k[1] < j0 + n} | {j0}) + [j0 + n]
+                    for t in range(t0, t0 + per_bank):
+                        for c0, c1 in zip(cuts, cuts[1:]):
+                            lo = (t - t0) * n + c0 - j0
                             wc, wt = holder(w_codes, (b, a), t)
                             xc, xj = holder(x_codes, (a,), c0)
                             nc.tensor.matmul_mx(
@@ -153,8 +176,8 @@ def tile_list_radial_shell_features_kernel(tc, xT, wgt, offs, w1, mu, amp, wf_wo
                                 lhsT_scale=w_scales[b][a][:, P * t : P * (t + 1)],
                                 rhs=xc[:, xj : xj + c1 - c0].bitcast(FP8X4),
                                 rhs_scale=x_scales[a][:, c0:c1],
-                                start=(a == 0),
-                                stop=(a == PASSES - 1),
+                                start=(a == 0 and lo == 0),
+                                stop=(a == PASSES - 1 and lo + c1 - c0 == per_bank * n),
                             )
                 if t0 in on_vector:
                     shifted = tile(f"shifted{b}_{j0}_{t0}", [P, per_bank, n], F32)
@@ -242,11 +265,14 @@ def tile_list_radial_shell_features_kernel(tc, xT, wgt, offs, w1, mu, amp, wf_wo
 
         q0, q1, q2, q3 = range(0, S, QUARTER)
         e0, e1 = q3, q3 + EIGHTH
+        nc.sync.dma_start(shell_rows[:32, QUARTER:], wgt[0:P:PACK, QUARTER:])
         nc.sync.dma_start(offsets[:], offs)
+        make_identity(nc, identity[:])
+        nc.vector.memset(shell_rows[32:64, QUARTER:], 0.0)
+        nc.gpsimd.memset(shell_rows[64:, QUARTER:], 0.0)
         nc.vector.memset(f_scales[:].rearrange("p b n -> p (b n)").bitcast(I32), 0)
-        load_weights(0, HALF)
+        load_weights(0, QUARTER)
         load_plane(0, 0)
-        load_weights(HALF, HALF)
         for a, i in [divmod(plane, PACK) for plane in range(1, PASSES * PACK - 1)]:
             load_plane(a, i)
         load_w(0, 0)
@@ -258,8 +284,9 @@ def tile_list_radial_shell_features_kernel(tc, xT, wgt, offs, w1, mu, amp, wf_wo
         load_along_r(amplitudes, amp)
         load_filter()
 
-        gather(0, 0, 0, HALF)
-        gather(0, 0, HALF, HALF)
+        spread_weights((q1, q2, q3), QUARTER)
+        for j0 in (q0, q1, q2, q3):
+            gather(0, 0, j0, QUARTER)
         for i in range(1, PACK):
             gather(0, i, 0, S)
         weave_x(SCALAR, 0, 0, S)
@@ -315,19 +342,21 @@ def tile_list_radial_shell_features_kernel(tc, xT, wgt, offs, w1, mu, amp, wf_wo
         store(VECTOR, q1, QUARTER, 2, 0)
         store(VECTOR, q1, QUARTER, 2, 1)
         finish_h(1, q2, QUARTER)
-        chunk(1, e0, EIGHTH, 4, "plane1", "plane6")
-        chunk(1, e1, EIGHTH, 4, "plane2", "plane7")
+        square_distances(1, q3, QUARTER, 2, "plane1")
+        exp_negative(1, e0, EIGHTH, "plane6")
+        exp_negative(1, e1, EIGHTH, "plane7")
         products(q2, QUARTER, 2, (0,))
         products(q2, QUARTER, 2, (1,))
         finish_h(0, q3, QUARTER)
-        store(VECTOR, q2, QUARTER, 2, 0)
-        products(e0, EIGHTH, 1, (0,))
+        products(e0, EIGHTH, 2, (0,))
         products(e1, EIGHTH, 2, (0,))
         finish_h(1, e0, EIGHTH)
-        products(e0, EIGHTH, 1, (1,))
+        products(e0, EIGHTH, 2, (1,))
         finish_h(1, e1, EIGHTH)
         products(e1, EIGHTH, 2, (1,))
+        store(SCALAR, q2, QUARTER, 2, 0)
         store(SCALAR, q2, QUARTER, 2, 1)
-        store(SCALAR, e0, EIGHTH, 1, 0)
+        store(VECTOR, e0, EIGHTH, 2, 0)
+        store(SCALAR, e0, EIGHTH, 2, 1)
         store(VECTOR, e1, EIGHTH, 2, 0)
         store(SCALAR, e1, EIGHTH, 2, 1)

@@ -123,8 +123,8 @@ def tile_list_radial_shell_features_kernel(tc, xT, wgt, offs, w1, mu, amp, wf_wo
             x_woven[(a, j0)] = woven
             copy_on(
                 engine,
-                woven[:].rearrange("p (c e i) -> p c i e", e=2, i=PACK),
-                picked[a][:, :, j0 : j0 + n].rearrange("p i (c e) -> p c i e", e=2),
+                woven[:].rearrange("p (c e i) -> p c i e", e=4, i=PACK),
+                picked[a][:, :, j0 : j0 + n].rearrange("p i (c e) -> p c i e", e=4),
             )
 
         def quantise_x(a, j0, n, tag=None):
@@ -214,9 +214,9 @@ def tile_list_radial_shell_features_kernel(tc, xT, wgt, offs, w1, mu, amp, wf_wo
             woven = whole[:, PACK * start : PACK * (start + n)]
             by_t = amplitudes[:, b, :PACK].rearrange("p (c t e) -> p c t e", c=1, e=1)
             nc.vector.tensor_tensor(
-                woven.rearrange("p (c e t) -> p c t e", e=2, t=PACK),
-                gauss[:, :, first : first + n].rearrange("p t (c e) -> p c t e", e=2),
-                by_t.to_broadcast([P, n // 2, PACK, 2]),
+                woven.rearrange("p (c e t) -> p c t e", e=4, t=PACK),
+                gauss[:, :, first : first + n].rearrange("p t (c e) -> p c t e", e=4),
+                by_t.to_broadcast([P, n // 4, PACK, 4]),
                 MULT,
             )
 
@@ -317,17 +317,19 @@ def tile_list_radial_shell_features_kernel(tc, xT, wgt, offs, w1, mu, amp, wf_wo
             weave_h(b, j0, n, tag, width)
             quantise_h(b, j0, n)
 
-        chunk(0, q0, QUARTER, 1, "plane0", "plane3")
-        chunk(0, q1, QUARTER, 2, "plane1", "plane4")
+        square_distances(0, 0, HALF, 1, "plane0")
+        exp_negative(0, q0, QUARTER, "plane3")
+        exp_negative(0, q1, QUARTER, "plane4")
         weave_w(1, 0)
         quantise_w(1, 0, 0, PACK)
         weave_w(1, 1)
         quantise_w(1, 1, 0, PACK)
         weave_x(VECTOR, 1, HALF, HALF, "w_raw11")
-        chunk(1, q0, QUARTER, 2, "plane2", "plane6")
+        square_distances(1, 0, HALF, 1, "plane2")
+        exp_negative(1, q0, QUARTER, "plane6")
         finish_h(0, q0, QUARTER, "w_woven11", HALF)
         quantise_x(1, HALF, HALF)
-        chunk(1, q1, QUARTER, 2, "plane0", "plane7")
+        exp_negative(1, q1, QUARTER, "plane7")
         finish_h(0, q1, QUARTER, "shared")
         finish_h(1, q0, QUARTER)
         chunk(0, q2, QUARTER, 2, "plane1", "w_raw00")

@@ -258,7 +258,7 @@ def tile_list_radial_shell_features_kernel(tc, xT, wgt, offs, w1, mu, amp, wf_wo
             m0 = which * per_bank
             result = tile(f"staging{j0}_{which}", [P, width], F32, tag)
             copy_on(engine, result[:], banks[(j0, which)][:, :width])
-            nc.sync.dma_start(
+            (nc.scalar if engine == SCALAR else nc.sync).dma_start(
                 out[P * m0 : P * (m0 + per_bank), j0 : j0 + n].rearrange("(m p) j -> p m j", p=P),
                 result[:].rearrange("p (m j) -> p m j", j=n),
             )
@@ -266,22 +266,23 @@ def tile_list_radial_shell_features_kernel(tc, xT, wgt, offs, w1, mu, amp, wf_wo
         q0, q1, q2, q3 = range(0, S, QUARTER)
         e0, e1 = q3, q3 + EIGHTH
         nc.sync.dma_start(shell_rows[:32, QUARTER:], wgt[0:P:PACK, QUARTER:])
-        nc.sync.dma_start(offsets[:], offs)
         make_identity(nc, identity[:])
         nc.vector.memset(shell_rows[32:64, QUARTER:], 0.0)
         nc.gpsimd.memset(shell_rows[64:, QUARTER:], 0.0)
         nc.vector.memset(f_scales[:].rearrange("p b n -> p (b n)").bitcast(I32), 0)
-        load_weights(0, QUARTER)
         load_plane(0, 0)
+        nc.sync.dma_start(offsets[:], offs)
+        load_weights(0, QUARTER)
         for a, i in [divmod(plane, PACK) for plane in range(1, PASSES * PACK - 1)]:
             load_plane(a, i)
+            if (a, i) == (0, PACK - 1):
+                load_along_r(centres, mu)
+                load_along_r(amplitudes, amp)
         load_w(0, 0)
         load_plane(1, PACK - 1)
         load_w(0, 1)
-        load_along_r(centres, mu)
         load_w(1, 0)
         load_w(1, 1)
-        load_along_r(amplitudes, amp)
         load_filter()
 
         spread_weights((q1, q2, q3), QUARTER)

@@ -15,19 +15,24 @@ U8 = mybir.dt.uint8
 FP8X4 = mybir.dt.float8_e4m3fn_x4
 FP4X4 = mybir.dt.float4_e2m1fn_x4
 MULT = mybir.AluOpType.mult
-SUBTRACT = mybir.AluOpType.subtract
 ACT = mybir.ActivationFunctionType
 
 P = 128
+QUADRANT = 32
 PACK = 4
+PAIRS = PACK // 2
 PASS = P * PACK
 PASSES = K // PASS
 BANK = 512
 BANKS = 8
 LIST_ROWS = 16
+LINE = 4
 HALF = S // 2
 QUARTER = S // 4
 EIGHTH = S // 8
+OUT_STEP = 128
+OUT_BANKS = 2
+OUT_TILES = N // P // OUT_BANKS
 VECTOR, SCALAR = "vector", "scalar"
 
 
@@ -37,17 +42,24 @@ def tile_list_radial_shell_features_kernel(tc, xT, wgt, offs, w1, mu, amp, wf_wo
         keep = ctx.enter_context(tc.tile_pool(name="keep", bufs=1))
         psum = ctx.enter_context(tc.psum_pool(name="psum", bufs=BANKS))
 
-        def tile(name, shape, dtype, tag=None):
-            return keep.tile(shape, dtype, name=name, tag=tag or name, align_bytes=64)
+        def tile(name, shape, dtype, on=None):
+            return keep.tile(shape, dtype, name=name, tag=on or name, align_bytes=64)
+
+        def grid(name, shape, dtype):
+            return [[tile(f"{name}{b}{a}", shape, dtype) for a in range(PASSES)] for b in range(PASSES)]
+
+        def next_bank():
+            return psum.tile([P, BANK], F32, name="bank", tag="bank")
 
         offsets = keep.tile([P, S // LIST_ROWS], U16, name="offsets")
         weights = tile("weights", [P, S], F32)
         planes = [[tile(f"plane{PACK * a + i}", [P, T], F32) for i in range(PACK)] for a in range(PASSES)]
         picked = [tile(f"picked{a}", [P, PACK, S], F32) for a in range(PASSES)]
-        w_raw = [[tile(f"w_raw{b}{a}", [P, PACK, PASS], F32) for a in range(PASSES)] for b in range(PASSES)]
-        w_woven = [[tile(f"w_woven{b}{a}", [P, PACK * P * PACK], BF16) for a in range(PASSES)] for b in range(PASSES)]
-        w_scales = [[tile(f"w_scales{b}{a}", [P, PASS], U8) for a in range(PASSES)] for b in range(PASSES)]
         x_scales = [tile(f"x_scales{a}", [P, S], U8) for a in range(PASSES)]
+        w_raw = grid("w_raw", [P, PACK, PASS], F32)
+        w_woven = grid("w_woven", [P, PACK * P * PACK], BF16)
+        w_codes = grid("w_codes", [P, PASS], U32)
+        w_scales = grid("w_scales", [P, PASS], U8)
         h_codes = [tile(f"h_codes{b}", [P, S], U32) for b in range(PASSES)]
         h_scales = [tile(f"h_scales{b}", [P, S], U8) for b in range(PASSES)]
         centres = tile("centres", [P, PASSES, 2 * PACK], F32)
@@ -55,35 +67,15 @@ def tile_list_radial_shell_features_kernel(tc, xT, wgt, offs, w1, mu, amp, wf_wo
         f_words = tile("f_words", [P, PASSES, 2 * N], U8)
         f_scales = tile("f_scales", [P, PASSES, N], U8)
         identity = tile("identity", [P, P], F32)
-        shell_rows = tile("shell_rows", [P, S], F32)
-        x_woven, x_codes, w_codes = {}, {}, {}
-        squares, exps, h_woven = {}, {}, {}
+        shell_rows = tile("shell_rows", [P, S - QUARTER], F32)
+        x_woven, x_codes, squares, exps, h_woven, out_banks = {}, {}, {}, {}, {}, {}
 
         x_rows = xT.rearrange("(a p i) t -> a i p t", a=PASSES, i=PACK)
         w_rows = w1.rearrange("(a p i) r -> a p i r", a=PASSES, i=PACK)
 
-        def load_weights(j0, n):
-            nc.sync.dma_start(weights[:, j0 : j0 + n], wgt[:, j0 : j0 + n])
-
-        def turn(src, n):
-            bank = psum.tile([P, BANK], F32, name="turned", tag="bank")
-            for c in range(n // P):
-                nc.tensor.transpose(bank[:, P * c : P * (c + 1)], src[:, P * c : P * (c + 1)], identity[:])
-            return bank[:, :n]
-
-        def spread_weights(firsts, n):
-            blocks = n // P
-            by_entry = [turn(shell_rows[:, j0 : j0 + n], n) for j0 in firsts]
-            spread = [tile(f"spread{j0}", [P, n], F32) for j0 in firsts]
-            for dst, src in zip(spread, by_entry):
-                nc.scalar.copy(
-                    dst[:].rearrange("j (c g r) -> j c g r", c=blocks, r=LIST_ROWS),
-                    src.rearrange("j (c g r) -> j c g r", c=blocks, r=PACK)[:, :, : P // LIST_ROWS, 0:1].to_broadcast(
-                        [P, blocks, P // LIST_ROWS, LIST_ROWS]
-                    ),
-                )
-            for j0, src in zip(firsts, spread):
-                copy_on(SCALAR, weights[:, j0 : j0 + n], turn(src[:], n))
+        def holder(tiles, index, j0):
+            first = max(start for which, start in tiles if which == index and start <= j0)
+            return tiles[(index, first)], j0 - first
 
         def load_plane(a, i):
             nc.sync.dma_start(planes[a][i][:], x_rows[a, i])
@@ -94,23 +86,30 @@ def tile_list_radial_shell_features_kernel(tc, xT, wgt, offs, w1, mu, amp, wf_wo
         def load_along_r(dst, vector):
             nc.sync.dma_start(dst[:, :, :PACK], vector.rearrange("(b p t) -> p b t", b=PASSES, t=PACK))
 
-        def load_filter():
-            nc.sync.dma_start(f_words[:].bitcast(I32), wf_words.rearrange("b p n -> p b n").bitcast(I32))
-            for q in range(4):
-                nc.sync.dma_start(
-                    f_scales[32 * q : 32 * q + 4].bitcast(I32),
-                    wf_scales[:, 4 * q : 4 * q + 4, :].rearrange("b r n -> r b n").bitcast(I32),
-                )
-
         def copy_on(engine, dst, src):
             if engine == VECTOR:
                 nc.vector.tensor_copy(dst, src)
             else:
                 nc.scalar.activation(dst, src, ACT.Copy)
 
-        def holder(tiles, key, j0):
-            first = max(k[-1] for k in tiles if k[:-1] == key and k[-1] <= j0)
-            return tiles[key + (first,)], j0 - first
+        def turn(src, n):
+            bank = next_bank()
+            for c in range(n // P):
+                nc.tensor.transpose(bank[:, P * c : P * (c + 1)], src[:, P * c : P * (c + 1)], identity[:])
+            return bank[:, :n]
+
+        def spread_weights(firsts, n):
+            blocks, repeats = n // P, P // QUADRANT
+            by_entry = [turn(shell_rows[:, j0 - QUARTER : j0 - QUARTER + n], n) for j0 in firsts]
+            spread = [tile(f"spread{j0}", [P, n], F32) for j0 in firsts]
+            for dst, src in zip(spread, by_entry):
+                rows = src.rearrange("j (c g e) -> j c g e", c=blocks, e=1)[:, :, :QUADRANT]
+                nc.scalar.copy(
+                    dst[:].rearrange("j (c g e) -> j c g e", c=blocks, e=repeats),
+                    rows.to_broadcast([P, blocks, QUADRANT, repeats]),
+                )
+            for j0, src in zip(firsts, spread):
+                copy_on(SCALAR, weights[:, j0 : j0 + n], turn(src[:], n))
 
         def gather(a, i, j0, n):
             listed = offsets[:, j0 // LIST_ROWS : (j0 + n) // LIST_ROWS]
@@ -118,77 +117,59 @@ def tile_list_radial_shell_features_kernel(tc, xT, wgt, offs, w1, mu, amp, wf_wo
                 picked[a][:, i, j0 : j0 + n], planes[a][i][:].indirect(listed), weights[:, j0 : j0 + n], MULT
             )
 
-        def weave_x(engine, a, j0, n, tag=None):
-            woven = tile(f"x_woven{a}_{j0}", [P, n * PACK], BF16, tag)
+        def weave_x(engine, a, j0, n):
+            woven = tile(f"x_woven{a}_{j0}", [P, n * PACK], BF16)
             x_woven[(a, j0)] = woven
             copy_on(
                 engine,
-                woven[:].rearrange("p (c e i) -> p c i e", e=4, i=PACK),
-                picked[a][:, :, j0 : j0 + n].rearrange("p i (c e) -> p c i e", e=4),
+                woven[:].rearrange("p (c e i) -> p c i e", e=LINE, i=PACK),
+                picked[a][:, :, j0 : j0 + n].rearrange("p i (c e) -> p c i e", e=LINE),
             )
 
-        def quantise_x(a, j0, n, tag=None):
-            woven, first = holder(x_woven, (a,), j0)
-            codes = tile(f"x_codes{a}_{j0}", [P, n], U32, tag)
+        def quantise_x(a, j0, n, on=None):
+            codes = tile(f"x_codes{a}_{j0}", [P, n], U32, on)
             x_codes[(a, j0)] = codes
+            nc.vector.quantize_mx(codes[:].bitcast(FP8X4), x_scales[a][:, j0 : j0 + n], x_woven[(a, j0)][:])
+
+        def woven_w(b, a, t0, count):
+            if (b, a, t0) == (PASSES - 1, PASSES - 1, PACK - 2):
+                return picked[PASSES - 1][:, PACK - 1, HALF:].bitcast(BF16)
+            return w_woven[b][a][:, P * PACK * t0 : P * PACK * (t0 + count)]
+
+        def weave_w(engine, b, a):
+            for pair in range(PAIRS):
+                copy_on(
+                    engine,
+                    woven_w(b, a, 2 * pair, 2).rearrange("p (e m i) -> p m i e", e=2, i=PACK),
+                    w_raw[b][a][:].rearrange("p i (m v e) -> p v m i e", v=PAIRS, e=2)[:, pair],
+                )
+
+        def quantise_w(b, a, t0, count):
+            cols = slice(P * t0, P * (t0 + count))
             nc.vector.quantize_mx(
-                codes[:].bitcast(FP8X4), x_scales[a][:, j0 : j0 + n], woven[:, PACK * first : PACK * (first + n)]
+                w_codes[b][a][:, cols].bitcast(FP8X4), w_scales[b][a][:, cols], woven_w(b, a, t0, count)
             )
 
-        def weave_w_pair(engine, b, a, pair):
-            width = 2 * P * PACK
-            copy_on(
-                engine,
-                w_woven[b][a][:, pair * width : (pair + 1) * width].rearrange("p (e m i) -> p m i e", e=2, i=PACK),
-                w_raw[b][a][:].rearrange("p i (m v e) -> p v m i e", v=2, e=2)[:, pair],
-            )
-
-        def weave_w(b, a):
-            nc.vector.tensor_copy(
-                w_woven[b][a][:].rearrange("p (v e m i) -> p v m i e", v=2, e=2, i=PACK),
-                w_raw[b][a][:].rearrange("p i (m v e) -> p v m i e", v=2, e=2),
-            )
-
-        def quantise_w(b, a, t0, count, tag=None):
-            codes = tile(f"w_codes{b}{a}_{t0}", [P, P * count], U32, tag)
-            w_codes[(b, a, t0)] = codes
-            nc.vector.quantize_mx(
-                codes[:].bitcast(FP8X4),
-                w_scales[b][a][:, P * t0 : P * (t0 + count)],
-                w_woven[b][a][:, P * PACK * t0 : P * PACK * (t0 + count)],
-            )
-
-        def square_distances(b, j0, n, per_bank, tag, on_vector=()):
-            square = tile(f"square{b}_{j0}", [P, PACK, n], F32, tag)
+        def square_distances(b, j0, n, per_bank, on):
+            square = tile(f"square{b}_{j0}", [P, PACK, n], F32, on)
             squares[(b, j0)] = square
             for t0 in range(0, PACK, per_bank):
-                bank = psum.tile([P, BANK], F32, name="distance_bank", tag="bank")
+                bank = next_bank()
                 for a in range(PASSES):
-                    cuts = sorted({k[1] for k in x_codes if k[0] == a and j0 <= k[1] < j0 + n} | {j0}) + [j0 + n]
+                    cuts = [j0] + [start for which, start in x_codes if which == a and j0 < start < j0 + n] + [j0 + n]
                     for t in range(t0, t0 + per_bank):
                         for c0, c1 in zip(cuts, cuts[1:]):
-                            lo = (t - t0) * n + c0 - j0
-                            wc, wt = holder(w_codes, (b, a), t)
-                            xc, xj = holder(x_codes, (a,), c0)
+                            first_out = (t - t0) * n + c0 - j0
+                            codes, first = holder(x_codes, a, c0)
                             nc.tensor.matmul_mx(
-                                bank[:, lo : lo + c1 - c0],
-                                lhsT=wc[:, P * wt : P * (wt + 1)].bitcast(FP8X4),
+                                bank[:, first_out : first_out + c1 - c0],
+                                lhsT=w_codes[b][a][:, P * t : P * (t + 1)].bitcast(FP8X4),
                                 lhsT_scale=w_scales[b][a][:, P * t : P * (t + 1)],
-                                rhs=xc[:, xj : xj + c1 - c0].bitcast(FP8X4),
+                                rhs=codes[:, first : first + c1 - c0].bitcast(FP8X4),
                                 rhs_scale=x_scales[a][:, c0:c1],
-                                start=(a == 0 and lo == 0),
-                                stop=(a == PASSES - 1 and lo + c1 - c0 == per_bank * n),
+                                start=(a == 0 and first_out == 0),
+                                stop=(a == PASSES - 1 and first_out + c1 - c0 == per_bank * n),
                             )
-                if t0 in on_vector:
-                    shifted = tile(f"shifted{b}_{j0}_{t0}", [P, per_bank, n], F32)
-                    nc.vector.tensor_tensor(
-                        shifted[:],
-                        bank[:, : per_bank * n].rearrange("p (t j) -> p t j", j=n),
-                        centres[:, b, t0 : t0 + per_bank].unsqueeze(2).to_broadcast([P, per_bank, n]),
-                        SUBTRACT,
-                    )
-                    nc.vector.tensor_tensor(square[:, t0 : t0 + per_bank, :], shifted[:], shifted[:], MULT)
-                    continue
                 for t in range(t0, t0 + per_bank):
                     nc.scalar.activation(
                         square[:, t, :],
@@ -198,92 +179,83 @@ def tile_list_radial_shell_features_kernel(tc, xT, wgt, offs, w1, mu, amp, wf_wo
                         scale=-1.0,
                     )
 
-        def exp_negative(b, j0, n, tag):
-            square, first = holder(squares, (b,), j0)
-            gauss = tile(f"gauss{b}_{j0}", [P, PACK, n], F32, tag)
+        def exp_negative(b, j0, n, on):
+            square, first = holder(squares, b, j0)
+            gauss = tile(f"gauss{b}_{j0}", [P, PACK, n], F32, on)
             exps[(b, j0)] = gauss
             nc.scalar.activation(gauss[:], square[:, :, first : first + n], ACT.Exp, scale=-1.0)
 
-        def weave_h(b, j0, n, tag, width=None):
-            gauss, first = holder(exps, (b,), j0)
-            if tag == "shared":
-                whole, start = holder(h_woven, (b,), j0)
-            else:
-                whole, start = tile(f"h_woven{b}_{j0}", [P, (width or n) * PACK], BF16, tag), 0
-                h_woven[(b, j0)] = whole
-            woven = whole[:, PACK * start : PACK * (start + n)]
+        def make_h(b, j0, n):
+            if (b, j0) not in h_woven:
+                h_woven[(b, j0)] = tile(f"h_woven{b}_{j0}", [P, n * PACK], BF16)[:]
+            woven = h_woven[(b, j0)]
             by_t = amplitudes[:, b, :PACK].rearrange("p (c t e) -> p c t e", c=1, e=1)
             nc.vector.tensor_tensor(
-                woven.rearrange("p (c e t) -> p c t e", e=4, t=PACK),
-                gauss[:, :, first : first + n].rearrange("p t (c e) -> p c t e", e=4),
-                by_t.to_broadcast([P, n // 4, PACK, 4]),
+                woven.rearrange("p (c e t) -> p c t e", e=LINE, t=PACK),
+                exps[(b, j0)][:].rearrange("p t (c e) -> p c t e", e=LINE),
+                by_t.to_broadcast([P, n // LINE, PACK, LINE]),
                 MULT,
             )
+            nc.vector.quantize_mx(h_codes[b][:, j0 : j0 + n].bitcast(FP8X4), h_scales[b][:, j0 : j0 + n], woven)
 
-        def quantise_h(b, j0, n):
-            woven, first = holder(h_woven, (b,), j0)
-            nc.vector.quantize_mx(
-                h_codes[b][:, j0 : j0 + n].bitcast(FP8X4),
-                h_scales[b][:, j0 : j0 + n],
-                woven[:, PACK * first : PACK * (first + n)],
-            )
+        def features(j0, n, halves):
+            for which in range(OUT_BANKS):
+                if (which, j0) not in out_banks:
+                    out_banks[(which, j0)] = next_bank()
+                for b in halves:
+                    for first_out in range(0, OUT_TILES * n, OUT_STEP):
+                        m = OUT_TILES * which + first_out // n
+                        moving = slice(j0 + first_out % n, j0 + first_out % n + OUT_STEP)
+                        nc.tensor.matmul_mx(
+                            out_banks[(which, j0)][:, first_out : first_out + OUT_STEP],
+                            lhsT=f_words[:, b, 2 * P * m : 2 * P * (m + 1)].bitcast(FP4X4),
+                            lhsT_scale=f_scales[:, b, P * m : P * (m + 1)],
+                            rhs=h_codes[b][:, moving].bitcast(FP8X4),
+                            rhs_scale=h_scales[b][:, moving],
+                            start=(b == 0 and first_out == 0),
+                            stop=(b == PASSES - 1 and first_out + OUT_STEP == OUT_TILES * n),
+                        )
 
-        banks, stagings = {}, {}
-
-        def products(j0, n, count, blocks):
-            per_bank = (N // P) // count
-            step = BANK if n == BANK else P
-            for m0 in range(0, N // P, per_bank):
-                if 0 in blocks:
-                    banks[(j0, m0 // per_bank)] = psum.tile([P, BANK], F32, name="feature_bank", tag="bank")
-                bank = banks[(j0, m0 // per_bank)]
-                for b in blocks:
-                    for m in range(m0, m0 + per_bank):
-                        for s0 in range(0, n, step):
-                            moving = slice(j0 + s0, j0 + s0 + step)
-                            first_out = (m - m0) * n + s0
-                            nc.tensor.matmul_mx(
-                                bank[:, first_out : first_out + step],
-                                lhsT=f_words[:, b, 2 * P * m : 2 * P * (m + 1)].bitcast(FP4X4),
-                                lhsT_scale=f_scales[:, b, P * m : P * (m + 1)],
-                                rhs=h_codes[b][:, moving].bitcast(FP8X4),
-                                rhs_scale=h_scales[b][:, moving],
-                                start=(b == 0 and first_out == 0),
-                                stop=(b == PASSES - 1 and first_out + step == per_bank * n),
-                            )
-
-        def store(engine, j0, n, count, which, tag=None):
-            per_bank = (N // P) // count
-            width = per_bank * n
-            m0 = which * per_bank
-            result = tile(f"staging{j0}_{which}", [P, width], F32, tag)
-            copy_on(engine, result[:], banks[(j0, which)][:, :width])
-            (nc.scalar if engine == SCALAR else nc.sync).dma_start(
-                out[P * m0 : P * (m0 + per_bank), j0 : j0 + n].rearrange("(m p) j -> p m j", p=P),
-                result[:].rearrange("p (m j) -> p m j", j=n),
-            )
+        def store(j0, n, engines):
+            for which, engine in enumerate(engines):
+                result = tile(f"result{which}_{j0}", [P, OUT_TILES * n], F32)
+                copy_on(engine, result[:], out_banks[(which, j0)][:, : OUT_TILES * n])
+                rows = slice(P * OUT_TILES * which, P * OUT_TILES * (which + 1))
+                queue = nc.scalar if engine == SCALAR else nc.sync
+                queue.dma_start(
+                    out[rows, j0 : j0 + n].rearrange("(m p) j -> p m j", p=P),
+                    result[:].rearrange("p (m j) -> p m j", j=n),
+                )
 
         q0, q1, q2, q3 = range(0, S, QUARTER)
         e0, e1 = q3, q3 + EIGHTH
-        nc.sync.dma_start(shell_rows[:32, QUARTER:], wgt[0:P:PACK, QUARTER:])
+        last = PACK - 1
+
+        nc.sync.dma_start(shell_rows[:QUADRANT], wgt[0 : P : P // QUADRANT, QUARTER:])
         make_identity(nc, identity[:])
-        nc.vector.memset(shell_rows[32:64, QUARTER:], 0.0)
-        nc.gpsimd.memset(shell_rows[64:, QUARTER:], 0.0)
+        nc.vector.memset(shell_rows[QUADRANT : 2 * QUADRANT], 0.0)
+        nc.gpsimd.memset(shell_rows[2 * QUADRANT :], 0.0)
         nc.vector.memset(f_scales[:].rearrange("p b n -> p (b n)").bitcast(I32), 0)
         load_plane(0, 0)
         nc.sync.dma_start(offsets[:], offs)
-        load_weights(0, QUARTER)
-        for a, i in [divmod(plane, PACK) for plane in range(1, PASSES * PACK - 1)]:
-            load_plane(a, i)
-            if (a, i) == (0, PACK - 1):
-                load_along_r(centres, mu)
-                load_along_r(amplitudes, amp)
+        nc.sync.dma_start(weights[:, :QUARTER], wgt[:, :QUARTER])
+        for i in range(1, PACK):
+            load_plane(0, i)
+        load_along_r(centres, mu)
+        load_along_r(amplitudes, amp)
+        for i in range(last):
+            load_plane(1, i)
         load_w(0, 0)
-        load_plane(1, PACK - 1)
+        load_plane(1, last)
         load_w(0, 1)
         load_w(1, 0)
         load_w(1, 1)
-        load_filter()
+        nc.sync.dma_start(f_words[:].bitcast(I32), wf_words.rearrange("b p n -> p b n").bitcast(I32))
+        for q in range(P // QUADRANT):
+            nc.sync.dma_start(
+                f_scales[QUADRANT * q : QUADRANT * q + 4].bitcast(I32),
+                wf_scales[:, 4 * q : 4 * q + 4, :].rearrange("b r n -> r b n").bitcast(I32),
+            )
 
         spread_weights((q1, q2, q3), QUARTER)
         for j0 in (q0, q1, q2, q3):
@@ -293,73 +265,69 @@ def tile_list_radial_shell_features_kernel(tc, xT, wgt, offs, w1, mu, amp, wf_wo
         weave_x(SCALAR, 0, 0, S)
         gather(1, 0, 0, S)
         gather(1, 1, 0, S)
-        quantise_x(0, 0, S, "plane5")
+        quantise_x(0, 0, S, on="plane5")
         gather(1, 2, 0, S)
-        for pair in range(2):
-            weave_w_pair(SCALAR, 0, 0, pair)
+        weave_w(SCALAR, 0, 0)
         quantise_w(0, 0, 0, PACK)
-        gather(1, 3, q0, QUARTER)
-        weave_x(SCALAR, 1, q0, QUARTER)
-        gather(1, 3, q1, QUARTER)
-        weave_x(SCALAR, 1, q1, QUARTER)
-        gather(1, 3, HALF, HALF)
-        quantise_x(1, q0, QUARTER)
-        weave_w_pair(VECTOR, 0, 1, 0)
-        weave_w_pair(SCALAR, 0, 1, 1)
-        quantise_x(1, q1, QUARTER)
+
+        for j0 in (q0, q1):
+            gather(1, last, j0, QUARTER)
+            weave_x(SCALAR, 1, j0, QUARTER)
+        weave_w(VECTOR, 0, 1)
         quantise_w(0, 1, 0, 2)
+        quantise_x(1, q0, QUARTER, on="w_raw01")
         quantise_w(0, 1, 2, 2)
+        quantise_x(1, q1, QUARTER)
 
-        def chunk(b, j0, n, per_bank, square_tag, exp_tag, on_vector=()):
-            square_distances(b, j0, n, per_bank, square_tag, on_vector)
-            exp_negative(b, j0, n, exp_tag)
+        square_distances(0, q0, QUARTER, 1, on="plane0")
+        exp_negative(0, q0, QUARTER, on="plane3")
+        square_distances(0, q1, QUARTER, 2, on="plane1")
+        exp_negative(0, q1, QUARTER, on="plane4")
 
-        def finish_h(b, j0, n, tag=None, width=None):
-            weave_h(b, j0, n, tag, width)
-            quantise_h(b, j0, n)
+        for a in range(PASSES):
+            weave_w(VECTOR, 1, a)
+            for pair in range(PAIRS):
+                quantise_w(1, a, 2 * pair, 2)
+        gather(1, last, HALF, HALF)
+        for j0 in (q2, q3):
+            weave_x(VECTOR, 1, j0, QUARTER)
+        for j0 in (q2, q3):
+            quantise_x(1, j0, QUARTER)
+        early_h = tile("early_h", [P, HALF * PACK], BF16, on="w_woven11")
+        for j0 in (q0, q1):
+            h_woven[(0, j0)] = early_h[:, PACK * j0 : PACK * (j0 + QUARTER)]
 
-        square_distances(0, 0, HALF, 1, "plane0")
-        exp_negative(0, q0, QUARTER, "plane3")
-        exp_negative(0, q1, QUARTER, "plane4")
-        weave_w(1, 0)
-        quantise_w(1, 0, 0, PACK)
-        weave_w(1, 1)
-        quantise_w(1, 1, 0, PACK)
-        weave_x(VECTOR, 1, HALF, HALF, "w_raw11")
-        square_distances(1, 0, HALF, 1, "plane2")
-        exp_negative(1, q0, QUARTER, "plane6")
-        finish_h(0, q0, QUARTER, "w_woven11", HALF)
-        quantise_x(1, HALF, HALF)
-        exp_negative(1, q1, QUARTER, "plane7")
-        finish_h(0, q1, QUARTER, "shared")
-        finish_h(1, q0, QUARTER)
-        chunk(0, q2, QUARTER, 2, "plane1", "w_raw00")
-        products(q0, QUARTER, 2, (0, 1))
-        finish_h(1, q1, QUARTER)
-        chunk(1, q2, QUARTER, 2, "plane2", "plane3")
-        products(q1, QUARTER, 2, (0, 1))
-        store(VECTOR, q0, QUARTER, 2, 0)
-        store(VECTOR, q0, QUARTER, 2, 1)
-        finish_h(0, q2, QUARTER)
-        chunk(0, q3, QUARTER, 2, "plane0", "plane4")
-        store(VECTOR, q1, QUARTER, 2, 0)
-        store(VECTOR, q1, QUARTER, 2, 1)
-        finish_h(1, q2, QUARTER)
-        square_distances(1, q3, QUARTER, 2, "plane1")
-        exp_negative(1, e0, EIGHTH, "plane6")
-        exp_negative(1, e1, EIGHTH, "plane7")
-        products(q2, QUARTER, 2, (0,))
-        products(q2, QUARTER, 2, (1,))
-        finish_h(0, q3, QUARTER)
-        products(e0, EIGHTH, 2, (0,))
-        products(e1, EIGHTH, 2, (0,))
-        finish_h(1, e0, EIGHTH)
-        products(e0, EIGHTH, 2, (1,))
-        finish_h(1, e1, EIGHTH)
-        products(e1, EIGHTH, 2, (1,))
-        store(SCALAR, q2, QUARTER, 2, 0)
-        store(SCALAR, q2, QUARTER, 2, 1)
-        store(VECTOR, e0, EIGHTH, 2, 0)
-        store(SCALAR, e0, EIGHTH, 2, 1)
-        store(VECTOR, e1, EIGHTH, 2, 0)
-        store(SCALAR, e1, EIGHTH, 2, 1)
+        square_distances(1, 0, HALF, 1, on="plane2")
+        exp_negative(1, q0, QUARTER, on="plane6")
+        make_h(0, q0, QUARTER)
+        exp_negative(1, q1, QUARTER, on="plane7")
+        make_h(0, q1, QUARTER)
+        make_h(1, q0, QUARTER)
+        square_distances(0, q2, QUARTER, 2, on="plane1")
+        exp_negative(0, q2, QUARTER, on="w_raw00")
+        features(q0, QUARTER, (0, 1))
+        make_h(1, q1, QUARTER)
+        square_distances(1, q2, QUARTER, 2, on="plane2")
+        exp_negative(1, q2, QUARTER, on="plane3")
+        features(q1, QUARTER, (0, 1))
+        store(q0, QUARTER, (VECTOR, VECTOR))
+        make_h(0, q2, QUARTER)
+        square_distances(0, q3, QUARTER, 2, on="plane0")
+        exp_negative(0, q3, QUARTER, on="plane4")
+        store(q1, QUARTER, (VECTOR, VECTOR))
+        make_h(1, q2, QUARTER)
+
+        square_distances(1, q3, QUARTER, 2, on="plane1")
+        exp_negative(1, e0, EIGHTH, on="plane6")
+        exp_negative(1, e1, EIGHTH, on="plane7")
+        for b in range(PASSES):
+            features(q2, QUARTER, (b,))
+        make_h(0, q3, QUARTER)
+        for j0 in (e0, e1):
+            features(j0, EIGHTH, (0,))
+        for j0 in (e0, e1):
+            make_h(1, j0, EIGHTH)
+            features(j0, EIGHTH, (1,))
+        store(q2, QUARTER, (SCALAR, SCALAR))
+        for j0 in (e0, e1):
+            store(j0, EIGHTH, (VECTOR, SCALAR))

@@ -25,6 +25,7 @@ PASS = P * PACK
 PASSES = K // PASS
 BANK = 512
 BANKS = 8
+SHELLS = 8
 LIST_ROWS = 16
 LINE = 4
 HALF = S // 2
@@ -67,7 +68,7 @@ def tile_list_radial_shell_features_kernel(tc, xT, wgt, offs, w1, mu, amp, wf_wo
         f_words = tile("f_words", [P, PASSES, 2 * N], U8)
         f_scales = tile("f_scales", [P, PASSES, N], U8)
         identity = tile("identity", [P, P], F32)
-        shell_rows = tile("shell_rows", [P, S - QUARTER], F32)
+        shell_blocks = tile("shell_blocks", [P, P], F32)
         x_woven, x_codes, squares, exps, h_woven, out_banks = {}, {}, {}, {}, {}, {}
 
         x_rows = xT.rearrange("(a p i) t -> a i p t", a=PASSES, i=PACK)
@@ -99,14 +100,13 @@ def tile_list_radial_shell_features_kernel(tc, xT, wgt, offs, w1, mu, amp, wf_wo
             return bank[:, :n]
 
         def spread_weights(firsts, n):
-            blocks, repeats = n // P, P // QUADRANT
-            by_entry = [turn(shell_rows[:, j0 - QUARTER : j0 - QUARTER + n], n) for j0 in firsts]
+            blocks = n // P
+            by_entry = turn(shell_blocks[:], P)[:, : SHELLS * S // P].rearrange("j (g c e) -> j c g e", g=SHELLS, e=1)
             spread = [tile(f"spread{j0}", [P, n], F32) for j0 in firsts]
-            for dst, src in zip(spread, by_entry):
-                rows = src.rearrange("j (c g e) -> j c g e", c=blocks, e=1)[:, :, :QUADRANT]
+            for j0, dst in zip(firsts, spread):
                 nc.scalar.copy(
-                    dst[:].rearrange("j (c g e) -> j c g e", c=blocks, e=repeats),
-                    rows.to_broadcast([P, blocks, QUADRANT, repeats]),
+                    dst[:].rearrange("j (c g e) -> j c g e", c=blocks, e=LIST_ROWS),
+                    by_entry[:, j0 // P : j0 // P + blocks].to_broadcast([P, blocks, SHELLS, LIST_ROWS]),
                 )
             for j0, src in zip(firsts, spread):
                 copy_on(SCALAR, weights[:, j0 : j0 + n], turn(src[:], n))
@@ -150,7 +150,7 @@ def tile_list_radial_shell_features_kernel(tc, xT, wgt, offs, w1, mu, amp, wf_wo
                 w_codes[b][a][:, cols].bitcast(FP8X4), w_scales[b][a][:, cols], woven_w(b, a, t0, count)
             )
 
-        def square_distances(b, j0, n, per_bank, on):
+        def square_distances(b, j0, n, per_bank, on, exps_after=1):
             square = tile(f"square{b}_{j0}", [P, PACK, n], F32, on)
             squares[(b, j0)] = square
             for t0 in range(0, PACK, per_bank):
@@ -171,13 +171,15 @@ def tile_list_radial_shell_features_kernel(tc, xT, wgt, offs, w1, mu, amp, wf_wo
                                 stop=(a == PASSES - 1 and first_out + c1 - c0 == per_bank * n),
                             )
                 for t in range(t0, t0 + per_bank):
-                    nc.scalar.activation(
-                        square[:, t, :],
-                        bank[:, (t - t0) * n : (t - t0 + 1) * n],
-                        ACT.Square,
-                        bias=centres[:, b, t : t + 1],
-                        scale=-1.0,
-                    )
+                    step = n // exps_after if t == PACK - 1 else n
+                    for c0 in range(0, n, step):
+                        nc.scalar.activation(
+                            square[:, t, c0 : c0 + step],
+                            bank[:, (t - t0) * n + c0 : (t - t0) * n + c0 + step],
+                            ACT.Square,
+                            bias=centres[:, b, t : t + 1],
+                            scale=-1.0,
+                        )
 
         def exp_negative(b, j0, n, on):
             square, first = holder(squares, b, j0)
@@ -185,7 +187,7 @@ def tile_list_radial_shell_features_kernel(tc, xT, wgt, offs, w1, mu, amp, wf_wo
             exps[(b, j0)] = gauss
             nc.scalar.activation(gauss[:], square[:, :, first : first + n], ACT.Exp, scale=-1.0)
 
-        def make_h(b, j0, n):
+        def weave_h(b, j0, n):
             if (b, j0) not in h_woven:
                 h_woven[(b, j0)] = tile(f"h_woven{b}_{j0}", [P, n * PACK], BF16)[:]
             woven = h_woven[(b, j0)]
@@ -196,7 +198,11 @@ def tile_list_radial_shell_features_kernel(tc, xT, wgt, offs, w1, mu, amp, wf_wo
                 by_t.to_broadcast([P, n // LINE, PACK, LINE]),
                 MULT,
             )
-            nc.vector.quantize_mx(h_codes[b][:, j0 : j0 + n].bitcast(FP8X4), h_scales[b][:, j0 : j0 + n], woven)
+
+        def quantise_h(b, j0, n):
+            nc.vector.quantize_mx(
+                h_codes[b][:, j0 : j0 + n].bitcast(FP8X4), h_scales[b][:, j0 : j0 + n], h_woven[(b, j0)]
+            )
 
         def features(j0, n, halves):
             for which in range(OUT_BANKS):
@@ -216,29 +222,27 @@ def tile_list_radial_shell_features_kernel(tc, xT, wgt, offs, w1, mu, amp, wf_wo
                             stop=(b == PASSES - 1 and first_out + OUT_STEP == OUT_TILES * n),
                         )
 
-        def store(j0, n, engines):
-            for which, engine in enumerate(engines):
-                result = tile(f"result{which}_{j0}", [P, OUT_TILES * n], F32)
-                copy_on(engine, result[:], out_banks[(which, j0)][:, : OUT_TILES * n])
-                rows = slice(P * OUT_TILES * which, P * OUT_TILES * (which + 1))
-                queue = nc.scalar if engine == SCALAR else nc.sync
-                queue.dma_start(
-                    out[rows, j0 : j0 + n].rearrange("(m p) j -> p m j", p=P),
-                    result[:].rearrange("p (m j) -> p m j", j=n),
-                )
+        def store(j0, n, which, engine):
+            result = tile(f"result{which}_{j0}", [P, OUT_TILES * n], F32)
+            copy_on(engine, result[:], out_banks[(which, j0)][:, : OUT_TILES * n])
+            rows = slice(P * OUT_TILES * which, P * OUT_TILES * (which + 1))
+            queue = nc.scalar if engine == SCALAR else nc.sync
+            queue.dma_start(
+                out[rows, j0 : j0 + n].rearrange("(m p) j -> p m j", p=P),
+                result[:].rearrange("p (m j) -> p m j", j=n),
+            )
 
         q0, q1, q2, q3 = range(0, S, QUARTER)
         e0, e1 = q3, q3 + EIGHTH
         last = PACK - 1
 
-        nc.sync.dma_start(shell_rows[:QUADRANT], wgt[0 : P : P // QUADRANT, QUARTER:])
+        nc.sync.dma_start(shell_blocks[: P // 2], wgt[0:P:LIST_ROWS, :].rearrange("g (c u) -> g c u", u=P))
         make_identity(nc, identity[:])
-        nc.vector.memset(shell_rows[QUADRANT : 2 * QUADRANT], 0.0)
-        nc.gpsimd.memset(shell_rows[2 * QUADRANT :], 0.0)
+        nc.vector.memset(shell_blocks[P // 2 :], 0.0)
         nc.vector.memset(f_scales[:].rearrange("p b n -> p (b n)").bitcast(I32), 0)
-        load_plane(0, 0)
         nc.sync.dma_start(offsets[:], offs)
         nc.sync.dma_start(weights[:, :QUARTER], wgt[:, :QUARTER])
+        load_plane(0, 0)
         for i in range(1, PACK):
             load_plane(0, i)
         load_along_r(centres, mu)
@@ -280,8 +284,8 @@ def tile_list_radial_shell_features_kernel(tc, xT, wgt, offs, w1, mu, amp, wf_wo
         quantise_x(1, q1, QUARTER)
 
         square_distances(0, q0, QUARTER, 1, on="plane0")
-        exp_negative(0, q0, QUARTER, on="plane3")
         square_distances(0, q1, QUARTER, 2, on="plane1")
+        exp_negative(0, q0, QUARTER, on="plane3")
         exp_negative(0, q1, QUARTER, on="plane4")
 
         for a in range(PASSES):
@@ -297,37 +301,49 @@ def tile_list_radial_shell_features_kernel(tc, xT, wgt, offs, w1, mu, amp, wf_wo
         for j0 in (q0, q1):
             h_woven[(0, j0)] = early_h[:, PACK * j0 : PACK * (j0 + QUARTER)]
 
-        square_distances(1, 0, HALF, 1, on="plane2")
+        square_distances(1, 0, HALF, 1, on="plane2", exps_after=2)
         exp_negative(1, q0, QUARTER, on="plane6")
-        make_h(0, q0, QUARTER)
+        weave_h(0, q0, QUARTER)
+        quantise_h(0, q0, QUARTER)
         exp_negative(1, q1, QUARTER, on="plane7")
-        make_h(0, q1, QUARTER)
-        make_h(1, q0, QUARTER)
+        weave_h(0, q1, QUARTER)
+        quantise_h(0, q1, QUARTER)
+        weave_h(1, q0, QUARTER)
+        quantise_h(1, q0, QUARTER)
         square_distances(0, q2, QUARTER, 2, on="plane1")
         exp_negative(0, q2, QUARTER, on="w_raw00")
         features(q0, QUARTER, (0, 1))
-        make_h(1, q1, QUARTER)
+        weave_h(1, q1, QUARTER)
+        quantise_h(1, q1, QUARTER)
         square_distances(1, q2, QUARTER, 2, on="plane2")
         exp_negative(1, q2, QUARTER, on="plane3")
         features(q1, QUARTER, (0, 1))
-        store(q0, QUARTER, (VECTOR, VECTOR))
-        make_h(0, q2, QUARTER)
+        store(q0, QUARTER, 0, SCALAR)
+        weave_h(0, q2, QUARTER)
+        store(q0, QUARTER, 1, VECTOR)
+        quantise_h(0, q2, QUARTER)
         square_distances(0, q3, QUARTER, 2, on="plane0")
         exp_negative(0, q3, QUARTER, on="plane4")
-        store(q1, QUARTER, (VECTOR, VECTOR))
-        make_h(1, q2, QUARTER)
-
-        square_distances(1, q3, QUARTER, 2, on="plane1")
+        weave_h(1, q2, QUARTER)
+        store(q1, QUARTER, 0, VECTOR)
+        quantise_h(1, q2, QUARTER)
+        square_distances(1, q3, QUARTER, 2, on="plane1", exps_after=2)
         exp_negative(1, e0, EIGHTH, on="plane6")
         exp_negative(1, e1, EIGHTH, on="plane7")
+        store(q1, QUARTER, 1, SCALAR)
         for b in range(PASSES):
             features(q2, QUARTER, (b,))
-        make_h(0, q3, QUARTER)
+        weave_h(0, q3, QUARTER)
+        quantise_h(0, q3, QUARTER)
         for j0 in (e0, e1):
             features(j0, EIGHTH, (0,))
         for j0 in (e0, e1):
-            make_h(1, j0, EIGHTH)
-            features(j0, EIGHTH, (1,))
-        store(q2, QUARTER, (SCALAR, SCALAR))
+            weave_h(1, j0, EIGHTH)
         for j0 in (e0, e1):
-            store(j0, EIGHTH, (VECTOR, SCALAR))
+            quantise_h(1, j0, EIGHTH)
+            features(j0, EIGHTH, (1,))
+        for which in range(OUT_BANKS):
+            store(q2, QUARTER, which, SCALAR)
+        for j0 in (e0, e1):
+            store(j0, EIGHTH, 0, VECTOR)
+            store(j0, EIGHTH, 1, SCALAR)

@@ -63,8 +63,9 @@ def tile_list_radial_shell_features_kernel(tc, xT, wgt, offs, w1, mu, amp, wf_wo
         w_scales = grid("w_scales", [P, PASS], U8)
         h_codes = [tile(f"h_codes{b}", [P, S], U32) for b in range(PASSES)]
         h_scales = [tile(f"h_scales{b}", [P, S], U8) for b in range(PASSES)]
-        centres = tile("centres", [P, PASSES, 2 * PACK], F32)
-        amplitudes = tile("amplitudes", [P, PASSES, 2 * PACK], F32)
+        along_r = tile("along_r", [P, PASS], F32)
+        by_partition = tile("by_partition", [P, 2 * PASSES, PACK], F32)
+        centres, amplitudes = by_partition[:, :PASSES], by_partition[:, PASSES:]
         f_words = tile("f_words", [P, PASSES, 2 * N], U8)
         f_scales = tile("f_scales", [P, PASSES, N], U8)
         identity = tile("identity", [P, P], F32)
@@ -84,8 +85,8 @@ def tile_list_radial_shell_features_kernel(tc, xT, wgt, offs, w1, mu, amp, wf_wo
         def load_w(b, a):
             nc.sync.dma_start(w_raw[b][a][:], w_rows[a, :, :, PASS * b : PASS * (b + 1)])
 
-        def load_along_r(dst, vector):
-            nc.sync.dma_start(dst[:, :, :PACK], vector.rearrange("(b p t) -> p b t", b=PASSES, t=PACK))
+        def load_along_r(row, vector):
+            nc.sync.dma_start(along_r[row : row + PASSES], vector.rearrange("(b r) -> b r", b=PASSES))
 
         def copy_on(engine, dst, src):
             if engine == VECTOR:
@@ -241,12 +242,14 @@ def tile_list_radial_shell_features_kernel(tc, xT, wgt, offs, w1, mu, amp, wf_wo
         nc.vector.memset(shell_blocks[P // 2 :], 0.0)
         nc.vector.memset(f_scales[:].rearrange("p b n -> p (b n)").bitcast(I32), 0)
         nc.sync.dma_start(offsets[:], offs)
-        nc.sync.dma_start(weights[:, :QUARTER], wgt[:, :QUARTER])
         load_plane(0, 0)
         for i in range(1, PACK):
             load_plane(0, i)
-        load_along_r(centres, mu)
-        load_along_r(amplitudes, amp)
+        first_row = QUADRANT - 2 * PASSES
+        load_along_r(first_row, mu)
+        load_along_r(first_row + PASSES, amp)
+        for rows in (slice(0, first_row), slice(QUADRANT, 2 * QUADRANT), slice(2 * QUADRANT, P)):
+            nc.gpsimd.memset(along_r[rows], 0.0)
         for i in range(last):
             load_plane(1, i)
         load_w(0, 0)
@@ -261,9 +264,17 @@ def tile_list_radial_shell_features_kernel(tc, xT, wgt, offs, w1, mu, amp, wf_wo
                 wf_scales[:, 4 * q : 4 * q + 4, :].rearrange("b r n -> r b n").bitcast(I32),
             )
 
-        spread_weights((q1, q2, q3), QUARTER)
+        spread_weights((q0, q1, q2, q3), QUARTER)
         for j0 in (q0, q1, q2, q3):
             gather(0, 0, j0, QUARTER)
+        bank = next_bank()
+        for t in range(PACK):
+            nc.tensor.transpose(bank[:, P * t : P * (t + 1)], along_r[:, t::PACK], identity[:])
+        copy_on(
+            SCALAR,
+            by_partition[:],
+            bank[:].rearrange("p (t row) -> p row t", t=PACK)[:, first_row:QUADRANT],
+        )
         for i in range(1, PACK):
             gather(0, i, 0, S)
         weave_x(SCALAR, 0, 0, S)

@@ -31,6 +31,7 @@ LINE = 4
 HALF = S // 2
 QUARTER = S // 4
 EIGHTH = S // 8
+SHARE = 96
 OUT_STEP = 128
 OUT_BANKS = 2
 OUT_TILES = N // P // OUT_BANKS
@@ -41,7 +42,8 @@ def tile_list_radial_shell_features_kernel(tc, xT, wgt, offs, w1, mu, amp, wf_wo
     nc = tc.nc
     with ExitStack() as ctx:
         keep = ctx.enter_context(tc.tile_pool(name="keep", bufs=1))
-        psum = ctx.enter_context(tc.psum_pool(name="psum", bufs=BANKS))
+        psum = ctx.enter_context(tc.psum_pool(name="psum", bufs=BANKS - 1))
+        psum_kept = ctx.enter_context(tc.psum_pool(name="psum_kept", bufs=1))
 
         def tile(name, shape, dtype, on=None):
             return keep.tile(shape, dtype, name=name, tag=on or name, align_bytes=64)
@@ -66,6 +68,10 @@ def tile_list_radial_shell_features_kernel(tc, xT, wgt, offs, w1, mu, amp, wf_wo
         along_r = tile("along_r", [P, PASS], F32)
         by_partition = tile("by_partition", [P, 2 * PASSES, PACK], F32)
         centres, amplitudes = by_partition[:, :PASSES], by_partition[:, PASSES:]
+        first_row = QUADRANT - 2 * PASSES
+        turned_r = psum_kept.tile([P, BANK], F32, name="turned_r")
+        in_psum = turned_r[:].rearrange("p (t row) -> p row t", t=PACK)[:, first_row:QUADRANT]
+        shared_h = tile("shared_h", [P, (2 * QUARTER - SHARE) * PACK], BF16)
         f_words = tile("f_words", [P, PASSES, 2 * N], U8)
         f_scales = tile("f_scales", [P, PASSES, N], U8)
         identity = tile("identity", [P, P], F32)
@@ -188,15 +194,27 @@ def tile_list_radial_shell_features_kernel(tc, xT, wgt, offs, w1, mu, amp, wf_wo
             exps[(b, j0)] = gauss
             nc.scalar.activation(gauss[:], square[:, :, first : first + n], ACT.Exp, scale=-1.0)
 
-        def weave_h(b, j0, n):
+        def weave_h(b, j0, n, side=None):
+            own = slice(0, n)
+            if side is not None:
+                start = side * (n - SHARE)
+                h_woven[(b, j0)] = shared_h[:, PACK * start : PACK * (start + n)]
+                own = slice(SHARE, n) if side else slice(0, n - SHARE)
+                given = slice(0, SHARE) if side else slice(n - SHARE, n)
+                nc.gpsimd.tensor_tensor(
+                    h_woven[(b, j0)].rearrange("p (j t) -> p j t", t=PACK)[:, given],
+                    exps[(b, j0)][:, :, given].rearrange("p t j -> p j t"),
+                    amplitudes[:, b : b + 1, :].to_broadcast([P, SHARE, PACK]),
+                    MULT,
+                )
             if (b, j0) not in h_woven:
                 h_woven[(b, j0)] = tile(f"h_woven{b}_{j0}", [P, n * PACK], BF16)[:]
-            woven = h_woven[(b, j0)]
-            by_t = amplitudes[:, b, :PACK].rearrange("p (c t e) -> p c t e", c=1, e=1)
+            woven = h_woven[(b, j0)][:, PACK * own.start : PACK * own.stop]
+            by_t = in_psum[:, PASSES + b, :].rearrange("p (c t e) -> p c t e", c=1, e=1)
             nc.vector.tensor_tensor(
                 woven.rearrange("p (c e t) -> p c t e", e=LINE, t=PACK),
-                exps[(b, j0)][:].rearrange("p t (c e) -> p c t e", e=LINE),
-                by_t.to_broadcast([P, n // LINE, PACK, LINE]),
+                exps[(b, j0)][:, :, own].rearrange("p t (c e) -> p c t e", e=LINE),
+                by_t.to_broadcast([P, (own.stop - own.start) // LINE, PACK, LINE]),
                 MULT,
             )
 
@@ -223,14 +241,15 @@ def tile_list_radial_shell_features_kernel(tc, xT, wgt, offs, w1, mu, amp, wf_wo
                             stop=(b == PASSES - 1 and first_out + OUT_STEP == OUT_TILES * n),
                         )
 
-        def store(j0, n, which, engine):
-            result = tile(f"result{which}_{j0}", [P, OUT_TILES * n], F32)
-            copy_on(engine, result[:], out_banks[(which, j0)][:, : OUT_TILES * n])
+        def store(j0, n, which, engine, result=None):
+            if result is None:
+                result = tile(f"result{which}_{j0}", [P, OUT_TILES * n], F32)[:]
+            copy_on(engine, result, out_banks[(which, j0)][:, : OUT_TILES * n])
             rows = slice(P * OUT_TILES * which, P * OUT_TILES * (which + 1))
             queue = nc.scalar if engine == SCALAR else nc.sync
             queue.dma_start(
                 out[rows, j0 : j0 + n].rearrange("(m p) j -> p m j", p=P),
-                result[:].rearrange("p (m j) -> p m j", j=n),
+                result.rearrange("p (m j) -> p m j", j=n),
             )
 
         q0, q1, q2, q3 = range(0, S, QUARTER)
@@ -245,7 +264,6 @@ def tile_list_radial_shell_features_kernel(tc, xT, wgt, offs, w1, mu, amp, wf_wo
         load_plane(0, 0)
         for i in range(1, PACK):
             load_plane(0, i)
-        first_row = QUADRANT - 2 * PASSES
         load_along_r(first_row, mu)
         load_along_r(first_row + PASSES, amp)
         for rows in (slice(0, first_row), slice(QUADRANT, 2 * QUADRANT), slice(2 * QUADRANT, P)):
@@ -267,14 +285,9 @@ def tile_list_radial_shell_features_kernel(tc, xT, wgt, offs, w1, mu, amp, wf_wo
         spread_weights((q0, q1, q2, q3), QUARTER)
         for j0 in (q0, q1, q2, q3):
             gather(0, 0, j0, QUARTER)
-        bank = next_bank()
         for t in range(PACK):
-            nc.tensor.transpose(bank[:, P * t : P * (t + 1)], along_r[:, t::PACK], identity[:])
-        copy_on(
-            SCALAR,
-            by_partition[:],
-            bank[:].rearrange("p (t row) -> p row t", t=PACK)[:, first_row:QUADRANT],
-        )
+            nc.tensor.transpose(turned_r[:, P * t : P * (t + 1)], along_r[:, t::PACK], identity[:])
+        copy_on(SCALAR, by_partition[:], in_psum)
         for i in range(1, PACK):
             gather(0, i, 0, S)
         weave_x(SCALAR, 0, 0, S)
@@ -324,27 +337,27 @@ def tile_list_radial_shell_features_kernel(tc, xT, wgt, offs, w1, mu, amp, wf_wo
         square_distances(0, q2, QUARTER, 2, on="plane1")
         exp_negative(0, q2, QUARTER, on="w_raw00")
         features(q0, QUARTER, (0, 1))
-        weave_h(1, q1, QUARTER)
+        weave_h(1, q1, QUARTER, 0)
         quantise_h(1, q1, QUARTER)
         square_distances(1, q2, QUARTER, 2, on="plane2")
         exp_negative(1, q2, QUARTER, on="plane3")
         features(q1, QUARTER, (0, 1))
-        store(q0, QUARTER, 0, SCALAR)
-        weave_h(0, q2, QUARTER)
+        store(q0, QUARTER, 0, VECTOR)
+        weave_h(0, q2, QUARTER, 1)
         store(q0, QUARTER, 1, VECTOR)
         quantise_h(0, q2, QUARTER)
         square_distances(0, q3, QUARTER, 2, on="plane0")
         exp_negative(0, q3, QUARTER, on="plane4")
-        weave_h(1, q2, QUARTER)
+        weave_h(1, q2, QUARTER, 0)
         store(q1, QUARTER, 0, VECTOR)
         quantise_h(1, q2, QUARTER)
         square_distances(1, q3, QUARTER, 2, on="plane1", exps_after=2)
         exp_negative(1, e0, EIGHTH, on="plane6")
         exp_negative(1, e1, EIGHTH, on="plane7")
-        store(q1, QUARTER, 1, SCALAR)
         for b in range(PASSES):
             features(q2, QUARTER, (b,))
-        weave_h(0, q3, QUARTER)
+        weave_h(0, q3, QUARTER, 1)
+        store(q1, QUARTER, 1, VECTOR)
         quantise_h(0, q3, QUARTER)
         for j0 in (e0, e1):
             features(j0, EIGHTH, (0,))
@@ -353,8 +366,9 @@ def tile_list_radial_shell_features_kernel(tc, xT, wgt, offs, w1, mu, amp, wf_wo
         for j0 in (e0, e1):
             quantise_h(1, j0, EIGHTH)
             features(j0, EIGHTH, (1,))
+        late = tile("late_results", [P, OUT_BANKS * BANK], F32, on="plane1")
         for which in range(OUT_BANKS):
-            store(q2, QUARTER, which, SCALAR)
+            store(q2, QUARTER, which, SCALAR, late[:, BANK * which : BANK * (which + 1)])
         for j0 in (e0, e1):
             store(j0, EIGHTH, 0, VECTOR)
             store(j0, EIGHTH, 1, SCALAR)

@@ -15,6 +15,7 @@ U8 = mybir.dt.uint8
 FP8X4 = mybir.dt.float8_e4m3fn_x4
 FP4X4 = mybir.dt.float4_e2m1fn_x4
 MULT = mybir.AluOpType.mult
+SUBTRACT = mybir.AluOpType.subtract
 ACT = mybir.ActivationFunctionType
 
 P = 128
@@ -31,7 +32,6 @@ LINE = 4
 HALF = S // 2
 QUARTER = S // 4
 EIGHTH = S // 8
-SHARE = 96
 OUT_STEP = 128
 OUT_BANKS = 2
 OUT_TILES = N // P // OUT_BANKS
@@ -63,7 +63,6 @@ def tile_list_radial_shell_features_kernel(tc, xT, wgt, offs, w1, mu, amp, wf_wo
         w_woven = grid("w_woven", [P, PACK * P * PACK], BF16)
         w_codes = grid("w_codes", [P, PASS], U32)
         w_scales = grid("w_scales", [P, PASS], U8)
-        h_codes = [tile(f"h_codes{b}", [P, S], U32) for b in range(PASSES)]
         h_scales = [tile(f"h_scales{b}", [P, S], U8) for b in range(PASSES)]
         along_r = tile("along_r", [P, PASS], F32)
         by_partition = tile("by_partition", [P, 2 * PASSES, PACK], F32)
@@ -71,12 +70,12 @@ def tile_list_radial_shell_features_kernel(tc, xT, wgt, offs, w1, mu, amp, wf_wo
         first_row = QUADRANT - 2 * PASSES
         turned_r = psum_kept.tile([P, BANK], F32, name="turned_r")
         in_psum = turned_r[:].rearrange("p (t row) -> p row t", t=PACK)[:, first_row:QUADRANT]
-        shared_h = tile("shared_h", [P, (2 * QUARTER - SHARE) * PACK], BF16)
+        shared_h = tile("shared_h", [P, 3 * QUARTER * PACK], BF16)
         f_words = tile("f_words", [P, PASSES, 2 * N], U8)
         f_scales = tile("f_scales", [P, PASSES, N], U8)
         identity = tile("identity", [P, P], F32)
         shell_blocks = tile("shell_blocks", [P, P], F32)
-        x_woven, x_codes, squares, exps, h_woven, out_banks = {}, {}, {}, {}, {}, {}
+        x_woven, x_codes, squares, exps, h_woven, h_codes, out_banks = {}, {}, {}, {}, {}, {}, {}
 
         x_rows = xT.rearrange("(a p i) t -> a i p t", a=PASSES, i=PACK)
         w_rows = w1.rearrange("(a p i) r -> a p i r", a=PASSES, i=PACK)
@@ -157,7 +156,7 @@ def tile_list_radial_shell_features_kernel(tc, xT, wgt, offs, w1, mu, amp, wf_wo
                 w_codes[b][a][:, cols].bitcast(FP8X4), w_scales[b][a][:, cols], woven_w(b, a, t0, count)
             )
 
-        def square_distances(b, j0, n, per_bank, on, exps_after=1):
+        def square_distances(b, j0, n, per_bank, on, exps_after=1, engine=SCALAR):
             square = tile(f"square{b}_{j0}", [P, PACK, n], F32, on)
             squares[(b, j0)] = square
             for t0 in range(0, PACK, per_bank):
@@ -177,6 +176,16 @@ def tile_list_radial_shell_features_kernel(tc, xT, wgt, offs, w1, mu, amp, wf_wo
                                 start=(a == 0 and first_out == 0),
                                 stop=(a == PASSES - 1 and first_out + c1 - c0 == per_bank * n),
                             )
+                if engine == VECTOR:
+                    sums = bank[:, : per_bank * n].rearrange("p (t j) -> p t j", j=n)
+                    distance = tile(f"distance{b}_{j0}_{t0}", [P, per_bank, n], F32)
+                    mus = centres[:, b, t0 : t0 + per_bank].rearrange("p (t j) -> p t j", j=1)
+                    nc.vector.tensor_tensor(distance[:], sums, mus.to_broadcast([P, per_bank, n]), SUBTRACT)
+                    for t in range(per_bank):
+                        nc.vector.scalar_tensor_tensor(
+                            square[:, t0 + t, :], sums[:, t], mus[:, t], distance[:, t], SUBTRACT, MULT
+                        )
+                    continue
                 for t in range(t0, t0 + per_bank):
                     step = n // exps_after if t == PACK - 1 else n
                     for c0 in range(0, n, step):
@@ -194,34 +203,30 @@ def tile_list_radial_shell_features_kernel(tc, xT, wgt, offs, w1, mu, amp, wf_wo
             exps[(b, j0)] = gauss
             nc.scalar.activation(gauss[:], square[:, :, first : first + n], ACT.Exp, scale=-1.0)
 
-        def weave_h(b, j0, n, side=None):
-            own = slice(0, n)
-            if side is not None:
-                start = side * (n - SHARE)
-                h_woven[(b, j0)] = shared_h[:, PACK * start : PACK * (start + n)]
-                own = slice(SHARE, n) if side else slice(0, n - SHARE)
-                given = slice(0, SHARE) if side else slice(n - SHARE, n)
+        def weave_h(b, j0, n, woven=None, given=slice(0, 0)):
+            if woven is None:
+                woven = tile(f"h_woven{b}_{j0}", [P, n * PACK], BF16)[:]
+            h_woven[(b, j0)] = woven
+            own = slice(given.stop, n) if given.start == 0 else slice(0, given.start)
+            if given.stop > given.start:
                 nc.gpsimd.tensor_tensor(
-                    h_woven[(b, j0)].rearrange("p (j t) -> p j t", t=PACK)[:, given],
+                    woven.rearrange("p (j t) -> p j t", t=PACK)[:, given],
                     exps[(b, j0)][:, :, given].rearrange("p t j -> p j t"),
-                    amplitudes[:, b : b + 1, :].to_broadcast([P, SHARE, PACK]),
+                    amplitudes[:, b : b + 1, :].to_broadcast([P, given.stop - given.start, PACK]),
                     MULT,
                 )
-            if (b, j0) not in h_woven:
-                h_woven[(b, j0)] = tile(f"h_woven{b}_{j0}", [P, n * PACK], BF16)[:]
-            woven = h_woven[(b, j0)][:, PACK * own.start : PACK * own.stop]
             by_t = in_psum[:, PASSES + b, :].rearrange("p (c t e) -> p c t e", c=1, e=1)
             nc.vector.tensor_tensor(
-                woven.rearrange("p (c e t) -> p c t e", e=LINE, t=PACK),
+                woven[:, PACK * own.start : PACK * own.stop].rearrange("p (c e t) -> p c t e", e=LINE, t=PACK),
                 exps[(b, j0)][:, :, own].rearrange("p t (c e) -> p c t e", e=LINE),
                 by_t.to_broadcast([P, (own.stop - own.start) // LINE, PACK, LINE]),
                 MULT,
             )
 
-        def quantise_h(b, j0, n):
-            nc.vector.quantize_mx(
-                h_codes[b][:, j0 : j0 + n].bitcast(FP8X4), h_scales[b][:, j0 : j0 + n], h_woven[(b, j0)]
-            )
+        def quantise_h(b, j0, n, on=None):
+            codes = tile(f"h_codes{b}_{j0}", [P, n], U32, on)
+            h_codes[(b, j0)] = codes
+            nc.vector.quantize_mx(codes[:].bitcast(FP8X4), h_scales[b][:, j0 : j0 + n], h_woven[(b, j0)])
 
         def features(j0, n, halves):
             for which in range(OUT_BANKS):
@@ -231,11 +236,12 @@ def tile_list_radial_shell_features_kernel(tc, xT, wgt, offs, w1, mu, amp, wf_wo
                     for first_out in range(0, OUT_TILES * n, OUT_STEP):
                         m = OUT_TILES * which + first_out // n
                         moving = slice(j0 + first_out % n, j0 + first_out % n + OUT_STEP)
+                        codes, first = holder(h_codes, b, moving.start)
                         nc.tensor.matmul_mx(
                             out_banks[(which, j0)][:, first_out : first_out + OUT_STEP],
                             lhsT=f_words[:, b, 2 * P * m : 2 * P * (m + 1)].bitcast(FP4X4),
                             lhsT_scale=f_scales[:, b, P * m : P * (m + 1)],
-                            rhs=h_codes[b][:, moving].bitcast(FP8X4),
+                            rhs=codes[:, first : first + OUT_STEP].bitcast(FP8X4),
                             rhs_scale=h_scales[b][:, moving],
                             start=(b == 0 and first_out == 0),
                             stop=(b == PASSES - 1 and first_out + OUT_STEP == OUT_TILES * n),
@@ -321,48 +327,58 @@ def tile_list_radial_shell_features_kernel(tc, xT, wgt, offs, w1, mu, amp, wf_wo
             weave_x(VECTOR, 1, j0, QUARTER)
         for j0 in (q2, q3):
             quantise_x(1, j0, QUARTER)
-        early_h = tile("early_h", [P, HALF * PACK], BF16, on="w_woven11")
-        for j0 in (q0, q1):
-            h_woven[(0, j0)] = early_h[:, PACK * j0 : PACK * (j0 + QUARTER)]
+        first_h = tile("first_h", [P, QUARTER * PACK], BF16, on="w_woven11")
+        second_h = tile("second_h", [P, QUARTER * PACK], BF16, on="x_woven1_768")
+        places = [(QUARTER, 2 * QUARTER)]
+
+        def weave_shared(b, j0, n, share):
+            low, high = places[-1]
+            below = len(places) % 2 == 1
+            start = low + share - n if below else high - share
+            places.append((start, start + n))
+            given = slice(n - share, n) if below else slice(0, share)
+            weave_h(b, j0, n, shared_h[:, PACK * start : PACK * (start + n)], given)
+
 
         square_distances(1, 0, HALF, 1, on="plane2", exps_after=2)
         exp_negative(1, q0, QUARTER, on="plane6")
-        weave_h(0, q0, QUARTER)
+        weave_h(0, q0, QUARTER, first_h[:])
         quantise_h(0, q0, QUARTER)
         exp_negative(1, q1, QUARTER, on="plane7")
-        weave_h(0, q1, QUARTER)
+        weave_h(0, q1, QUARTER, second_h[:], slice(0, EIGHTH))
+        weave_h(1, q0, QUARTER, shared_h[:, PACK * QUARTER : 2 * PACK * QUARTER])
         quantise_h(0, q1, QUARTER)
-        weave_h(1, q0, QUARTER)
         quantise_h(1, q0, QUARTER)
         square_distances(0, q2, QUARTER, 2, on="plane1")
         exp_negative(0, q2, QUARTER, on="w_raw00")
         features(q0, QUARTER, (0, 1))
-        weave_h(1, q1, QUARTER, 0)
+        weave_shared(1, q1, QUARTER, 96)
+        store(q0, QUARTER, 0, VECTOR)
         quantise_h(1, q1, QUARTER)
         square_distances(1, q2, QUARTER, 2, on="plane2")
         exp_negative(1, q2, QUARTER, on="plane3")
         features(q1, QUARTER, (0, 1))
-        store(q0, QUARTER, 0, VECTOR)
-        weave_h(0, q2, QUARTER, 1)
+        weave_shared(0, q2, QUARTER, 96)
         store(q0, QUARTER, 1, VECTOR)
         quantise_h(0, q2, QUARTER)
         square_distances(0, q3, QUARTER, 2, on="plane0")
         exp_negative(0, q3, QUARTER, on="plane4")
-        weave_h(1, q2, QUARTER, 0)
-        store(q1, QUARTER, 0, VECTOR)
+        weave_shared(1, q2, QUARTER, 128)
+        held = tile("held_results", [P, OUT_BANKS * BANK], F32, on="plane2")
+        for which in range(OUT_BANKS):
+            store(q1, QUARTER, which, VECTOR, held[:, BANK * which : BANK * (which + 1)])
         quantise_h(1, q2, QUARTER)
         square_distances(1, q3, QUARTER, 2, on="plane1", exps_after=2)
         exp_negative(1, e0, EIGHTH, on="plane6")
         exp_negative(1, e1, EIGHTH, on="plane7")
         for b in range(PASSES):
             features(q2, QUARTER, (b,))
-        weave_h(0, q3, QUARTER, 1)
-        store(q1, QUARTER, 1, VECTOR)
+        weave_shared(0, q3, QUARTER, 64)
         quantise_h(0, q3, QUARTER)
         for j0 in (e0, e1):
             features(j0, EIGHTH, (0,))
-        for j0 in (e0, e1):
-            weave_h(1, j0, EIGHTH)
+        weave_h(1, e0, EIGHTH)
+        weave_shared(1, e1, EIGHTH, 48)
         for j0 in (e0, e1):
             quantise_h(1, j0, EIGHTH)
             features(j0, EIGHTH, (1,))

@@ -15,7 +15,6 @@ U8 = mybir.dt.uint8
 FP8X4 = mybir.dt.float8_e4m3fn_x4
 FP4X4 = mybir.dt.float4_e2m1fn_x4
 MULT = mybir.AluOpType.mult
-SUBTRACT = mybir.AluOpType.subtract
 ACT = mybir.ActivationFunctionType
 
 P = 128
@@ -27,6 +26,7 @@ PASSES = K // PASS
 BANK = 512
 BANKS = 8
 SHELLS = 8
+BLOCKS = S // P
 LIST_ROWS = 16
 LINE = 4
 HALF = S // 2
@@ -35,6 +35,10 @@ EIGHTH = S // 8
 OUT_STEP = 128
 OUT_BANKS = 2
 OUT_TILES = N // P // OUT_BANKS
+SHARE_SHORT = 48
+SHARE_ALONE = 64
+SHARE_ONE_COPY = 96
+SHARE_TWO_CALLS = 128
 VECTOR, SCALAR = "vector", "scalar"
 
 
@@ -65,17 +69,19 @@ def tile_list_radial_shell_features_kernel(tc, xT, wgt, offs, w1, mu, amp, wf_wo
         w_scales = grid("w_scales", [P, PASS], U8)
         h_scales = [tile(f"h_scales{b}", [P, S], U8) for b in range(PASSES)]
         along_r = tile("along_r", [P, PASS], F32)
-        by_partition = tile("by_partition", [P, 2 * PASSES, PACK], F32)
-        centres, amplitudes = by_partition[:, :PASSES], by_partition[:, PASSES:]
         first_row = QUADRANT - 2 * PASSES
         turned_r = psum_kept.tile([P, BANK], F32, name="turned_r")
-        in_psum = turned_r[:].rearrange("p (t row) -> p row t", t=PACK)[:, first_row:QUADRANT]
+        rows_in_psum = turned_r[:].rearrange("p (t row) -> p row t", t=PACK)[:, first_row:QUADRANT]
+        rows_in_sbuf = tile("rows_in_sbuf", [P, 2 * PASSES, PACK], F32)
+        centres, amplitudes = rows_in_sbuf[:, :PASSES], rows_in_sbuf[:, PASSES:]
+        amplitudes_in_psum = rows_in_psum[:, PASSES:]
         shared_h = tile("shared_h", [P, 3 * QUARTER * PACK], BF16)
         f_words = tile("f_words", [P, PASSES, 2 * N], U8)
         f_scales = tile("f_scales", [P, PASSES, N], U8)
         identity = tile("identity", [P, P], F32)
         shell_blocks = tile("shell_blocks", [P, P], F32)
         x_woven, x_codes, squares, exps, h_woven, h_codes, out_banks = {}, {}, {}, {}, {}, {}, {}
+        places = []
 
         x_rows = xT.rearrange("(a p i) t -> a i p t", a=PASSES, i=PACK)
         w_rows = w1.rearrange("(a p i) r -> a p i r", a=PASSES, i=PACK)
@@ -107,7 +113,7 @@ def tile_list_radial_shell_features_kernel(tc, xT, wgt, offs, w1, mu, amp, wf_wo
 
         def spread_weights(firsts, n):
             blocks = n // P
-            by_entry = turn(shell_blocks[:], P)[:, : SHELLS * S // P].rearrange("j (g c e) -> j c g e", g=SHELLS, e=1)
+            by_entry = turn(shell_blocks[:], P)[:, : SHELLS * BLOCKS].rearrange("j (g c e) -> j c g e", g=SHELLS, e=1)
             spread = [tile(f"spread{j0}", [P, n], F32) for j0 in firsts]
             for j0, dst in zip(firsts, spread):
                 nc.scalar.copy(
@@ -156,7 +162,7 @@ def tile_list_radial_shell_features_kernel(tc, xT, wgt, offs, w1, mu, amp, wf_wo
                 w_codes[b][a][:, cols].bitcast(FP8X4), w_scales[b][a][:, cols], woven_w(b, a, t0, count)
             )
 
-        def square_distances(b, j0, n, per_bank, on, exps_after=1, engine=SCALAR):
+        def square_distances(b, j0, n, per_bank, on, exps_after=1):
             square = tile(f"square{b}_{j0}", [P, PACK, n], F32, on)
             squares[(b, j0)] = square
             for t0 in range(0, PACK, per_bank):
@@ -176,16 +182,6 @@ def tile_list_radial_shell_features_kernel(tc, xT, wgt, offs, w1, mu, amp, wf_wo
                                 start=(a == 0 and first_out == 0),
                                 stop=(a == PASSES - 1 and first_out + c1 - c0 == per_bank * n),
                             )
-                if engine == VECTOR:
-                    sums = bank[:, : per_bank * n].rearrange("p (t j) -> p t j", j=n)
-                    distance = tile(f"distance{b}_{j0}_{t0}", [P, per_bank, n], F32)
-                    mus = centres[:, b, t0 : t0 + per_bank].rearrange("p (t j) -> p t j", j=1)
-                    nc.vector.tensor_tensor(distance[:], sums, mus.to_broadcast([P, per_bank, n]), SUBTRACT)
-                    for t in range(per_bank):
-                        nc.vector.scalar_tensor_tensor(
-                            square[:, t0 + t, :], sums[:, t], mus[:, t], distance[:, t], SUBTRACT, MULT
-                        )
-                    continue
                 for t in range(t0, t0 + per_bank):
                     step = n // exps_after if t == PACK - 1 else n
                     for c0 in range(0, n, step):
@@ -203,28 +199,46 @@ def tile_list_radial_shell_features_kernel(tc, xT, wgt, offs, w1, mu, amp, wf_wo
             exps[(b, j0)] = gauss
             nc.scalar.activation(gauss[:], square[:, :, first : first + n], ACT.Exp, scale=-1.0)
 
-        def weave_h(b, j0, n, woven=None, given=slice(0, 0)):
-            if woven is None:
-                woven = tile(f"h_woven{b}_{j0}", [P, n * PACK], BF16)[:]
-            h_woven[(b, j0)] = woven
-            own = slice(given.stop, n) if given.start == 0 else slice(0, given.start)
-            if given.stop > given.start:
-                nc.gpsimd.tensor_tensor(
-                    woven.rearrange("p (j t) -> p j t", t=PACK)[:, given],
-                    exps[(b, j0)][:, :, given].rearrange("p t j -> p j t"),
-                    amplitudes[:, b : b + 1, :].to_broadcast([P, given.stop - given.start, PACK]),
-                    MULT,
-                )
-            by_t = in_psum[:, PASSES + b, :].rearrange("p (c t e) -> p c t e", c=1, e=1)
+        def amplify(b, j0, entries):
+            by_t = amplitudes_in_psum[:, b, :].rearrange("p (c t e) -> p c t e", c=1, e=1)
+            woven = h_woven[(b, j0)][:, PACK * entries.start : PACK * entries.stop]
             nc.vector.tensor_tensor(
-                woven[:, PACK * own.start : PACK * own.stop].rearrange("p (c e t) -> p c t e", e=LINE, t=PACK),
-                exps[(b, j0)][:, :, own].rearrange("p t (c e) -> p c t e", e=LINE),
-                by_t.to_broadcast([P, (own.stop - own.start) // LINE, PACK, LINE]),
+                woven.rearrange("p (c e t) -> p c t e", e=LINE, t=PACK),
+                exps[(b, j0)][:, :, entries].rearrange("p t (c e) -> p c t e", e=LINE),
+                by_t.to_broadcast([P, (entries.stop - entries.start) // LINE, PACK, LINE]),
                 MULT,
             )
 
-        def quantise_h(b, j0, n, on=None):
-            codes = tile(f"h_codes{b}_{j0}", [P, n], U32, on)
+        def amplify_on_gpsimd(b, j0, entries):
+            nc.gpsimd.tensor_tensor(
+                h_woven[(b, j0)].rearrange("p (j t) -> p j t", t=PACK)[:, entries],
+                exps[(b, j0)][:, :, entries].rearrange("p t j -> p j t"),
+                amplitudes[:, b : b + 1, :].to_broadcast([P, entries.stop - entries.start, PACK]),
+                MULT,
+            )
+
+        def amplify_on_tile(b, j0, n, share, on):
+            h_woven[(b, j0)] = tile(f"h_woven{b}_{j0}", [P, n * PACK], BF16, on)[:]
+            amplify_on_gpsimd(b, j0, slice(0, share))
+            amplify(b, j0, slice(share, n))
+
+        def place_h(b, j0, start, n):
+            h_woven[(b, j0)] = shared_h[:, PACK * start : PACK * (start + n)]
+            places.append((start, start + n))
+
+        def amplify_behind(b, j0, n, share):
+            low, high = places[-1]
+            if len(places) % 2:
+                place_h(b, j0, low + share - n, n)
+                given, own = slice(n - share, n), slice(0, n - share)
+            else:
+                place_h(b, j0, high - share, n)
+                given, own = slice(0, share), slice(share, n)
+            amplify_on_gpsimd(b, j0, given)
+            amplify(b, j0, own)
+
+        def quantise_h(b, j0, n):
+            codes = tile(f"h_codes{b}_{j0}", [P, n], U32)
             h_codes[(b, j0)] = codes
             nc.vector.quantize_mx(codes[:].bitcast(FP8X4), h_scales[b][:, j0 : j0 + n], h_woven[(b, j0)])
 
@@ -247,9 +261,7 @@ def tile_list_radial_shell_features_kernel(tc, xT, wgt, offs, w1, mu, amp, wf_wo
                             stop=(b == PASSES - 1 and first_out + OUT_STEP == OUT_TILES * n),
                         )
 
-        def store(j0, n, which, engine, result=None):
-            if result is None:
-                result = tile(f"result{which}_{j0}", [P, OUT_TILES * n], F32)[:]
+        def store(j0, n, which, engine, result):
             copy_on(engine, result, out_banks[(which, j0)][:, : OUT_TILES * n])
             rows = slice(P * OUT_TILES * which, P * OUT_TILES * (which + 1))
             queue = nc.scalar if engine == SCALAR else nc.sync
@@ -258,17 +270,25 @@ def tile_list_radial_shell_features_kernel(tc, xT, wgt, offs, w1, mu, amp, wf_wo
                 result.rearrange("p (m j) -> p m j", j=n),
             )
 
+        def store_bank(j0, n, which, engine):
+            store(j0, n, which, engine, tile(f"result{which}_{j0}", [P, OUT_TILES * n], F32)[:])
+
+        def store_held(j0, n, engine, on):
+            width = OUT_TILES * n
+            results = tile(f"results{j0}", [P, OUT_BANKS * width], F32, on)
+            for which in range(OUT_BANKS):
+                store(j0, n, which, engine, results[:, width * which : width * (which + 1)])
+
         q0, q1, q2, q3 = range(0, S, QUARTER)
         e0, e1 = q3, q3 + EIGHTH
         last = PACK - 1
 
-        nc.sync.dma_start(shell_blocks[: P // 2], wgt[0:P:LIST_ROWS, :].rearrange("g (c u) -> g c u", u=P))
+        nc.sync.dma_start(shell_blocks[: SHELLS * BLOCKS], wgt[0:P:LIST_ROWS, :].rearrange("g (c u) -> g c u", u=P))
         make_identity(nc, identity[:])
-        nc.vector.memset(shell_blocks[P // 2 :], 0.0)
+        nc.vector.memset(shell_blocks[SHELLS * BLOCKS :], 0.0)
         nc.vector.memset(f_scales[:].rearrange("p b n -> p (b n)").bitcast(I32), 0)
         nc.sync.dma_start(offsets[:], offs)
-        load_plane(0, 0)
-        for i in range(1, PACK):
+        for i in range(PACK):
             load_plane(0, i)
         load_along_r(first_row, mu)
         load_along_r(first_row + PASSES, amp)
@@ -293,7 +313,7 @@ def tile_list_radial_shell_features_kernel(tc, xT, wgt, offs, w1, mu, amp, wf_wo
             gather(0, 0, j0, QUARTER)
         for t in range(PACK):
             nc.tensor.transpose(turned_r[:, P * t : P * (t + 1)], along_r[:, t::PACK], identity[:])
-        copy_on(SCALAR, by_partition[:], in_psum)
+        copy_on(SCALAR, rows_in_sbuf[:], rows_in_psum)
         for i in range(1, PACK):
             gather(0, i, 0, S)
         weave_x(SCALAR, 0, 0, S)
@@ -327,64 +347,52 @@ def tile_list_radial_shell_features_kernel(tc, xT, wgt, offs, w1, mu, amp, wf_wo
             weave_x(VECTOR, 1, j0, QUARTER)
         for j0 in (q2, q3):
             quantise_x(1, j0, QUARTER)
-        first_h = tile("first_h", [P, QUARTER * PACK], BF16, on="w_woven11")
-        second_h = tile("second_h", [P, QUARTER * PACK], BF16, on="x_woven1_768")
-        places = [(QUARTER, 2 * QUARTER)]
-
-        def weave_shared(b, j0, n, share):
-            low, high = places[-1]
-            below = len(places) % 2 == 1
-            start = low + share - n if below else high - share
-            places.append((start, start + n))
-            given = slice(n - share, n) if below else slice(0, share)
-            weave_h(b, j0, n, shared_h[:, PACK * start : PACK * (start + n)], given)
-
 
         square_distances(1, 0, HALF, 1, on="plane2", exps_after=2)
         exp_negative(1, q0, QUARTER, on="plane6")
-        weave_h(0, q0, QUARTER, first_h[:])
+        amplify_on_tile(0, q0, QUARTER, SHARE_SHORT, on="w_woven11")
         quantise_h(0, q0, QUARTER)
         exp_negative(1, q1, QUARTER, on="plane7")
-        weave_h(0, q1, QUARTER, second_h[:], slice(0, EIGHTH))
-        weave_h(1, q0, QUARTER, shared_h[:, PACK * QUARTER : 2 * PACK * QUARTER])
+        amplify_on_tile(0, q1, QUARTER, SHARE_TWO_CALLS, on=f"x_woven1_{q3}")
+        place_h(1, q0, QUARTER, QUARTER)
+        amplify(1, q0, slice(0, QUARTER))
         quantise_h(0, q1, QUARTER)
         quantise_h(1, q0, QUARTER)
+
         square_distances(0, q2, QUARTER, 2, on="plane1")
         exp_negative(0, q2, QUARTER, on="w_raw00")
         features(q0, QUARTER, (0, 1))
-        weave_shared(1, q1, QUARTER, 96)
-        store(q0, QUARTER, 0, VECTOR)
+        amplify_behind(1, q1, QUARTER, SHARE_ONE_COPY)
+        store_bank(q0, QUARTER, 0, VECTOR)
         quantise_h(1, q1, QUARTER)
         square_distances(1, q2, QUARTER, 2, on="plane2")
         exp_negative(1, q2, QUARTER, on="plane3")
         features(q1, QUARTER, (0, 1))
-        weave_shared(0, q2, QUARTER, 96)
-        store(q0, QUARTER, 1, VECTOR)
+        amplify_behind(0, q2, QUARTER, SHARE_ONE_COPY)
+        store_bank(q0, QUARTER, 1, VECTOR)
         quantise_h(0, q2, QUARTER)
         square_distances(0, q3, QUARTER, 2, on="plane0")
         exp_negative(0, q3, QUARTER, on="plane4")
-        weave_shared(1, q2, QUARTER, 128)
-        held = tile("held_results", [P, OUT_BANKS * BANK], F32, on="plane2")
-        for which in range(OUT_BANKS):
-            store(q1, QUARTER, which, VECTOR, held[:, BANK * which : BANK * (which + 1)])
+        amplify_behind(1, q2, QUARTER, SHARE_TWO_CALLS)
+        store_held(q1, QUARTER, VECTOR, on="plane2")
         quantise_h(1, q2, QUARTER)
+
         square_distances(1, q3, QUARTER, 2, on="plane1", exps_after=2)
         exp_negative(1, e0, EIGHTH, on="plane6")
         exp_negative(1, e1, EIGHTH, on="plane7")
         for b in range(PASSES):
             features(q2, QUARTER, (b,))
-        weave_shared(0, q3, QUARTER, 64)
+        amplify_behind(0, q3, QUARTER, SHARE_ALONE)
         quantise_h(0, q3, QUARTER)
         for j0 in (e0, e1):
             features(j0, EIGHTH, (0,))
-        weave_h(1, e0, EIGHTH)
-        weave_shared(1, e1, EIGHTH, 48)
+        h_woven[(1, e0)] = tile("h_woven_e0", [P, EIGHTH * PACK], BF16)[:]
+        amplify(1, e0, slice(0, EIGHTH))
+        amplify_behind(1, e1, EIGHTH, SHARE_SHORT)
         for j0 in (e0, e1):
             quantise_h(1, j0, EIGHTH)
             features(j0, EIGHTH, (1,))
-        late = tile("late_results", [P, OUT_BANKS * BANK], F32, on="plane1")
-        for which in range(OUT_BANKS):
-            store(q2, QUARTER, which, SCALAR, late[:, BANK * which : BANK * (which + 1)])
+        store_held(q2, QUARTER, SCALAR, on="plane1")
         for j0 in (e0, e1):
-            store(j0, EIGHTH, 0, VECTOR)
-            store(j0, EIGHTH, 1, SCALAR)
+            store_bank(j0, EIGHTH, 0, VECTOR)
+            store_bank(j0, EIGHTH, 1, SCALAR)

@@ -199,28 +199,26 @@ def tile_list_radial_shell_features_kernel(tc, xT, wgt, offs, w1, mu, amp, wf_wo
             exps[(b, j0)] = gauss
             nc.scalar.activation(gauss[:], square[:, :, first : first + n], ACT.Exp, scale=-1.0)
 
-        def amplify(b, j0, entries):
-            by_t = amplitudes_in_psum[:, b, :].rearrange("p (c t e) -> p c t e", c=1, e=1)
+        def amplify(engine, amps, b, j0, entries):
+            by_t = amps[:, b, :].rearrange("p (c t e) -> p c t e", c=1, e=1)
             woven = h_woven[(b, j0)][:, PACK * entries.start : PACK * entries.stop]
-            nc.vector.tensor_tensor(
+            engine.tensor_tensor(
                 woven.rearrange("p (c e t) -> p c t e", e=LINE, t=PACK),
                 exps[(b, j0)][:, :, entries].rearrange("p t (c e) -> p c t e", e=LINE),
                 by_t.to_broadcast([P, (entries.stop - entries.start) // LINE, PACK, LINE]),
                 MULT,
             )
 
+        def amplify_on_vector(b, j0, entries):
+            amplify(nc.vector, amplitudes_in_psum, b, j0, entries)
+
         def amplify_on_gpsimd(b, j0, entries):
-            nc.gpsimd.tensor_tensor(
-                h_woven[(b, j0)].rearrange("p (j t) -> p j t", t=PACK)[:, entries],
-                exps[(b, j0)][:, :, entries].rearrange("p t j -> p j t"),
-                amplitudes[:, b : b + 1, :].to_broadcast([P, entries.stop - entries.start, PACK]),
-                MULT,
-            )
+            amplify(nc.gpsimd, amplitudes, b, j0, entries)
 
         def amplify_on_tile(b, j0, n, share, on):
             h_woven[(b, j0)] = tile(f"h_woven{b}_{j0}", [P, n * PACK], BF16, on)[:]
             amplify_on_gpsimd(b, j0, slice(0, share))
-            amplify(b, j0, slice(share, n))
+            amplify_on_vector(b, j0, slice(share, n))
 
         def place_h(b, j0, start, n):
             h_woven[(b, j0)] = shared_h[:, PACK * start : PACK * (start + n)]
@@ -235,7 +233,7 @@ def tile_list_radial_shell_features_kernel(tc, xT, wgt, offs, w1, mu, amp, wf_wo
                 place_h(b, j0, high - share, n)
                 given, own = slice(0, share), slice(share, n)
             amplify_on_gpsimd(b, j0, given)
-            amplify(b, j0, own)
+            amplify_on_vector(b, j0, own)
 
         def quantise_h(b, j0, n):
             codes = tile(f"h_codes{b}_{j0}", [P, n], U32)
@@ -350,12 +348,13 @@ def tile_list_radial_shell_features_kernel(tc, xT, wgt, offs, w1, mu, amp, wf_wo
 
         square_distances(1, 0, HALF, 1, on="plane2", exps_after=2)
         exp_negative(1, q0, QUARTER, on="plane6")
-        amplify_on_tile(0, q0, QUARTER, SHARE_SHORT, on="w_woven11")
+        h_woven[(0, q0)] = tile("h_woven_q0", [P, QUARTER * PACK], BF16, on="w_woven11")[:]
+        amplify_on_vector(0, q0, slice(0, QUARTER))
         quantise_h(0, q0, QUARTER)
         exp_negative(1, q1, QUARTER, on="plane7")
         amplify_on_tile(0, q1, QUARTER, SHARE_TWO_CALLS, on=f"x_woven1_{q3}")
         place_h(1, q0, QUARTER, QUARTER)
-        amplify(1, q0, slice(0, QUARTER))
+        amplify_on_vector(1, q0, slice(0, QUARTER))
         quantise_h(0, q1, QUARTER)
         quantise_h(1, q0, QUARTER)
 
@@ -387,7 +386,7 @@ def tile_list_radial_shell_features_kernel(tc, xT, wgt, offs, w1, mu, amp, wf_wo
         for j0 in (e0, e1):
             features(j0, EIGHTH, (0,))
         h_woven[(1, e0)] = tile("h_woven_e0", [P, EIGHTH * PACK], BF16)[:]
-        amplify(1, e0, slice(0, EIGHTH))
+        amplify_on_vector(1, e0, slice(0, EIGHTH))
         amplify_behind(1, e1, EIGHTH, SHARE_SHORT)
         for j0 in (e0, e1):
             quantise_h(1, j0, EIGHTH)

@@ -32,7 +32,6 @@ LINE = 4
 HALF = S // 2
 QUARTER = S // 4
 EIGHTH = S // 8
-OUT_STEP = 128
 OUT_BANKS = 2
 OUT_TILES = N // P // OUT_BANKS
 SHARE_SHORT = 48
@@ -245,18 +244,17 @@ def tile_list_radial_shell_features_kernel(tc, xT, wgt, offs, w1, mu, amp, wf_wo
                 if (which, j0) not in out_banks:
                     out_banks[(which, j0)] = next_bank()
                 for b in halves:
-                    for first_out in range(0, OUT_TILES * n, OUT_STEP):
+                    codes, first = holder(h_codes, b, j0)
+                    for first_out in range(0, OUT_TILES * n, n):
                         m = OUT_TILES * which + first_out // n
-                        moving = slice(j0 + first_out % n, j0 + first_out % n + OUT_STEP)
-                        codes, first = holder(h_codes, b, moving.start)
                         nc.tensor.matmul_mx(
-                            out_banks[(which, j0)][:, first_out : first_out + OUT_STEP],
+                            out_banks[(which, j0)][:, first_out : first_out + n],
                             lhsT=f_words[:, b, 2 * P * m : 2 * P * (m + 1)].bitcast(FP4X4),
                             lhsT_scale=f_scales[:, b, P * m : P * (m + 1)],
-                            rhs=codes[:, first : first + OUT_STEP].bitcast(FP8X4),
-                            rhs_scale=h_scales[b][:, moving],
+                            rhs=codes[:, first : first + n].bitcast(FP8X4),
+                            rhs_scale=h_scales[b][:, j0 : j0 + n],
                             start=(b == 0 and first_out == 0),
-                            stop=(b == PASSES - 1 and first_out + OUT_STEP == OUT_TILES * n),
+                            stop=(b == PASSES - 1 and first_out + n == OUT_TILES * n),
                         )
 
         def store(j0, n, which, engine, result):

@@ -128,19 +128,20 @@ def tile_list_radial_shell_features_kernel(tc, xT, wgt, offs, w1, mu, amp, wf_wo
                 picked[a][:, i, j0 : j0 + n], planes[a][i][:].indirect(listed), weights[:, j0 : j0 + n], MULT
             )
 
-        def weave_x(engine, a, j0, n):
-            woven = tile(f"x_woven{a}_{j0}", [P, n * PACK], BF16)
+        def weave_x(engine, a, j0, n, woven=None, values=slice(0, PACK)):
+            if woven is None:
+                woven = tile(f"x_woven{a}_{j0}", [P, n * PACK], BF16)[:]
             x_woven[(a, j0)] = woven
             copy_on(
                 engine,
-                woven[:].rearrange("p (c e i) -> p c i e", e=LINE, i=PACK),
-                picked[a][:, :, j0 : j0 + n].rearrange("p i (c e) -> p c i e", e=LINE),
+                woven.rearrange("p (c e i) -> p c i e", e=LINE, i=PACK)[:, :, values],
+                picked[a][:, values, j0 : j0 + n].rearrange("p i (c e) -> p c i e", e=LINE),
             )
 
         def quantise_x(a, j0, n, on=None):
             codes = tile(f"x_codes{a}_{j0}", [P, n], U32, on)
             x_codes[(a, j0)] = codes
-            nc.vector.quantize_mx(codes[:].bitcast(FP8X4), x_scales[a][:, j0 : j0 + n], x_woven[(a, j0)][:])
+            nc.vector.quantize_mx(codes[:].bitcast(FP8X4), x_scales[a][:, j0 : j0 + n], x_woven[(a, j0)])
 
         def woven_w(b, a, t0, count):
             if (b, a, t0) == (PASSES - 1, PASSES - 1, PACK - 2):
@@ -213,11 +214,6 @@ def tile_list_radial_shell_features_kernel(tc, xT, wgt, offs, w1, mu, amp, wf_wo
 
         def amplify_on_gpsimd(b, j0, entries):
             amplify(nc.gpsimd, amplitudes, b, j0, entries)
-
-        def amplify_on_tile(b, j0, n, share, on):
-            h_woven[(b, j0)] = tile(f"h_woven{b}_{j0}", [P, n * PACK], BF16, on)[:]
-            amplify_on_gpsimd(b, j0, slice(0, share))
-            amplify_on_vector(b, j0, slice(share, n))
 
         def place_h(b, j0, start, n):
             h_woven[(b, j0)] = shared_h[:, PACK * start : PACK * (start + n)]
@@ -316,6 +312,8 @@ def tile_list_radial_shell_features_kernel(tc, xT, wgt, offs, w1, mu, amp, wf_wo
         gather(1, 0, 0, S)
         gather(1, 1, 0, S)
         quantise_x(0, 0, S, on="plane5")
+        late_x = tile("late_x", [P, HALF * PACK], BF16)
+        weave_x(SCALAR, 1, q2, QUARTER, late_x[:, : PACK * QUARTER], slice(0, 2))
         gather(1, 2, 0, S)
         weave_w(SCALAR, 0, 0)
         quantise_w(0, 0, 0, PACK)
@@ -339,8 +337,8 @@ def tile_list_radial_shell_features_kernel(tc, xT, wgt, offs, w1, mu, amp, wf_wo
             for pair in range(PAIRS):
                 quantise_w(1, a, 2 * pair, 2)
         gather(1, last, HALF, HALF)
-        for j0 in (q2, q3):
-            weave_x(VECTOR, 1, j0, QUARTER)
+        weave_x(VECTOR, 1, q2, QUARTER, late_x[:, : PACK * QUARTER], slice(2, PACK))
+        weave_x(VECTOR, 1, q3, QUARTER, late_x[:, PACK * QUARTER :])
         for j0 in (q2, q3):
             quantise_x(1, j0, QUARTER)
 
@@ -350,7 +348,10 @@ def tile_list_radial_shell_features_kernel(tc, xT, wgt, offs, w1, mu, amp, wf_wo
         amplify_on_vector(0, q0, slice(0, QUARTER))
         quantise_h(0, q0, QUARTER)
         exp_negative(1, q1, QUARTER, on="plane7")
-        amplify_on_tile(0, q1, QUARTER, SHARE_TWO_CALLS, on=f"x_woven1_{q3}")
+        own = QUARTER - SHARE_TWO_CALLS
+        h_woven[(0, q1)] = late_x[:, PACK * (QUARTER - own) : PACK * (2 * QUARTER - own)]
+        amplify_on_gpsimd(0, q1, slice(own, QUARTER))
+        amplify_on_vector(0, q1, slice(0, own))
         place_h(1, q0, QUARTER, QUARTER)
         amplify_on_vector(1, q0, slice(0, QUARTER))
         quantise_h(0, q1, QUARTER)

from contextlib import ExitStack

import concourse.mybir as mybir
from concourse.masks import make_identity

K, T, S, H, N = 1024, 2048, 1024, 1024, 512
FLOPS = 2 * K * H * S + 2 * H * N * S

F32 = mybir.dt.float32
BF16 = mybir.dt.bfloat16
I32 = mybir.dt.int32
U32 = mybir.dt.uint32
U16 = mybir.dt.uint16
U8 = mybir.dt.uint8
FP8X4 = mybir.dt.float8_e4m3fn_x4
FP4X4 = mybir.dt.float4_e2m1fn_x4
MULT = mybir.AluOpType.mult
ACT = mybir.ActivationFunctionType

P = 128
QUADRANT = 32
PACK = 4
PAIRS = PACK // 2
PASS = P * PACK
PASSES = K // PASS
BANK = 512
BANKS = 8
SHELLS = 8
BLOCKS = S // P
LIST_ROWS = 16
LINE = 4
HALF = S // 2
QUARTER = S // 4
EIGHTH = S // 8
OUT_BANKS = 2
OUT_TILES = N // P // OUT_BANKS
SHARE_SHORT = 48
SHARE_ALONE = 64
SHARE_ONE_COPY = 96
SHARE_TWO_CALLS = 128
VECTOR, SCALAR = "vector", "scalar"


def tile_list_radial_shell_features_kernel(tc, xT, wgt, offs, w1, mu, amp, wf_words, wf_scales, out):
    nc = tc.nc
    with ExitStack() as ctx:
        keep = ctx.enter_context(tc.tile_pool(name="keep", bufs=1))
        psum = ctx.enter_context(tc.psum_pool(name="psum", bufs=BANKS - 1))
        psum_kept = ctx.enter_context(tc.psum_pool(name="psum_kept", bufs=1))

        def tile(name, shape, dtype, on=None):
            return keep.tile(shape, dtype, name=name, tag=on or name, align_bytes=64)

        def grid(name, shape, dtype):
            return [[tile(f"{name}{b}{a}", shape, dtype) for a in range(PASSES)] for b in range(PASSES)]

        def next_bank():
            return psum.tile([P, BANK], F32, name="bank", tag="bank")

        offsets = keep.tile([P, S // LIST_ROWS], U16, name="offsets")
        weights = tile("weights", [P, S], F32)
        planes = [[tile(f"plane{PACK * a + i}", [P, T], F32) for i in range(PACK)] for a in range(PASSES)]
        picked = [tile(f"picked{a}", [P, PACK, S], F32) for a in range(PASSES)]
        x_scales = [tile(f"x_scales{a}", [P, S], U8) for a in range(PASSES)]
        w_raw = grid("w_raw", [P, PACK, PASS], F32)
        w_woven = grid("w_woven", [P, PACK * P * PACK], BF16)
        w_codes = grid("w_codes", [P, PASS], U32)
        w_scales = grid("w_scales", [P, PASS], U8)
        h_scales = [tile(f"h_scales{b}", [P, S], U8) for b in range(PASSES)]
        along_r = tile("along_r", [P, PASS], F32)
        first_row = QUADRANT - 2 * PASSES
        turned_r = psum_kept.tile([P, BANK], F32, name="turned_r")
        rows_in_psum = turned_r[:].rearrange("p (t row) -> p row t", t=PACK)[:, first_row:QUADRANT]
        rows_in_sbuf = tile("rows_in_sbuf", [P, 2 * PASSES, PACK], F32)
        centres, amplitudes = rows_in_sbuf[:, :PASSES], rows_in_sbuf[:, PASSES:]
        amplitudes_in_psum = rows_in_psum[:, PASSES:]
        shared_h = tile("shared_h", [P, 3 * QUARTER * PACK], BF16)
        f_words = tile("f_words", [P, PASSES, 2 * N], U8)
        f_scales = tile("f_scales", [P, PASSES, N], U8)
        identity = tile("identity", [P, P], F32)
        shell_blocks = tile("shell_blocks", [P, P], F32)
        x_woven, x_codes, squares, exps, h_woven, h_codes, out_banks = {}, {}, {}, {}, {}, {}, {}
        places = []

        x_rows = xT.rearrange("(a p i) t -> a i p t", a=PASSES, i=PACK)
        w_rows = w1.rearrange("(a p i) r -> a p i r", a=PASSES, i=PACK)

        def holder(tiles, index, j0):
            first = max(start for which, start in tiles if which == index and start <= j0)
            return tiles[(index, first)], j0 - first

        def load_plane(a, i):
            nc.sync.dma_start(planes[a][i][:], x_rows[a, i])

        def load_w(b, a):
            nc.sync.dma_start(w_raw[b][a][:], w_rows[a, :, :, PASS * b : PASS * (b + 1)])

        def load_along_r(row, vector):
            nc.sync.dma_start(along_r[row : row + PASSES], vector.rearrange("(b r) -> b r", b=PASSES))

        def copy_on(engine, dst, src):
            if engine == VECTOR:
                nc.vector.tensor_copy(dst, src)
            else:
                nc.scalar.activation(dst, src, ACT.Copy)

        def turn(src, n):
            bank = next_bank()
            for c in range(n // P):
                nc.tensor.transpose(bank[:, P * c : P * (c + 1)], src[:, P * c : P * (c + 1)], identity[:])
            return bank[:, :n]

        def spread_weights(firsts, n):
            blocks = n // P
            by_entry = turn(shell_blocks[:], P)[:, : SHELLS * BLOCKS].rearrange("j (g c e) -> j c g e", g=SHELLS, e=1)
            spread = [tile(f"spread{j0}", [P, n], F32) for j0 in firsts]
            for j0, dst in zip(firsts, spread):
                nc.scalar.copy(
                    dst[:].rearrange("j (c g e) -> j c g e", c=blocks, e=LIST_ROWS),
                    by_entry[:, j0 // P : j0 // P + blocks].to_broadcast([P, blocks, SHELLS, LIST_ROWS]),
                )
            for j0, src in zip(firsts, spread):
                copy_on(SCALAR, weights[:, j0 : j0 + n], turn(src[:], n))

        def gather(a, i, j0, n):
            listed = offsets[:, j0 // LIST_ROWS : (j0 + n) // LIST_ROWS]
            nc.vector.tensor_tensor(
                picked[a][:, i, j0 : j0 + n], planes[a][i][:].indirect(listed), weights[:, j0 : j0 + n], MULT
            )

        def weave_x(engine, a, j0, n, woven=None, values=slice(0, PACK)):
            if woven is None:
                woven = tile(f"x_woven{a}_{j0}", [P, n * PACK], BF16)[:]
            x_woven[(a, j0)] = woven
            copy_on(
                engine,
                woven.rearrange("p (c e i) -> p c i e", e=LINE, i=PACK)[:, :, values],
                picked[a][:, values, j0 : j0 + n].rearrange("p i (c e) -> p c i e", e=LINE),
            )

        def quantise_x(a, j0, n, on=None):
            codes = tile(f"x_codes{a}_{j0}", [P, n], U32, on)
            x_codes[(a, j0)] = codes
            nc.vector.quantize_mx(codes[:].bitcast(FP8X4), x_scales[a][:, j0 : j0 + n], x_woven[(a, j0)])

        def woven_w(b, a, t0, count):
            if (b, a, t0) == (PASSES - 1, PASSES - 1, PACK - 2):
                return picked[PASSES - 1][:, PACK - 1, HALF:].bitcast(BF16)
            return w_woven[b][a][:, P * PACK * t0 : P * PACK * (t0 + count)]

        def weave_w(engine, b, a):
            for pair in range(PAIRS):
                copy_on(
                    engine,
                    woven_w(b, a, 2 * pair, 2).rearrange("p (e m i) -> p m i e", e=2, i=PACK),
                    w_raw[b][a][:].rearrange("p i (m v e) -> p v m i e", v=PAIRS, e=2)[:, pair],
                )

        def quantise_w(b, a, t0, count):
            cols = slice(P * t0, P * (t0 + count))
            nc.vector.quantize_mx(
                w_codes[b][a][:, cols].bitcast(FP8X4), w_scales[b][a][:, cols], woven_w(b, a, t0, count)
            )

        def square_distances(b, j0, n, per_bank, on, exps_after=1):
            square = tile(f"square{b}_{j0}", [P, PACK, n], F32, on)
            squares[(b, j0)] = square
            for t0 in range(0, PACK, per_bank):
                bank = next_bank()
                for a in range(PASSES):
                    cuts = [j0] + [start for which, start in x_codes if which == a and j0 < start < j0 + n] + [j0 + n]
                    for t in range(t0, t0 + per_bank):
                        for c0, c1 in zip(cuts, cuts[1:]):
                            first_out = (t - t0) * n + c0 - j0
                            codes, first = holder(x_codes, a, c0)
                            nc.tensor.matmul_mx(
                                bank[:, first_out : first_out + c1 - c0],
                                lhsT=w_codes[b][a][:, P * t : P * (t + 1)].bitcast(FP8X4),
                                lhsT_scale=w_scales[b][a][:, P * t : P * (t + 1)],
                                rhs=codes[:, first : first + c1 - c0].bitcast(FP8X4),
                                rhs_scale=x_scales[a][:, c0:c1],
                                start=(a == 0 and first_out == 0),
                                stop=(a == PASSES - 1 and first_out + c1 - c0 == per_bank * n),
                            )
                for t in range(t0, t0 + per_bank):
                    step = n // exps_after if t == PACK - 1 else n
                    for c0 in range(0, n, step):
                        nc.scalar.activation(
                            square[:, t, c0 : c0 + step],
                            bank[:, (t - t0) * n + c0 : (t - t0) * n + c0 + step],
                            ACT.Square,
                            bias=centres[:, b, t : t + 1],
                            scale=-1.0,
                        )

        def exp_negative(b, j0, n, on):
            square, first = holder(squares, b, j0)
            gauss = tile(f"gauss{b}_{j0}", [P, PACK, n], F32, on)
            exps[(b, j0)] = gauss
            nc.scalar.activation(gauss[:], square[:, :, first : first + n], ACT.Exp, scale=-1.0)

        def amplify(engine, amps, b, j0, entries):
            by_t = amps[:, b, :].rearrange("p (c t e) -> p c t e", c=1, e=1)
            woven = h_woven[(b, j0)][:, PACK * entries.start : PACK * entries.stop]
            engine.tensor_tensor(
                woven.rearrange("p (c e t) -> p c t e", e=LINE, t=PACK),
                exps[(b, j0)][:, :, entries].rearrange("p t (c e) -> p c t e", e=LINE),
                by_t.to_broadcast([P, (entries.stop - entries.start) // LINE, PACK, LINE]),
                MULT,
            )

        def amplify_on_vector(b, j0, entries):
            amplify(nc.vector, amplitudes_in_psum, b, j0, entries)

        def amplify_on_gpsimd(b, j0, entries):
            amplify(nc.gpsimd, amplitudes, b, j0, entries)

        def place_h(b, j0, start, n):
            h_woven[(b, j0)] = shared_h[:, PACK * start : PACK * (start + n)]
            places.append((start, start + n))

        def amplify_behind(b, j0, n, share):
            low, high = places[-1]
            if len(places) % 2:
                place_h(b, j0, low + share - n, n)
                given, own = slice(n - share, n), slice(0, n - share)
            else:
                place_h(b, j0, high - share, n)
                given, own = slice(0, share), slice(share, n)
            amplify_on_gpsimd(b, j0, given)
            amplify_on_vector(b, j0, own)

        def quantise_h(b, j0, n):
            codes = tile(f"h_codes{b}_{j0}", [P, n], U32)
            h_codes[(b, j0)] = codes
            nc.vector.quantize_mx(codes[:].bitcast(FP8X4), h_scales[b][:, j0 : j0 + n], h_woven[(b, j0)])

        def features(j0, n, halves):
            for which in range(OUT_BANKS):
                if (which, j0) not in out_banks:
                    out_banks[(which, j0)] = next_bank()
                for b in halves:
                    codes, first = holder(h_codes, b, j0)
                    for first_out in range(0, OUT_TILES * n, n):
                        m = OUT_TILES * which + first_out // n
                        nc.tensor.matmul_mx(
                            out_banks[(which, j0)][:, first_out : first_out + n],
                            lhsT=f_words[:, b, 2 * P * m : 2 * P * (m + 1)].bitcast(FP4X4),
                            lhsT_scale=f_scales[:, b, P * m : P * (m + 1)],
                            rhs=codes[:, first : first + n].bitcast(FP8X4),
                            rhs_scale=h_scales[b][:, j0 : j0 + n],
                            start=(b == 0 and first_out == 0),
                            stop=(b == PASSES - 1 and first_out + n == OUT_TILES * n),
                        )

        def store(j0, n, which, engine, result):
            copy_on(engine, result, out_banks[(which, j0)][:, : OUT_TILES * n])
            rows = slice(P * OUT_TILES * which, P * OUT_TILES * (which + 1))
            queue = nc.scalar if engine == SCALAR else nc.sync
            queue.dma_start(
                out[rows, j0 : j0 + n].rearrange("(m p) j -> p m j", p=P),
                result.rearrange("p (m j) -> p m j", j=n),
            )

        def store_bank(j0, n, which, engine):
            store(j0, n, which, engine, tile(f"result{which}_{j0}", [P, OUT_TILES * n], F32)[:])

        def store_held(j0, n, engine, on):
            width = OUT_TILES * n
            results = tile(f"results{j0}", [P, OUT_BANKS * width], F32, on)
            for which in range(OUT_BANKS):
                store(j0, n, which, engine, results[:, width * which : width * (which + 1)])

        q0, q1, q2, q3 = range(0, S, QUARTER)
        e0, e1 = q3, q3 + EIGHTH
        last = PACK - 1

        nc.sync.dma_start(shell_blocks[: SHELLS * BLOCKS], wgt[0:P:LIST_ROWS, :].rearrange("g (c u) -> g c u", u=P))
        make_identity(nc, identity[:])
        nc.vector.memset(shell_blocks[SHELLS * BLOCKS :], 0.0)
        nc.vector.memset(f_scales[:].rearrange("p b n -> p (b n)").bitcast(I32), 0)
        nc.sync.dma_start(offsets[:], offs)
        for i in range(PACK):
            load_plane(0, i)
        load_along_r(first_row, mu)
        load_along_r(first_row + PASSES, amp)
        for rows in (slice(0, first_row), slice(QUADRANT, 2 * QUADRANT), slice(2 * QUADRANT, P)):
            nc.gpsimd.memset(along_r[rows], 0.0)
        for i in range(last):
            load_plane(1, i)
        load_w(0, 0)
        load_plane(1, last)
        load_w(0, 1)
        load_w(1, 0)
        load_w(1, 1)
        nc.sync.dma_start(f_words[:].bitcast(I32), wf_words.rearrange("b p n -> p b n").bitcast(I32))
        for q in range(P // QUADRANT):
            nc.sync.dma_start(
                f_scales[QUADRANT * q : QUADRANT * q + 4].bitcast(I32),
                wf_scales[:, 4 * q : 4 * q + 4, :].rearrange("b r n -> r b n").bitcast(I32),
            )

        spread_weights((q0, q1, q2, q3), QUARTER)
        for j0 in (q0, q1, q2, q3):
            gather(0, 0, j0, QUARTER)
        for t in range(PACK):
            nc.tensor.transpose(turned_r[:, P * t : P * (t + 1)], along_r[:, t::PACK], identity[:])
        copy_on(SCALAR, rows_in_sbuf[:], rows_in_psum)
        for i in range(1, PACK):
            gather(0, i, 0, S)
        weave_x(SCALAR, 0, 0, S)
        gather(1, 0, 0, S)
        gather(1, 1, 0, S)
        quantise_x(0, 0, S, on="plane5")
        late_x = tile("late_x", [P, HALF * PACK], BF16)
        weave_x(SCALAR, 1, q2, QUARTER, late_x[:, : PACK * QUARTER], slice(0, 2))
        gather(1, 2, 0, S)
        weave_w(SCALAR, 0, 0)
        quantise_w(0, 0, 0, PACK)

        for j0 in (q0, q1):
            gather(1, last, j0, QUARTER)
            weave_x(SCALAR, 1, j0, QUARTER)
        weave_w(VECTOR, 0, 1)
        quantise_w(0, 1, 0, 2)
        quantise_x(1, q0, QUARTER, on="w_raw01")
        quantise_w(0, 1, 2, 2)
        quantise_x(1, q1, QUARTER)

        square_distances(0, q0, QUARTER, 1, on="plane0")
        square_distances(0, q1, QUARTER, 2, on="plane1")
        exp_negative(0, q0, QUARTER, on="plane3")
        exp_negative(0, q1, QUARTER, on="plane4")

        for a in range(PASSES):
            weave_w(VECTOR, 1, a)
            for pair in range(PAIRS):
                quantise_w(1, a, 2 * pair, 2)
        gather(1, last, HALF, HALF)
        weave_x(VECTOR, 1, q2, QUARTER, late_x[:, : PACK * QUARTER], slice(2, PACK))
        weave_x(VECTOR, 1, q3, QUARTER, late_x[:, PACK * QUARTER :])
        for j0 in (q2, q3):
            quantise_x(1, j0, QUARTER)

        square_distances(1, 0, HALF, 1, on="plane2", exps_after=2)
        exp_negative(1, q0, QUARTER, on="plane6")
        h_woven[(0, q0)] = tile("h_woven_q0", [P, QUARTER * PACK], BF16, on="w_woven11")[:]
        amplify_on_vector(0, q0, slice(0, QUARTER))
        quantise_h(0, q0, QUARTER)
        exp_negative(1, q1, QUARTER, on="plane7")
        own = QUARTER - SHARE_TWO_CALLS
        h_woven[(0, q1)] = late_x[:, PACK * (QUARTER - own) : PACK * (2 * QUARTER - own)]
        amplify_on_gpsimd(0, q1, slice(own, QUARTER))
        amplify_on_vector(0, q1, slice(0, own))
        place_h(1, q0, QUARTER, QUARTER)
        amplify_on_vector(1, q0, slice(0, QUARTER))
        quantise_h(0, q1, QUARTER)
        quantise_h(1, q0, QUARTER)

        square_distances(0, q2, QUARTER, 2, on="plane1")
        exp_negative(0, q2, QUARTER, on="w_raw00")
        features(q0, QUARTER, (0, 1))
        amplify_behind(1, q1, QUARTER, SHARE_ONE_COPY)
        store_bank(q0, QUARTER, 0, VECTOR)
        quantise_h(1, q1, QUARTER)
        square_distances(1, q2, QUARTER, 2, on="plane2")
        exp_negative(1, q2, QUARTER, on="plane3")
        features(q1, QUARTER, (0, 1))
        amplify_behind(0, q2, QUARTER, SHARE_ONE_COPY)
        store_bank(q0, QUARTER, 1, VECTOR)
        quantise_h(0, q2, QUARTER)
        square_distances(0, q3, QUARTER, 2, on="plane0")
        exp_negative(0, q3, QUARTER, on="plane4")
        amplify_behind(1, q2, QUARTER, SHARE_TWO_CALLS)
        store_held(q1, QUARTER, VECTOR, on="plane2")
        quantise_h(1, q2, QUARTER)

        square_distances(1, q3, QUARTER, 2, on="plane1", exps_after=2)
        exp_negative(1, e0, EIGHTH, on="plane6")
        exp_negative(1, e1, EIGHTH, on="plane7")
        for b in range(PASSES):
            features(q2, QUARTER, (b,))
        amplify_behind(0, q3, QUARTER, SHARE_ALONE)
        quantise_h(0, q3, QUARTER)
        for j0 in (e0, e1):
            features(j0, EIGHTH, (0,))
        h_woven[(1, e0)] = tile("h_woven_e0", [P, EIGHTH * PACK], BF16)[:]
        amplify_on_vector(1, e0, slice(0, EIGHTH))
        amplify_behind(1, e1, EIGHTH, SHARE_SHORT)
        for j0 in (e0, e1):
            quantise_h(1, j0, EIGHTH)
            features(j0, EIGHTH, (1,))
        store_held(q2, QUARTER, SCALAR, on="plane1")
        for j0 in (e0, e1):
            store_bank(j0, EIGHTH, 0, VECTOR)
            store_bank(j0, EIGHTH, 1, SCALAR)
